import numpy as np, ml_dtypes
CORES = [16,17,18,19,32,33,34,35]
N = 8
import mx_ref
BF = ml_dtypes.bfloat16
def gcols(t, e):
    v = np.concatenate([t.reshape(8, 16, -1, 4), np.zeros((8, 16, 1, 4), BF)], axis=2)
    return np.ascontiguousarray(np.stack([v[g][:, e[g]] for g in range(8)])).reshape(128, -1)
def pick(q, e):
    c = np.concatenate([q[0].reshape(128, -1, 4), np.zeros((128, 1, 4), np.uint8)], axis=1); s = np.concatenate([q[1], np.ones((16, 1), np.uint8)], axis=1)
    return (np.ascontiguousarray(c[:, e].reshape(128, -1)), np.ascontiguousarray(s[:, e]))
def join(*qs):
    return (np.concatenate([q[0] for q in qs], axis=1), np.concatenate([q[1] for q in qs], axis=1))
def put(q, e, v):
    c, s = q[0].reshape(128, -1, 4).copy(), q[1].copy(); c[:, e] = v[0].reshape(128, -1, 4); s[:, e] = v[1]
    return (c.reshape(128, -1), s)
def pk(c, s):
    return (np.ascontiguousarray(c), mx_ref.live(s))
def emit(q):
    return q[0], q[1]
def packed(v, rng):
    q = [mx_ref.quantize(np.ascontiguousarray(v[r])) for r in range(N)]
    return np.stack([a for a, b in q]), np.stack([mx_ref.plane(b, rng) for a, b in q])
def values_of_codes():
    e, c = np.zeros((128, 128, 4), np.float32), np.zeros((128, 2, 4), np.uint8)
    e[np.arange(128), np.arange(128), 0] = 1
    c[:127, :, 0] = np.arange(256).reshape(2, 128).T[:127]
    return mx_ref.matmul(mx_ref.quantize(e.reshape(128, 512).astype(BF)), (c.reshape(128, 8), np.full((16, 2), 127, np.uint8))).T.reshape(-1).astype(np.float64)
CODE_VALUE, SCALE_VALUE = values_of_codes(), 2.0 ** (np.arange(256) - 127.0)
def decode(q):
    return (CODE_VALUE[q[0]].reshape(16, 8, -1, 4) * SCALE_VALUE[q[1]][:, None, :, None] + 0.0).reshape(128, -1).astype(np.float32)
def f(rng, *shape):
    return mx_ref.flush((rng.standard_normal(shape, dtype=np.float32) * np.exp2(rng.integers(-2, 3, shape[:-1] + (1,)))).astype(BF))
def wide(rng, *shape, cols=0):
    v = rng.standard_normal(shape, dtype=np.float32) * np.exp2(rng.integers(-12, 13, shape)).astype(np.float32)
    if cols: v *= np.repeat(np.exp2(rng.integers(-cols, cols + 1, shape[:-2] + (1, shape[-1] // 4))) * (rng.random(shape[:-2] + (1, shape[-1] // 4)) > 0.0625), 4, axis=-1).astype(np.float32)
    return mx_ref.flush(v.astype(BF))
C, L, K = 256, 16, 128
MASKS = [1, 2, 4]
def big(v):
    v = v.astype(np.float32)
    v[np.abs(v) < np.float32(2.0 ** -16)] = 0
    return v.astype(BF)
def numbers_of(rng):
    return {"x": big(f(rng, N, 128, 4 * C)), "u": np.array(f(rng, N, 128, 512)), "v": np.array(f(rng, N, 128, 512))}
def layers(rng, still=[]):
    w = big(f(rng, N, 128, 2048)).reshape(N, 8, 16, 4, 8, 16, 4)
    for i in still:
        w[:, :, i] = 0
        w[:, :, :, :, :, i] = 0
    return w
def weights(rng, w):
    c, s = packed(np.ascontiguousarray(w).reshape(N, 128, 2048), rng)
    return {"wc": c, "ws": s}
def bare(u):
    u = u.reshape(N, 128, 128, 4)
    u[:, :, ::16] = 0
    u[:, :, 1::16] = 0
    return u
def back(x):
    return np.ascontiguousarray(x).astype(np.float32).reshape(N, 128, 4 * C).astype(BF)
def setup_inputs(rng):
    return {**numbers_of(rng), **weights(rng, layers(rng))}
def setup_inputs_ties(rng):
    d = numbers_of(rng)
    x = d["x"].astype(np.float32).reshape(N, 8, 16, C, 4)
    x[:, :, 0] = 0
    for b in range(2): x[:, :, 0, :, b] = np.minimum(rng.integers(0, 3, (N, 8, L, L)), rng.integers(0, 3, (N, 8, L, 1))).reshape(N, 8, C)
    u = bare(d["u"])
    o = rng.permutation(N)
    for r in range(N):
        k = 0.0 if r == o[0] else -1.0 if r == o[1] else 1.0
        for h in range(0, 128, 16):
            u[r, h, h, 0] = k
            u[r, h, h + 1, 1] = k
    return {"x": back(x), "u": u.reshape(N, 128, 512), "v": d["v"], **weights(rng, layers(rng, [0]))}
def setup_inputs_near(rng):
    d = numbers_of(rng)
    x = d["x"].astype(np.float32).reshape(N, 8, 16, C, 4)
    u = bare(d["u"])
    x[:, :, :2] = 0
    x[:, :, 8:] = 0
    o = rng.permutation(8) % 4
    for g in range(8):
        h, a = 16 * g, 2.0 ** -30 if o[g] >= 2 else 1.0
        if o[g] == 3:
            x[:, g, 10:12, :, 0] = 2.0 ** -29 * (1.0 + 0.125 * rng.integers(0, 6, (N, 2, C)))
            u[:, h + 10, h, 0] = -a
            u[:, h + 11, h + 1, 0] = -a
            continue
        i = h + 1 if o[g] == 1 else h
        x[:, g, 0, :, 0] = rng.integers(0, 2, (N, 1)) * 2.0 - 1.0
        x[:, g, 8:10] = ((rng.integers(0, 16, (N, 2, C))[..., None] >> np.arange(4)) & 1) * np.exp2(np.arange(4) - 23.0)
        x[:, g, 11, :, 0] = 2.0 ** -10
        u[:, h, i, 0] = a
        u[:, h + 11, i, 0] = a
        u[:, h + 8, h] = a
        u[:, h + 9, h + 1] = a
        if o[g] == 1: x[np.arange(N), g, 0, rng.integers(0, C, N), 0] = -2.0 ** 29
        else:
            for r in range(N):
                k = rng.permutation(L)
                x[r, g, 0, L * k[0]:L * k[0] + L, 0] = -2.0 ** 29
                x[r, g, 0, L * k[1] + rng.integers(0, L), 0] = 2.0 ** 29 * (rng.integers(0, 2) * 2.0 - 1.0)
    return {"x": back(x), "u": u.reshape(N, 128, 512), "v": d["v"], **weights(rng, layers(rng, [0, 1] + [8 + i for i in range(8)]))}
def setup_inputs_huge(rng):
    d = numbers_of(rng)
    x = -2.0 ** 30 * np.where(rng.random((N, 8, 16, C, 4)) < rng.random((N, 8, 1, C, 1)), 0.9375, 0.875)
    u = bare(d["u"])
    o = rng.permutation(8)
    for g in range(8):
        for b in range(2):
            for h in rng.permutation(8)[:8 if o[g] < 3 else 2]: u[:, 16 * h:16 * h + 16, 16 * g + b] = 2.0 ** 30 if o[g] % 2 == 0 else -2.0 ** 30
    w = np.zeros((N, 128, 4, 128, 4), np.float32)
    i = np.arange(128)
    for b in range(4): w[:, i, b, i, b] = -2
    return {"x": back(x), "u": u.reshape(N, 128, 512), "v": d["v"], **weights(rng, w.astype(BF))}
def setup_inputs_late(rng):
    d = numbers_of(rng)
    x = d["x"].astype(np.float32).reshape(N, 8, 16, C, 4)
    x[:, :, 8:] = (1.125 + 0.25 * rng.integers(0, 4, (N, 8, 8, C, 4))) * np.exp2(rng.integers(-1, 2, (N, 8, 8, C, 4))) * rng.choice([-1.0, 1.0], (N, 8, 8, C, 4))
    x[:, :, 8, :, 2:] = 1.96875 * 2.0 ** 13 * rng.choice([-1.0, 1.0], (8, 1, 1))
    u = bare(d["u"])
    for h in range(0, 128, 16):
        u[:, h, h, 0] = 1.0
        u[:, h, h + 1, 1] = 1.0
    s = MASKS[0]
    none = rng.permutation([r for r in range(N) if r < r ^ s])[:N // 4]
    for r in range(N):
        if min(r, r ^ s) in none: x[r, :, :8] = 0
        else:
            a = np.zeros((8, L, L), np.float32)
            np.put_along_axis(a, rng.integers(0, L, (8, L, 1)), np.exp2(np.argsort(rng.random((8, L, 1)), axis=1).astype(np.float32)), axis=2)
            x[r, :, 0] = 0
            x[r, :, 0, :, 0] = a.reshape(8, C)
            for h in range(0, 128, 16): u[r, h + 9, h + 1, 1] = 0.125
    w = layers(rng)
    w[:, :, 0] = 0
    w[:, :, 8] = 0
    for g in range(8):
        w[:, g, 8, 2:, g, 8, 2] = 16
        w[:, g, 8, 2:, g, 8, 3] = 15
    return {"x": back(x), "u": u.reshape(N, 128, 512), "v": d["v"], **weights(rng, w)}
def setup_inputs_spread(rng):
    d = setup_inputs(rng)
    d["x"] = big(wide(rng, N, 128, 4 * C, cols=6))
    return d
def check_inputs(d):
    b = []
    for k in ("x", "u", "v"):
        a = np.abs(d[k].astype(np.float32))
        if not (np.isfinite(a).all() and ((a == 0) | (a >= 2.0 ** -30) & (a <= 2.0 ** 30)).all()): b.append("a value of " + k)
    none, least, most = [emit(mx_ref.quantize(np.full((128, 16), k, np.float32).astype(BF)))[1][0, 0] for k in (0.0, 2.0 ** -30, 2.0 ** 30)]
    for r in range(N):
        if ((d["wc"][r] == 0x7F) | (d["wc"][r] == 0xFF)).any(): b.append("wc: a code that is no number")
        s = mx_ref.live(d["ws"][r])
        if ((s != none) & ((s < least) | (s > most))).any(): b.append("ws: a scale out of range")
    return b
def reference(x, u, v, wc, ws):
    qu = [mx_ref.quantize(u[r]) for r in range(N)]
    lay = [pk(wc[r], ws[r]) for r in range(N)]
    now = [x[r] for r in range(N)]
    for s in MASKS:
        q = [mx_ref.quantize(now[r]) for r in range(N)]
        t = [decode(q[r]) for r in range(N)]
        score = [mx_ref.matmul(qu[r], q[r]) + np.float32(0.0) for r in range(N)]
        made = []
        for r in range(N):
            d = r ^ s
            both = score[r][::16].reshape(8, L, 1, L) + score[d][1::16].reshape(8, 1, L, L)
            best, middle = np.max(both, axis=3).reshape(8, C), np.argmax(both, axis=3).reshape(8, C)
            e = np.argsort(-best, axis=1, kind="stable")[:, :K]
            m = np.take_along_axis(middle, e, axis=1)
            one = gcols(t[r].astype(BF), e // L * L + m).astype(np.float32)
            two = decode(mx_ref.quantize(gcols(t[d].astype(BF), e % L * L + m)))
            z = mx_ref.quantize(((one + two) * np.float32(0.5)).astype(BF))
            h = np.stack([mx_ref.matmul(pick(lay[r], np.arange(128 * b, 128 * b + 128)), z) * np.float32(0.03125) for b in range(4)], axis=2).reshape(8, 16, K, 4)
            n = t[r].reshape(8, 16, C, 4).copy()
            for g in range(8): n[g][:, e[g]] = n[g][:, e[g]] + h[g]
            made.append(n.reshape(128, 4 * C).astype(BF))
        now = made
    y = np.zeros((N, 128, C), np.float32)
    oc, osc = np.zeros((N, 128, 4 * C), np.uint8), np.zeros((N, 16, C), np.uint8)
    for r in range(N):
        q = mx_ref.quantize(now[r])
        y[r] = mx_ref.matmul(mx_ref.quantize(v[r]), q)
        oc[r], osc[r] = emit(q)
    return {"y": y, "oc": oc, "osc": osc}

@@ -1,0 +1,457 @@
+from concourse.mybir import dt, AluOpType, ActivationFunctionType
+
+ALU, ACT = AluOpType, ActivationFunctionType
+F, B, I, U, X4, U8 = "float32", "bfloat16", "int32", "uint16", "float8_e4m3fn_x4", "uint8"
+MASKS = [1, 2, 4]
+NV = 8
+NS = 16 - NV
+BIG = 1.0e29
+WM = 8193.0
+
+
+def _sb(n, d):
+    return ("sbuf", [128, n], d)
+
+
+SCRATCH = {
+    "x0": _sb(1024, B), "xs": _sb(1024, B), "xq": _sb(256, X4), "xp": _sb(256, U8),
+    "ub": _sb(512, B), "uq": _sb(128, X4), "up": _sb(128, U8), "u0q": _sb(256, X4), "u0p": _sb(256, U8),
+    "vb": _sb(512, B), "vq": _sb(128, X4), "vp": _sb(128, U8),
+    "wq": _sb(512, X4), "wp": _sb(512, U8),
+    "ones": _sb(128, B), "ident": _sb(128, B), "eb": _sb(520, B), "eq": _sb(512, X4), "ep": _sb(512, U8),
+    "pi": _sb(2, I), "pb": _sb(8, I), "pf": _sb(8, F), "pc": _sb(8, F), "i16": _sb(16, F), "ibc": _sb(16, F),
+    "jj": _sb(384, B), "ii": _sb(256, F), "ka": _sb(256, F), "kb": _sb(256, F), "tmpc": _sb(8, F),
+    "iu": _sb(16, I), "i01": _sb(16, F), "tmpb": _sb(48, F),
+    "o_u": _sb(16, U), "o_d": _sb(4, U), "o_m": _sb(24, U), "o_i": _sb(16, U), "o_b": _sb(16, U),
+    "o_s": _sb(8, U), "o_e": _sb(2, U), "o_c": _sb(16, U),
+    "kmax": _sb(384, B), "kw": _sb(256, F), "kq": _sb(256, B), "km": _sb(256, F), "c128": _sb(16, F),
+    "o1": _sb(264, F), "i2": _sb(64, F), "o2": _sb(64, F), "s0": _sb(384, F), "s1": _sb(256, F),
+    "tt": _sb(1024, B), "win": _sb(4 * 384, B), "tw": _sb(1024, B),
+    "sm": _sb(384, F), "pm": _sb(392, F), "bc": _sb(256, F), "row": _sb(256, F), "bst": _sb(16, F),
+    "cm": _sb(256, F), "cnt": _sb(256, F), "vx": _sb(256, F), "ee": _sb(256, B), "es": _sb(256, B), "e2": _sb(16, F),
+    "cb": _sb(NV * 256, B), "so": _sb(NV * 128, B), "sg": _sb(NS * 256, B), "jk": _sb(NS * 256, B),
+    "aca": _sb(16, F), "acb": _sb(16, F), "t1": _sb(16, F), "t2": _sb(16, F), "l_s": _sb(16, U),
+    "sw": _sb(272, F), "tb": _sb(256, F), "ts": _sb(256, F), "vi": _sb(16, I), "li": _sb(16, I),
+    "l_k": _sb(16, U), "l_a": _sb(16, U),
+    "r1": _sb(16, F), "r2": _sb(16, F), "r3": _sb(16, F), "r4": _sb(16, F), "l_x": _sb(16, U),
+    "ag": _sb(512, F), "te": _sb(512, F), "zt": _sb(512, B), "zq": _sb(128, X4), "zp": _sb(128, U8),
+    "yb": _sb(256, F),
+}
+for _r in range(3):
+    SCRATCH["ss%d" % _r] = _sb(32, F)
+    SCRATCH["sl%d" % _r] = _sb(32, F)
+    SCRATCH["tq%d" % _r] = _sb(256, X4)
+    SCRATCH["tp%d" % _r] = _sb(256, U8)
+    SCRATCH["lq%d" % _r] = _sb(256, X4)
+    SCRATCH["lp%d" % _r] = _sb(256, U8)
+for _k in range(8):
+    SCRATCH["ps%d" % _k] = ("psum", [128, 512], F)
+
+NC, ND = 100, 16
+SEMAPHORES = (["c%d" % k for k in range(NC)] + ["d%d" % k for k in range(ND)]
+              + ["%s%d" % (n, r) for n in ("as", "aq", "gs", "gq", "gp") for r in range(3)])
+
+
+def _bits(engs):
+    m = 0
+    for e in engs:
+        m |= 1 << e
+    return m
+
+
+def rank_program(g, core, T, topo):
+    rank = T.rank_of(core)
+    if rank is None:
+        return
+    eng = {"G": g, "V": g.vector, "S": g.scalar, "P": g.tensor, "Y": g.sync}
+    ops = []
+
+    def w(name, a=0, b=None, s=1):
+        if b is None:
+            b = SCRATCH[name][1][1]
+        ap = T[name][:, a:b] if s == 1 else T[name][:, a:b:s]
+        if s == 1:
+            m = ((1 << (b - a)) - 1) << a
+        else:
+            m = _bits(range(a, b, s))
+        return (ap, [(name, m)])
+
+    def ind(win, off):
+        return (win[0].indirect(off[0]), win[1] + off[1])
+
+    def ap(v):
+        return v[0] if isinstance(v, tuple) else v
+
+    def acc(vs):
+        out = []
+        for v in vs:
+            if isinstance(v, tuple):
+                out += v[1]
+        return out
+
+    def op(q, kind, fn, reads, writes, sem=None):
+        ops.append({"q": q, "kind": kind, "fn": fn, "r": acc(reads), "w": acc(writes), "sem": sem})
+
+    def copy(o, i):
+        op("V", "c", lambda e: e.tensor_copy(ap(o), ap(i)), [i], [o])
+
+    def scatter(win, off, i):
+        op("V", "c", lambda e: e.tensor_copy(win[0].indirect(off[0]), ap(i)), [i, off], [win])
+
+    def tt(o, a, b, f):
+        op("V", "c", lambda e: e.tensor_tensor(ap(o), ap(a), ap(b), f), [a, b], [o])
+
+    def ts(o, a, s1, f1, s2=None, f2=None):
+        if f2 is None:
+            op("V", "c", lambda e: e.tensor_scalar(ap(o), ap(a), ap(s1), None, f1), [a, s1], [o])
+        else:
+            op("V", "c", lambda e: e.tensor_scalar(ap(o), ap(a), ap(s1), ap(s2), f1, f2), [a, s1, s2], [o])
+
+    def scan(o, a, b, init, f0, f1):
+        op("V", "c", lambda e: e.tensor_tensor_scan(ap(o), ap(a), ap(b), ap(init), f0, f1), [a, b, init], [o])
+
+    def trans(o, i):
+        op("V", "c", lambda e: e.transpose(ap(o), ap(i)), [i], [o])
+
+    def memset(o, c):
+        op("V", "c", lambda e: e.memset(ap(o), c), [], [o])
+
+    def quant(q, p, i):
+        op("V", "c", lambda e: e.quantize_mx(ap(q), ap(p), ap(i)), [i], [q, p])
+
+    def act(o, i, f, bias=None, scale=None, accum=None):
+        kw = {}
+        if bias is not None:
+            kw["bias"] = ap(bias)
+        if scale is not None:
+            kw["scale"] = ap(scale)
+        if accum is not None:
+            kw["accum_out"] = ap(accum)
+        op("S", "c", lambda e: e.activation(ap(o), ap(i), f, **kw), [i, bias, scale], [o, accum])
+
+    def mm(bank, n, lq, lp, rq, rp):
+        o = w("ps%d" % bank, 0, n)
+        op("P", "c", lambda e: e.matmul_mx(ap(o), ap(lq), ap(lp), ap(rq), ap(rp), True, True), [lq, lp, rq, rp], [o])
+
+    def iota(o, pat, base, cm, small):
+        if small:
+            op("G", "c", lambda e: e.iota(ap(o), pat, base, cm, allow_small_or_imprecise_dtypes=True), [], [o])
+        else:
+            op("G", "c", lambda e: e.iota(ap(o), pat, base, cm), [], [o])
+
+    def dma(q, o, i):
+        op(q, "d", lambda e: e.dma_start(ap(o), ap(i)), [i], [o])
+
+    def u8(v):
+        return (v[0].bitcast(dt.uint8), v[1])
+
+    def send(dst, o, i, rsem, lsem, engs):
+        rid, pid, _ = topo.addr(dst)
+        op("G", "r", lambda e: e.remote_dma(o, ap(i), T.sem[rsem], T.sem[lsem], pid, rid, _bits(engs)),
+           [i], [], (lsem, len(engs)))
+
+    def arrive(views, sem, n):
+        op("X", "x", None, [], views, (sem, n))
+
+    def col(name, k):
+        return w(name, k, k + 1)
+
+    def part(name, k, n=128):
+        return w(name, n * k, n * k + n)
+
+    def quant_x(name):
+        for h in range(2):
+            quant(part("xq", h), part("xp", h), part(name, h, 512))
+
+    def unpack(q, p):
+        for b in range(4):
+            mm(b, 256, part("eq", b), part("ep", b), w(q), w(p))
+
+    dma("Y", w("x0"), T.x[:])
+    dma("S", w("ub"), T.u[:])
+    memset(w("ones"), 1.0)
+    iota(w("pi", 0, 1), [[0, 1]], 0, 1, False)
+    iota(w("i16"), [[16, 16]], 0, 0, True)
+    op("G", "c", lambda e: e.affine_select(T.ident[:], T.ones[:], [[-1, 128]], ALU.is_equal, 0.0, 0, 1),
+       [w("ones")], [w("ident")])
+    iota(w("iu", 0, 8), [[16, 8]], 0, 0, False)
+    iota(w("iu", 8, 16), [[32, 4], [-16, 2]], 16, 0, False)
+    iota(w("jj"), [[0, 24], [1, 16]], 0, 0, True)
+    iota(w("ibc"), [[1, 8], [0, 2]], 0, 0, True)
+    iota(w("i01"), [[0, 8], [1, 2]], 0, 0, True)
+    iota(w("ii"), [[1, 16], [0, 16]], 0, 0, True)
+    memset(w("o1", 256, 264), 0.0)
+    p_ = w("pi", 0, 1)
+    for k, m in enumerate((15, 16, 31, 14, 1, 6)):
+        ts(col("pb", k), p_, m, ALU.bitwise_and)
+    ts(col("pb", 6), p_, 4, ALU.logical_shift_right, 1, ALU.bitwise_and)
+    memset(w("eb"), 0.0)
+    copy(w("pf", 0, 7), w("pb", 0, 7))
+    qf, hf, rf, q14, par, q6, hb = [col("pf", k) for k in range(7)]
+    copy(w("eb", 3, 515, 4), w("ident"))
+    tt(col("pc", 0), par, hb, ALU.is_equal)
+    ts(col("pc", 1), q14, 16.0, ALU.mult, -255.0, ALU.add)
+    ts(col("pc", 2), par, 128.0, ALU.mult, hf, ALU.add)
+    ts(col("pc", 3), hf, 2.0, ALU.mult, -256.0, ALU.add)
+    ts(w("tmpc", 0, 4, 2), w("i16", 0, 2), col("pc", 1), ALU.add)
+    ts(w("tmpc", 1, 4, 2), w("i16", 0, 2), col("pc", 1), ALU.add)
+    ts(col("pc", 4), qf, 16.0, ALU.mult)
+    ts(col("pc", 5), hf, 127.0, ALU.add)
+    ts(w("o_d"), w("tmpc", 0, 4), col("pc", 0), ALU.mult, 256.0, ALU.add)
+    ts(col("tmpc", 4), q6, 16.0, ALU.mult, col("pc", 2), ALU.add)
+    copy(w("o_u"), w("iu"))
+    for b in range(4):
+        quant(part("eq", b), part("ep", b), w("eb", 3 - b, 515 - b))
+    quant(w("uq"), w("up"), w("ub"))
+
+    def late_constants():
+        ts(w("o_s"), w("i16", 0, 8), 2.0, ALU.mult, rf, ALU.add)
+        ts(w("o_m", 0, 16), w("i16"), 0.0, ALU.mult, rf, ALU.add)
+        ts(col("pc", 6), hf, -2.0, ALU.mult, 16.0, ALU.add)
+        ts(w("kmax"), w("jj"), 0.0, ALU.is_equal, -BIG, ALU.mult)
+        ts(col("pc", 7), col("pc", 6), rf, ALU.add)
+        memset(w("pm", 0, 8), 0.0)
+        ts(w("o_i"), w("i16"), 15.0, ALU.add)
+        ts(w("o_c"), w("i16"), 0.0625, ALU.mult)
+        ts(w("o_m", 16, 24), w("i16", 0, 8), 0.0, ALU.mult, col("pc", 7), ALU.add)
+        ts(w("tmpb", 0, 16), w("ibc"), 16.0, ALU.mult, hf, ALU.add)
+        ts(w("tmpb", 16, 32), w("i01"), hb, ALU.is_equal)
+        ts(w("kw"), w("jj", 0, 256), 0.0, ALU.not_equal)
+        ts(w("tmpb", 0, 16), w("tmpb", 0, 16), -256.0, ALU.add)
+        ts(w("tmpb", 32, 48), w("ibc"), 16.0, ALU.mult, 271.0, ALU.add)
+        ts(w("kq"), w("jj", 0, 256), qf, ALU.not_equal)
+        tt(w("tmpb", 0, 16), w("tmpb", 0, 16), w("tmpb", 16, 32), ALU.mult)
+        memset(w("kw", 15, 256, 16), WM)
+        ts(col("o_e", 0), col("tmpc", 4), 15.0, ALU.add)
+        tt(w("tmpb", 16, 32), w("tmpb", 0, 16), w("tmpb", 32, 48), ALU.add)
+        ts(w("c128"), w("i16"), 128.0, ALU.add, qf, ALU.add)
+        memset(w("sw"), -1.0)
+        copy(w("o_b"), w("tmpb", 16, 32))
+        act(w("ka"), w("ii"), ACT.Identity, bias=col("pc", 4), scale=131328.0)
+        act(w("kb"), w("kq"), ACT.Copy, scale=-67108864.0)
+        tt(w("km"), w("ka"), w("kb"), ALU.add)
+
+    X = "x0"
+    for R, mask in enumerate(MASKS):
+        peer = T.cores[rank ^ mask]
+        en = topo.engines(core, peer)
+        if R == 0:
+            e_s, e_q = en[:len(en) // 2], en[len(en) // 2:]
+        else:
+            e_s, e_q = en, en
+        quant_x(X)
+        for h in range(2):
+            mm(4 + 3 * h, 128, w("uq"), w("up"), part("xq", h), part("xp", h))
+        if R == 0:
+            dma("Y", u8(w("wq")), (T.wc[:], w("x0")[1]))
+            dma("Y", w("wp"), T.ws[:])
+            dma("Y", w("vb"), T.v[:])
+            act(w("u0p"), ind(w("up"), w("o_u")), ACT.Copy)
+        unpack("xq", "xp")
+        for h in range(2):
+            trans(part("o1", h), w("ps%d" % (4 + 3 * h), 0, 128))
+        copy(w("i2"), ind(w("o1"), w("o_d")))
+        trans(w("o2"), w("i2"))
+        for h in range(2):
+            tt(part("ss%d" % R, h, 16), part("o2", 2 * h, 16), part("o2", 2 * h + 1, 16), ALU.add)
+        send(peer, T["sl%d" % R][:], w("ss%d" % R), "as%d" % R, "gs%d" % R, e_s)
+        if R == 0:
+            op("V", "c", lambda e: e.tensor_copy(T.u0q[:].bitcast(dt.uint32),
+                                                 T.uq[:].bitcast(dt.uint32).indirect(T.o_u[:])),
+               [w("uq"), w("o_u")], [w("u0q")])
+        for h in range(2):
+            mm(5 + h, 256, part("u0q", h), part("u0p", h), w("xq"), w("xp"))
+        for b in range(3):
+            act(w("tt", b, 1024, 4), w("ps%d" % b, 0, 256), ACT.Copy)
+        copy(w("tt", 3, 1024, 4), w("ps3", 0, 256))
+        quant(w("tq%d" % R), w("tp%d" % R), w("tt"))
+        send(peer, T["lq%d" % R][:].bitcast(dt.uint8), u8(w("tq%d" % R)), "aq%d" % R, "gq%d" % R, e_q)
+        send(peer, T["lp%d" % R][:], w("tp%d" % R), "aq%d" % R, "gp%d" % R, e_q)
+        act(w("s1"), w("ps6", 0, 256), ACT.Copy)
+        act(w("s0", 0, 256), w("ps5", 0, 256), ACT.Copy)
+        if R == 0:
+            late_constants()
+        act(w("s0", 256, 384), ind(w("s1"), w("o_s")), ACT.Copy)
+        for b in range(4):
+            ts(w("win", 384 * b + 128, 384 * b + 384), w("tt", b, 1024, 4), 32.0, ALU.mult)
+        if R == 1:
+            quant(w("vq"), w("vp"), w("vb"))
+        arrive([w("sl%d" % R)], "as%d" % R, len(e_s))
+        arrive([w("lq%d" % R), w("lp%d" % R)], "aq%d" % R, 2 * len(e_q))
+        tt(w("sm"), ind(w("sl%d" % R), w("o_m")), w("s0"), ALU.add)
+        scan(w("pm", 8, 392), w("kmax"), w("sm"), 0.0, ALU.add, ALU.max)
+        act(w("bc"), ind(w("pm", 8, 392), w("o_b")), ACT.Copy)
+        copy(w("bst"), w("pm", 23, 264, 16))
+        tt(w("cm"), ind(w("bst"), w("o_c")), w("pm", 7, 263), ALU.is_gt)
+        trans(w("row"), w("bc"))
+        scan(w("cnt"), w("cm"), w("kw"), 0.0, ALU.add, ALU.mult)
+
+        def own(k):
+            return col("bst", k)
+
+        def v_cmp(k):
+            a = 16 * (k + 1)
+            ts(w("cb", 256 * k, 256 * k + a), w("row", 0, a), own(k), ALU.is_ge, 2.0, ALU.mult)
+            ts(w("cb", 256 * k + a, 256 * k + 256), w("row", a, 256), own(k), ALU.is_gt, 2.0, ALU.mult)
+
+        def v_sum(k):
+            scan(part("so", k), part("cb", 2 * k), part("cb", 2 * k + 1), col("e2", k), ALU.add, ALU.add)
+
+        def s_cmp(k):
+            act(part("sg", k - NV, 256), w("row"), ACT.Sign, bias=own(k), scale=-1.0)
+
+        def s_sum(k):
+            o, a = 256 * (k - NV), 16 * (k + 1)
+            if a < 256:
+                act(w("jk", o + a, o + 256), w("sg", o + a, o + 256), ACT.Sign, bias=-0.5, scale=-1.0, accum=col("acb", k))
+                act(w("jk", o, o + a), w("sg", o, o + a), ACT.Sign, bias=0.5, scale=-1.0, accum=col("aca", k))
+            else:
+                act(w("jk", o, o + a), w("sg", o, o + a), ACT.Relu, accum=col("aca", k))
+
+        s_cmp(NV)
+        for k in range(NV, 16):
+            if k + 1 < 16:
+                s_cmp(k + 1)
+            s_sum(k)
+        tt(w("ee"), ind(w("bst"), w("o_c")), w("row"), ALU.is_equal)
+        tt(w("vx"), ind(w("cnt"), w("o_i")), w("km"), ALU.add)
+        scan(w("es"), w("kq"), w("ee"), 0.0, ALU.mult, ALU.add)
+        v_cmp(0)
+        ts(w("e2"), w("es", 15, 256, 16), -2.0, ALU.mult, col("pc", 3), ALU.add)
+        for k in range(NV):
+            if k == 1:
+                ts(col("t1", 15), col("e2", 15), 0.5, ALU.mult, 384.0, ALU.add)
+            if k + 1 < NV:
+                v_cmp(k + 1)
+            else:
+                tt(w("t1", NV, 15), w("acb", NV, 15), w("e2", NV, 15), ALU.add)
+            v_sum(k)
+        tt(w("t2", NV, 15), w("aca", NV, 15), w("t1", NV, 15), ALU.add)
+        ts(w("l_s", 0, NV), w("so", 127, NV * 128, 128), 0.5, ALU.mult, 128.0, ALU.add)
+        ts(w("l_s", NV, 15), w("t2", NV, 15), 0.5, ALU.mult, 256.0, ALU.add)
+        ts(col("l_s", 15), col("aca", 15), -1.0, ALU.mult, col("t1", 15), ALU.add)
+        unpack("lq%d" % R, "lp%d" % R)
+        for b in range(4):
+            act(part("tw", b, 256), w("ps%d" % b, 0, 256), ACT.Copy, scale=0.5)
+        scatter(w("sw"), w("l_s"), w("vx"))
+        trans(part("tb", 0), w("sw", 0, 128))
+        trans(part("tb", 1), w("sw", 16, 144))
+        for h in range(2):
+            scan(part("ts", h), w("kmax", 0, 128), part("tb", h), 0.0, ALU.add, ALU.max)
+        ts(w("l_a"), ind(w("ts"), w("o_e", 0, 1)), 2.0 ** -13, ALU.mult)
+        copy(w("vi"), ind(w("ts"), w("o_e", 0, 1)))
+        vi = w("vi", 0, 8)
+        ts(w("r1"), w("l_s"), hf, ALU.subtract)
+        ts(w("li", 0, 8), vi, 255, ALU.bitwise_and)
+        ts(w("li", 8, 16), vi, 4, ALU.logical_shift_right, 255, ALU.bitwise_and)
+        ts(w("r2"), w("l_s"), col("pc", 5), ALU.subtract, 1000.0, ALU.mult)
+        copy(w("l_k"), w("li"))
+        tt(w("r3"), w("r1"), w("r2"), ALU.max)
+        la, lb, le = w("l_a", 0, 8), w("l_k", 0, 8), w("l_k", 8, 16)
+
+        def tw_(b):
+            return w("win", 384 * b + 128, 384 * b + 384)
+
+        def fw(b):
+            return part("win", b, 384)
+
+        for b in range(4):
+            act(part("ag", b), ind(tw_(b), la), ACT.Copy, scale=2.0 ** -6)
+        for b in range(4):
+            tt(w("zt", b, 512, 4), ind(part("tw", b, 256), lb), part("ag", b), ALU.add)
+        tt(w("r4"), w("r3"), w("c128"), ALU.min)
+        quant(w("zq"), w("zp"), w("zt"))
+        copy(w("l_x"), w("r4"))
+        for b in range(4):
+            act(part("te", b), ind(tw_(b), le), ACT.Copy)
+        for b in range(4):
+            mm(4 + b, 128, part("wq", b), part("wp", b), w("zq"), w("zp"))
+        for b in range(4):
+            tt(w("win", 384 * b, 384 * b + 128), w("ps%d" % (4 + b), 0, 128), part("te", b), ALU.add)
+        for b in range(2):
+            act(w("xs", b, 1024, 4), ind(fw(b), w("l_x")), ACT.Copy, scale=2.0 ** -5)
+        ts(w("xs", 512 + 2, 1024, 4), ind(fw(2), w("l_x", 8, 16)), 2.0 ** -5, ALU.mult)
+        act(w("xs", 2, 512, 4), ind(fw(2), w("l_x", 0, 8)), ACT.Copy, scale=2.0 ** -5)
+        ts(w("xs", 3, 1024, 4), ind(fw(3), w("l_x")), 2.0 ** -5, ALU.mult)
+        X = "xs"
+
+    quant_x(X)
+    for h in range(2):
+        mm(h, 128, w("vq"), w("vp"), part("xq", h), part("xp", h))
+    dma("Y", T.oc[:], u8(w("xq")))
+    for k in range(4):
+        dma("Y" if k < 2 else "S", T.osc[4 * k:4 * k + 4, :], (T.xp[32 * k:32 * k + 4, :], w("xp")[1]))
+    copy(part("yb", 0), w("ps0", 0, 128))
+    act(part("yb", 1), w("ps1", 0, 128), ACT.Copy)
+    dma("Y", T.y[:, 0:128], part("yb", 0))
+    dma("S", T.y[:, 128:256], part("yb", 1))
+
+    _emit(eng, ops, T)
+
+
+def _emit(eng, ops, T):
+    known = {q: 0 for q in eng}
+    seen = {}
+    for n, o in enumerate(ops):
+        deps = set()
+        for wr, accs in ((False, o["r"]), (True, o["w"])):
+            for name, m in accs:
+                psum = name.startswith("ps") and name[2:].isdigit()
+                for k, kw, km in seen.get(name, []):
+                    if psum and ops[k]["q"] != o["q"]:
+                        deps.add(k)
+                    elif (wr or kw) and (m & km):
+                        deps.add(k)
+        for wr, accs in ((False, o["r"]), (True, o["w"])):
+            for name, m in accs:
+                seen.setdefault(name, []).append((n, wr, m))
+        deps.discard(n)
+        o["waits"], o["sig"] = [], False
+        if o["kind"] == "x":
+            o["clo"] = 0
+            continue
+        q = o["q"]
+        for k in sorted(deps, reverse=True):
+            if not known[q] >> k & 1:
+                o["waits"].append(k)
+                ops[k]["sig"] = True
+                known[q] |= ops[k]["clo"] | 1 << k
+        o["clo"] = known[q]
+    tail = [k for k, o in enumerate(ops) if o["kind"] == "r" and not o["sig"]]
+    tail_d = [k for k, o in enumerate(ops) if o["kind"] == "d" and not o["sig"]]
+    for k in tail_d:
+        ops[k]["sig"] = True
+    waiters = {}
+    for n, o in enumerate(ops):
+        for k in o["waits"]:
+            waiters.setdefault(k, []).append(n)
+    groups = {}
+    for n, o in enumerate(ops):
+        if o["kind"] in ("c", "d") and o["sig"]:
+            groups.setdefault((o["kind"], tuple(waiters.get(n, [-n]))), []).append(n)
+    pool = {"c": [[0, 0] for _ in range(NC)], "d": [[0, 0] for _ in range(ND)]}
+    for (kind, _), members in groups.items():
+        step = 1 if kind == "c" else 16
+        for s, st in enumerate(pool[kind]):
+            if all(st[0] & ~ops[k]["clo"] == 0 for k in members):
+                st[0] = _bits(members)
+                st[1] += step * len(members)
+                for k in members:
+                    ops[k]["sem"] = ("%s%d" % (kind, s), st[1])
+                    ops[k]["step"] = step
+                break
+        else:
+            raise ValueError("out of semaphores")
+    for o in ops:
+        if o["kind"] == "x":
+            continue
+        e = eng[o["q"]]
+        for sem in dict.fromkeys(ops[k]["sem"] for k in o["waits"]):
+            e.wait_ge(T.sem[sem[0]], sem[1])
+        ins = o["fn"](e)
+        if o["kind"] != "r" and o["sig"]:
+            ins.then_inc(T.sem[o["sem"][0]], o["step"])
+    for k in tail:
+        eng["G"].wait_ge(T.sem[ops[k]["sem"][0]], ops[k]["sem"][1])
+    for k in tail_d:
+        eng[ops[k]["q"]].wait_ge(T.sem[ops[k]["sem"][0]], ops[k]["sem"][1])

@@ -1,12 +1,17 @@
+from concourse.bass import DstId, RemoteDMATransfer
 from concourse.mybir import dt, AluOpType, ActivationFunctionType
 
 ALU, ACT = AluOpType, ActivationFunctionType
 F, B, I, U, X4, U8 = "float32", "bfloat16", "int32", "uint16", "float8_e4m3fn_x4", "uint8"
 MASKS = [1, 2, 4]
-NV = 8
+NV = 9
 NS = 16 - NV
+INT = True
+WV = 0
 BIG = 1.0e29
-WM = 8193.0
+WM = 8193
+LISTS = {"o_u": (0, 16), "o_d": (16, 4), "o_s": (20, 24), "o_m": (44, 24), "o_i": (68, 16), "o_t": (84, 2),
+         "o_c": (86, 32), "o_4": (118, 16), "o_e": (134, 2)}
 
 
 def _sb(n, d):
@@ -19,27 +24,23 @@ SCRATCH = {
     "vb": _sb(512, B), "vq": _sb(128, X4), "vp": _sb(128, U8),
     "wq": _sb(512, X4), "wp": _sb(512, U8),
     "ones": _sb(128, B), "ident": _sb(128, B), "eb": _sb(520, B), "eq": _sb(512, X4), "ep": _sb(512, U8),
-    "pi": _sb(2, I), "pb": _sb(8, I), "pf": _sb(8, F), "pc": _sb(8, F), "i16": _sb(16, F), "ibc": _sb(16, F),
-    "jj": _sb(384, B), "ii": _sb(256, F), "ka": _sb(256, F), "kb": _sb(256, F), "tmpc": _sb(8, F),
-    "iu": _sb(16, I), "i01": _sb(16, F), "tmpb": _sb(48, F),
-    "o_u": _sb(16, U), "o_d": _sb(4, U), "o_m": _sb(24, U), "o_i": _sb(16, U), "o_b": _sb(16, U),
-    "o_s": _sb(8, U), "o_e": _sb(2, U), "o_c": _sb(16, U),
-    "kmax": _sb(384, B), "kw": _sb(256, F), "kq": _sb(256, B), "km": _sb(256, F), "c128": _sb(16, F),
-    "o1": _sb(264, F), "i2": _sb(64, F), "o2": _sb(64, F), "s0": _sb(384, F), "s1": _sb(256, F),
+    "gb": _sb(224, F), "gc": _sb(224, F), "pc": _sb(16, F), "i16": _sb(32, F), "ibc": _sb(16, F), "i01": _sb(16, F),
+    "ist": _sb(16, F), "jj": _sb(256, B), "ft": _sb(136, F), "lo": _sb(136, U),
+    "kmax": _sb(256, B), "kz": _sb(512, B), "ka": _sb(32, F), "kb": _sb(32, F),
+    "o1": _sb(288, F), "s0": _sb(384, F), "s1": _sb(512, F),
     "tt": _sb(1024, B), "win": _sb(4 * 384, B), "tw": _sb(1024, B),
-    "sm": _sb(384, F), "pm": _sb(392, F), "bc": _sb(256, F), "row": _sb(256, F), "bst": _sb(16, F),
-    "cm": _sb(256, F), "cnt": _sb(256, F), "vx": _sb(256, F), "ee": _sb(256, B), "es": _sb(256, B), "e2": _sb(16, F),
-    "cb": _sb(NV * 256, B), "so": _sb(NV * 128, B), "sg": _sb(NS * 256, B), "jk": _sb(NS * 256, B),
-    "aca": _sb(16, F), "acb": _sb(16, F), "t1": _sb(16, F), "t2": _sb(16, F), "l_s": _sb(16, U),
-    "sw": _sb(272, F), "tb": _sb(256, F), "ts": _sb(256, F), "vi": _sb(16, I), "li": _sb(16, I),
-    "l_k": _sb(16, U), "l_a": _sb(16, U),
-    "r1": _sb(16, F), "r2": _sb(16, F), "r3": _sb(16, F), "r4": _sb(16, F), "l_x": _sb(16, U),
+    "sm": _sb(384, F), "pm": _sb(640, F), "bc": _sb(256, F), "bst": _sb(32, F),
+    "ee": _sb(512, B), "es": _sb(512, B), "q1": _sb(32, F), "ac": _sb(128, F), "pw": _sb(256, F), "pr": _sb(256, F),
+    "cb": _sb(NV * 256, B), "so": _sb(16 * 128, B), "sg": _sb(NS * 256, B), "jk": _sb(NS * 256, B),
+    "l_s": _sb(16, U), "sw": _sb(272, I if INT else F), "tb": _sb(256, I if INT else F), "i2": _sb(64, F),
+    "o2": _sb(64, F), "vi": _sb(16, I), "li": _sb(32, I), "l_k": _sb(32, U), "l_a": _sb(16, U),
+    "xa": _sb(32, F), "xb": _sb(32, F), "xo": _sb(32, F), "l_x": _sb(16, U),
     "ag": _sb(512, F), "te": _sb(512, F), "zt": _sb(512, B), "zq": _sb(128, X4), "zp": _sb(128, U8),
     "yb": _sb(256, F),
 }
 for _r in range(3):
-    SCRATCH["ss%d" % _r] = _sb(32, F)
-    SCRATCH["sl%d" % _r] = _sb(32, F)
+    SCRATCH["ss%d" % _r] = _sb(64, F)
+    SCRATCH["sl%d" % _r] = _sb(48, F)
     SCRATCH["tq%d" % _r] = _sb(256, X4)
     SCRATCH["tp%d" % _r] = _sb(256, U8)
     SCRATCH["lq%d" % _r] = _sb(256, X4)
@@ -47,7 +48,7 @@ for _r in range(3):
 for _k in range(8):
     SCRATCH["ps%d" % _k] = ("psum", [128, 512], F)
 
-NC, ND = 100, 16
+NC, ND = 110, 16
 SEMAPHORES = (["c%d" % k for k in range(NC)] + ["d%d" % k for k in range(ND)]
               + ["%s%d" % (n, r) for n in ("as", "aq", "gs", "gq", "gp") for r in range(3)])
 
@@ -129,11 +130,14 @@ def rank_program(g, core, T, topo):
             kw["accum_out"] = ap(accum)
         op("S", "c", lambda e: e.activation(ap(o), ap(i), f, **kw), [i, bias, scale], [o, accum])
 
+    def lin(o, i, scale=None, bias=None):
+        act(o, i, ACT.Identity, bias=bias, scale=scale)
+
     def mm(bank, n, lq, lp, rq, rp):
         o = w("ps%d" % bank, 0, n)
         op("P", "c", lambda e: e.matmul_mx(ap(o), ap(lq), ap(lp), ap(rq), ap(rp), True, True), [lq, lp, rq, rp], [o])
 
-    def iota(o, pat, base, cm, small):
+    def iota(o, pat, base, cm=0, small=True):
         if small:
             op("G", "c", lambda e: e.iota(ap(o), pat, base, cm, allow_small_or_imprecise_dtypes=True), [], [o])
         else:
@@ -149,6 +153,13 @@ def rank_program(g, core, T, topo):
         rid, pid, _ = topo.addr(dst)
         op("G", "r", lambda e: e.remote_dma(o, ap(i), T.sem[rsem], T.sem[lsem], pid, rid, _bits(engs)),
            [i], [], (lsem, len(engs)))
+
+    def fold(dst, o, a, b, rsem, lsem, engs):
+        rid, pid, _ = topo.addr(dst)
+        op("G", "r", lambda e: e.remote_dma_fused(
+            [RemoteDMATransfer(dst_ids=[DstId(rid=rid, pnc=pid)], dma_engine_mask=_bits(engs), remote_sem=T.sem[rsem],
+                               srcs=[ap(a), ap(b)], dsts=[o], alu_op=1)], local_sem=T.sem[lsem]),
+           [a, b], [], (lsem, len(engs)))
 
     def arrive(views, sem, n):
         op("X", "x", None, [], views, (sem, n))
@@ -167,69 +178,95 @@ def rank_program(g, core, T, topo):
         for b in range(4):
             mm(b, 256, part("eq", b), part("ep", b), w(q), w(p))
 
+    def lst(name, a=0, b=None, table="lo"):
+        o, n = LISTS[name]
+        return w(table, o + a, o + (n if b is None else b))
+
+    def flt(name, a=0, b=None):
+        return lst(name, a, b, "ft")
+
     dma("Y", w("x0"), T.x[:])
     dma("S", w("ub"), T.u[:])
     memset(w("ones"), 1.0)
-    iota(w("pi", 0, 1), [[0, 1]], 0, 1, False)
-    iota(w("i16"), [[16, 16]], 0, 0, True)
-    op("G", "c", lambda e: e.affine_select(T.ident[:], T.ones[:], [[-1, 128]], ALU.is_equal, 0.0, 0, 1),
-       [w("ones")], [w("ident")])
-    iota(w("iu", 0, 8), [[16, 8]], 0, 0, False)
-    iota(w("iu", 8, 16), [[32, 4], [-16, 2]], 16, 0, False)
-    iota(w("jj"), [[0, 24], [1, 16]], 0, 0, True)
-    iota(w("ibc"), [[1, 8], [0, 2]], 0, 0, True)
-    iota(w("i01"), [[0, 8], [1, 2]], 0, 0, True)
-    iota(w("ii"), [[1, 16], [0, 16]], 0, 0, True)
-    memset(w("o1", 256, 264), 0.0)
-    p_ = w("pi", 0, 1)
-    for k, m in enumerate((15, 16, 31, 14, 1, 6)):
-        ts(col("pb", k), p_, m, ALU.bitwise_and)
-    ts(col("pb", 6), p_, 4, ALU.logical_shift_right, 1, ALU.bitwise_and)
+    BASES = [("d", -1, (1, 0, 1)), ("y", 15, (0, 16, 0)), ("q", 0, (0, 2, 1)), ("hf", 0, (16, 0, 0)),
+             ("rf", 0, (16, 2, 1)), ("u", 128, (16, 16, 0))]
+    base = {}
+    for k, (name, b0, (sh, sb, st)) in enumerate(BASES):
+        iota(part("gb", k, 32), [[sh, 2], [sb, 8], [st, 2]], b0)
+        base[name] = 32 * k
+        if k == 0:
+            op("G", "c", lambda e: e.affine_select(T.ident[:], T.ones[:], [[-1, 128]], ALU.is_equal, 0.0, 0, 1),
+               [w("ones")], [w("ident")])
+    base["oe"] = 192
+    for h in range(2):
+        iota(part("gb", 12 + h, 16), [[0, 2], [32, 4], [128, 2]], 16 * h)
+
+    def bs(name, n=1):
+        return w("gc", base[name], base[name] + n)
+
+    iota(flt("o_u"), [[16, 2], [32, 4], [0, 2]], 0)
+    iota(w("ibc"), [[1, 8], [0, 2]], 0)
+    iota(w("i16"), [[16, 32]], 0)
+    iota(w("ist"), [[32, 8], [256, 2]], 0)
+    iota(w("i01"), [[0, 8], [32, 2]], 0)
+    iota(flt("o_i"), [[16, 16]], 15)
+    iota(flt("o_c"), [[1, 32]], 0)
+    iota(flt("o_4"), [[4, 16]], 0)
     memset(w("eb"), 0.0)
-    copy(w("pf", 0, 7), w("pb", 0, 7))
-    qf, hf, rf, q14, par, q6, hb = [col("pf", k) for k in range(7)]
+    memset(w("o1", 256, 288), 0.0)
     copy(w("eb", 3, 515, 4), w("ident"))
-    tt(col("pc", 0), par, hb, ALU.is_equal)
-    ts(col("pc", 1), q14, 16.0, ALU.mult, -255.0, ALU.add)
-    ts(col("pc", 2), par, 128.0, ALU.mult, hf, ALU.add)
-    ts(col("pc", 3), hf, 2.0, ALU.mult, -256.0, ALU.add)
-    ts(w("tmpc", 0, 4, 2), w("i16", 0, 2), col("pc", 1), ALU.add)
-    ts(w("tmpc", 1, 4, 2), w("i16", 0, 2), col("pc", 1), ALU.add)
-    ts(col("pc", 4), qf, 16.0, ALU.mult)
-    ts(col("pc", 5), hf, 127.0, ALU.add)
-    ts(w("o_d"), w("tmpc", 0, 4), col("pc", 0), ALU.mult, 256.0, ALU.add)
-    ts(col("tmpc", 4), q6, 16.0, ALU.mult, col("pc", 2), ALU.add)
-    copy(w("o_u"), w("iu"))
     for b in range(4):
         quant(part("eq", b), part("ep", b), w("eb", 3 - b, 515 - b))
+    trans(w("gc"), w("gb"))
+    same, q_, hf, rf = col("pc", 0), bs("q"), bs("hf"), bs("rf")
+    act(same, bs("d"), ACT.Abs)
+    lin(col("pc", 1), bs("y"), 2.0, -285.0)
+    lin(col("pc", 3), hf, 15.0, q_)
+    lin(col("pc", 2), col("pc", 1), same, 256.0)
+    lin(flt("o_d"), w("ibc", 0, 4), 16.0, col("pc", 2))
+    lin(flt("o_s", 0, 8), w("i16", 1, 16, 2), None, col("pc", 3))
+    lin(flt("o_s", 8, 24), w("ist"), None, rf)
     quant(w("uq"), w("up"), w("ub"))
+    lin(flt("o_m", 0, 8), bs("hf", 8), None, rf)
+    lin(flt("o_m", 8, 24), w("i01"), None, q_)
+    lin(flt("o_t"), bs("u", 2), same, bs("y"))
+    lin(flt("o_e"), bs("oe", 2))
+
+    def late_counts():
+        iota(w("jj"), [[0, 16], [1, 16]], 0)
+        iota(w("ka"), [[WM - 2, 2], [0, 16]], -WM)
+        iota(w("ac"), [[0, 128]], 0)
+        iota(w("xa", 0, 32, 2), [[0, 16]], 1000)
+        iota(w("sw", 0, 16), [[0, 16]], 0, small=not INT)
 
     def late_constants():
-        ts(w("o_s"), w("i16", 0, 8), 2.0, ALU.mult, rf, ALU.add)
-        ts(w("o_m", 0, 16), w("i16"), 0.0, ALU.mult, rf, ALU.add)
-        ts(col("pc", 6), hf, -2.0, ALU.mult, 16.0, ALU.add)
+        copy(w("lo", 44, 136), w("ft", 44, 136))
         ts(w("kmax"), w("jj"), 0.0, ALU.is_equal, -BIG, ALU.mult)
-        ts(col("pc", 7), col("pc", 6), rf, ALU.add)
-        memset(w("pm", 0, 8), 0.0)
-        ts(w("o_i"), w("i16"), 15.0, ALU.add)
-        ts(w("o_c"), w("i16"), 0.0625, ALU.mult)
-        ts(w("o_m", 16, 24), w("i16", 0, 8), 0.0, ALU.mult, col("pc", 7), ALU.add)
-        ts(w("tmpb", 0, 16), w("ibc"), 16.0, ALU.mult, hf, ALU.add)
-        ts(w("tmpb", 16, 32), w("i01"), hb, ALU.is_equal)
-        ts(w("kw"), w("jj", 0, 256), 0.0, ALU.not_equal)
-        ts(w("tmpb", 0, 16), w("tmpb", 0, 16), -256.0, ALU.add)
-        ts(w("tmpb", 32, 48), w("ibc"), 16.0, ALU.mult, 271.0, ALU.add)
-        ts(w("kq"), w("jj", 0, 256), qf, ALU.not_equal)
-        tt(w("tmpb", 0, 16), w("tmpb", 0, 16), w("tmpb", 16, 32), ALU.mult)
-        memset(w("kw", 15, 256, 16), WM)
-        ts(col("o_e", 0), col("tmpc", 4), 15.0, ALU.add)
-        tt(w("tmpb", 16, 32), w("tmpb", 0, 16), w("tmpb", 32, 48), ALU.add)
-        ts(w("c128"), w("i16"), 128.0, ALU.add, qf, ALU.add)
-        memset(w("sw"), -1.0)
-        copy(w("o_b"), w("tmpb", 16, 32))
-        act(w("ka"), w("ii"), ACT.Identity, bias=col("pc", 4), scale=131328.0)
-        act(w("kb"), w("kq"), ACT.Copy, scale=-67108864.0)
-        tt(w("km"), w("ka"), w("kb"), ALU.add)
+        ts(w("kz", 0, 256), w("jj", 0, 256), 0.0, ALU.not_equal)
+        ts(w("kz", 256, 512), w("jj", 0, 256), q_, ALU.not_equal)
+
+    def later_constants():
+        lin(col("pc", 4), q_, 16.0, 16.0 * WM)
+        lin(w("kb", 16, 16 + NV), bs("hf", NV), 2.0, -256.0)
+        lin(col("pc", 5), hf, 8208.0, col("pc", 4))
+        lin(w("kb", 16 + NV, 32), bs("hf", NS), 2.0)
+        lin(col("pc", 6), hf, -1.0, 128.0)
+        lin(w("kb", 0, 16), w("ibc"), 262656.0, col("pc", 5))
+        lin(col("pc", 7), hf, -1000.0, 500.0)
+        lin(w("xb", 1, 32, 2), w("i16", 8, 24), None, q_)
+
+    def tw_(b):
+        return w("win", 384 * b + 128, 384 * b + 384)
+
+    def fw(b):
+        return part("win", b, 384)
+
+    def bank(b, n=256):
+        return w("ps%d" % b, 0, n)
+
+    def own_scores():
+        for h in range(2):
+            mm(5 + h, 256, part("u0q", h), part("u0p", h), w("xq"), w("xp"))
 
     X = "x0"
     for R, mask in enumerate(MASKS):
@@ -246,128 +283,137 @@ def rank_program(g, core, T, topo):
             dma("Y", u8(w("wq")), (T.wc[:], w("x0")[1]))
             dma("Y", w("wp"), T.ws[:])
             dma("Y", w("vb"), T.v[:])
-            act(w("u0p"), ind(w("up"), w("o_u")), ACT.Copy)
+        if R > 0:
+            own_scores()
         unpack("xq", "xp")
         for h in range(2):
-            trans(part("o1", h), w("ps%d" % (4 + 3 * h), 0, 128))
-        copy(w("i2"), ind(w("o1"), w("o_d")))
-        trans(w("o2"), w("i2"))
-        for h in range(2):
-            tt(part("ss%d" % R, h, 16), part("o2", 2 * h, 16), part("o2", 2 * h + 1, 16), ALU.add)
-        send(peer, T["sl%d" % R][:], w("ss%d" % R), "as%d" % R, "gs%d" % R, e_s)
+            trans(part("o1", h), bank(4 + 3 * h, 128))
+            if R == 0 and h == 0:
+                copy(w("lo", 0, 44), w("ft", 0, 44))
+                act(w("u0p"), ind(w("up"), lst("o_u")), ACT.Copy)
+        copy(w("i2"), ind(w("o1"), lst("o_d")))
+        trans(w("ss%d" % R), w("i2"))
+        fold(peer, T["sl%d" % R][:], w("ss%d" % R, 0, 48), w("ss%d" % R, 16, 64), "as%d" % R, "gs%d" % R, e_s)
         if R == 0:
+            late_counts()
             op("V", "c", lambda e: e.tensor_copy(T.u0q[:].bitcast(dt.uint32),
-                                                 T.uq[:].bitcast(dt.uint32).indirect(T.o_u[:])),
-               [w("uq"), w("o_u")], [w("u0q")])
+                                                 T.uq[:].bitcast(dt.uint32).indirect(lst("o_u")[0])),
+               [w("uq"), lst("o_u")], [w("u0q")])
+            own_scores()
+            act(w("tt", 3, 1024, 4), bank(3), ACT.Copy)
         for h in range(2):
-            mm(5 + h, 256, part("u0q", h), part("u0p", h), w("xq"), w("xp"))
+            act(part("s1", h, 256), bank(5 + h), ACT.Copy)
+        act(w("s0"), ind(w("s1"), lst("o_s")), ACT.Copy)
+        if R > 0:
+            act(w("tt", 3, 1024, 4), bank(3), ACT.Copy)
         for b in range(3):
-            act(w("tt", b, 1024, 4), w("ps%d" % b, 0, 256), ACT.Copy)
-        copy(w("tt", 3, 1024, 4), w("ps3", 0, 256))
+            copy(w("tt", b, 1024, 4), bank(b))
         quant(w("tq%d" % R), w("tp%d" % R), w("tt"))
         send(peer, T["lq%d" % R][:].bitcast(dt.uint8), u8(w("tq%d" % R)), "aq%d" % R, "gq%d" % R, e_q)
         send(peer, T["lp%d" % R][:], w("tp%d" % R), "aq%d" % R, "gp%d" % R, e_q)
-        act(w("s1"), w("ps6", 0, 256), ACT.Copy)
-        act(w("s0", 0, 256), w("ps5", 0, 256), ACT.Copy)
         if R == 0:
             late_constants()
-        act(w("s0", 256, 384), ind(w("s1"), w("o_s")), ACT.Copy)
+            later_constants()
         for b in range(4):
-            ts(w("win", 384 * b + 128, 384 * b + 384), w("tt", b, 1024, 4), 32.0, ALU.mult)
-        if R == 1:
-            quant(w("vq"), w("vp"), w("vb"))
+            if b < WV:
+                ts(tw_(b), w("tt", b, 1024, 4), 32.0, ALU.mult)
+            else:
+                act(tw_(b), bank(b), ACT.Copy, scale=32.0)
         arrive([w("sl%d" % R)], "as%d" % R, len(e_s))
         arrive([w("lq%d" % R), w("lp%d" % R)], "aq%d" % R, 2 * len(e_q))
-        tt(w("sm"), ind(w("sl%d" % R), w("o_m")), w("s0"), ALU.add)
-        scan(w("pm", 8, 392), w("kmax"), w("sm"), 0.0, ALU.add, ALU.max)
-        act(w("bc"), ind(w("pm", 8, 392), w("o_b")), ACT.Copy)
-        copy(w("bst"), w("pm", 23, 264, 16))
-        tt(w("cm"), ind(w("bst"), w("o_c")), w("pm", 7, 263), ALU.is_gt)
-        trans(w("row"), w("bc"))
-        scan(w("cnt"), w("cm"), w("kw"), 0.0, ALU.add, ALU.mult)
+        row0 = 384
+        tt(w("sm", 128, 384), ind(w("sl%d" % R), lst("o_m", 8, 24)), w("s0", 128, 384), ALU.add)
+        tt(w("sm", 0, 128), ind(w("sl%d" % R), lst("o_m", 0, 8)), w("s0", 0, 128), ALU.add)
+        scan(w("pm", 128, 384), w("kmax"), w("sm", 128, 384), 0.0, ALU.add, ALU.max)
+        scan(w("pm", 0, 128), w("kmax", 0, 128), w("sm", 0, 128), 0.0, ALU.add, ALU.max)
+        act(w("bc"), ind(w("pm", 128, 384), lst("o_i")), ACT.Copy)
+        copy(w("bst", 0, 16), w("pm", 143, 384, 16))
+        act(w("bst", 16, 32), ind(w("pm", 0, 384), lst("o_t", 0, 1)), ACT.Copy)
+        for h in range(2):
+            tt(part("ee", h), ind(w("bst", 0, 16), lst("o_c", 8 * h, 8 * h + 8)), part("pm", 1 + h), ALU.is_equal)
+            if h == 0:
+                trans(w("pm", row0, row0 + 256), w("bc"))
+        tt(w("ee", 256, 512), ind(w("bst", 16, 32), lst("o_c", 0, 16)), w("pm", 384, 640), ALU.is_equal)
 
         def own(k):
-            return col("bst", k)
+            return col("bst", 16 + k)
+
+        def row(a=0, b=256):
+            return w("pm", row0 + a, row0 + b)
+
+        def slot(k, n):
+            return col("ac", 64 + 4 * k + n)
 
         def v_cmp(k):
             a = 16 * (k + 1)
-            ts(w("cb", 256 * k, 256 * k + a), w("row", 0, a), own(k), ALU.is_ge, 2.0, ALU.mult)
-            ts(w("cb", 256 * k + a, 256 * k + 256), w("row", a, 256), own(k), ALU.is_gt, 2.0, ALU.mult)
+            ts(w("cb", 256 * k, 256 * k + a), row(0, a), own(k), ALU.is_ge, 2.0, ALU.mult)
+            ts(w("cb", 256 * k + a, 256 * k + 256), row(a, 256), own(k), ALU.is_gt, 2.0, ALU.mult)
 
         def v_sum(k):
-            scan(part("so", k), part("cb", 2 * k), part("cb", 2 * k + 1), col("e2", k), ALU.add, ALU.add)
+            scan(part("so", k), part("cb", 2 * k), part("cb", 2 * k + 1), slot(k, 0), ALU.add, ALU.add)
 
         def s_cmp(k):
-            act(part("sg", k - NV, 256), w("row"), ACT.Sign, bias=own(k), scale=-1.0)
+            act(part("sg", k - NV, 256), row(), ACT.Sign, bias=own(k), scale=-1.0)
 
         def s_sum(k):
             o, a = 256 * (k - NV), 16 * (k + 1)
             if a < 256:
-                act(w("jk", o + a, o + 256), w("sg", o + a, o + 256), ACT.Sign, bias=-0.5, scale=-1.0, accum=col("acb", k))
-                act(w("jk", o, o + a), w("sg", o, o + a), ACT.Sign, bias=0.5, scale=-1.0, accum=col("aca", k))
-            else:
-                act(w("jk", o, o + a), w("sg", o, o + a), ACT.Relu, accum=col("aca", k))
+                act(w("jk", o + a, o + 256), w("sg", o + a, o + 256), ACT.Sign, bias=-0.5, scale=-1.0, accum=slot(k, 2))
+            act(w("jk", o, o + a), w("sg", o, o + a), ACT.Sign, bias=0.5, scale=-1.0, accum=slot(k, 1))
 
+        v_cmp(0)
+        scan(w("es"), w("kz"), w("ee"), 0.0, ALU.mult, ALU.add)
+        v_cmp(1)
+        tt(w("q1"), w("es", 15, 512, 16), w("ka"), ALU.mult)
+        v_cmp(2)
+        tt(w("ac", 0, 128, 4), w("q1"), w("kb"), ALU.add)
         s_cmp(NV)
         for k in range(NV, 16):
             if k + 1 < 16:
                 s_cmp(k + 1)
             s_sum(k)
-        tt(w("ee"), ind(w("bst"), w("o_c")), w("row"), ALU.is_equal)
-        tt(w("vx"), ind(w("cnt"), w("o_i")), w("km"), ALU.add)
-        scan(w("es"), w("kq"), w("ee"), 0.0, ALU.mult, ALU.add)
-        v_cmp(0)
-        ts(w("e2"), w("es", 15, 256, 16), -2.0, ALU.mult, col("pc", 3), ALU.add)
+            if k == NV + 2:
+                act(w("pw"), ind(w("ac", 0, 64), lst("o_4")), ACT.Copy)
         for k in range(NV):
-            if k == 1:
-                ts(col("t1", 15), col("e2", 15), 0.5, ALU.mult, 384.0, ALU.add)
-            if k + 1 < NV:
-                v_cmp(k + 1)
-            else:
-                tt(w("t1", NV, 15), w("acb", NV, 15), w("e2", NV, 15), ALU.add)
+            if k + 3 < NV:
+                v_cmp(k + 3)
             v_sum(k)
-        tt(w("t2", NV, 15), w("aca", NV, 15), w("t1", NV, 15), ALU.add)
-        ts(w("l_s", 0, NV), w("so", 127, NV * 128, 128), 0.5, ALU.mult, 128.0, ALU.add)
-        ts(w("l_s", NV, 15), w("t2", NV, 15), 0.5, ALU.mult, 256.0, ALU.add)
-        ts(col("l_s", 15), col("aca", 15), -1.0, ALU.mult, col("t1", 15), ALU.add)
+        trans(part("pr", 0), part("pw", 0))
+        scan(w("so", 128 * NV + 31, 2048, 32), w("kz", 0, 16 * NS, 4), w("ac", 64 + 4 * NV, 128), 0.0, ALU.mult, ALU.add)
+        twice = w("so", 127, 2048, 128)
+        trans(part("pr", 1), part("pw", 1))
+        ts(w("l_s"), twice, 0.5, ALU.mult, 128.0, ALU.add)
+        ts(w("xb", 0, 32, 2), twice, 0.5, ALU.mult, col("pc", 6), ALU.add)
+        ts(w("xa", 1, 32, 2), twice, 500.0, ALU.mult, col("pc", 7), ALU.add)
+        scatter(w("sw"), w("l_s"), w("pr"))
         unpack("lq%d" % R, "lp%d" % R)
         for b in range(4):
-            act(part("tw", b, 256), w("ps%d" % b, 0, 256), ACT.Copy, scale=0.5)
-        scatter(w("sw"), w("l_s"), w("vx"))
+            act(part("tw", b, 256), bank(b), ACT.Copy, scale=0.5)
+        scan(w("xo"), w("xa"), w("xb"), 0.0, ALU.max, ALU.min)
         trans(part("tb", 0), w("sw", 0, 128))
         trans(part("tb", 1), w("sw", 16, 144))
-        for h in range(2):
-            scan(part("ts", h), w("kmax", 0, 128), part("tb", h), 0.0, ALU.add, ALU.max)
-        ts(w("l_a"), ind(w("ts"), w("o_e", 0, 1)), 2.0 ** -13, ALU.mult)
-        copy(w("vi"), ind(w("ts"), w("o_e", 0, 1)))
-        vi = w("vi", 0, 8)
-        ts(w("r1"), w("l_s"), hf, ALU.subtract)
-        ts(w("li", 0, 8), vi, 255, ALU.bitwise_and)
-        ts(w("li", 8, 16), vi, 4, ALU.logical_shift_right, 255, ALU.bitwise_and)
-        ts(w("r2"), w("l_s"), col("pc", 5), ALU.subtract, 1000.0, ALU.mult)
-        copy(w("l_k"), w("li"))
-        tt(w("r3"), w("r1"), w("r2"), ALU.max)
-        la, lb, le = w("l_a", 0, 8), w("l_k", 0, 8), w("l_k", 8, 16)
-
-        def tw_(b):
-            return w("win", 384 * b + 128, 384 * b + 384)
-
-        def fw(b):
-            return part("win", b, 384)
+        copy(w("l_x"), w("xo", 1, 32, 2))
+        picked = ind(w("tb"), lst("o_e", 0, 1))
+        ts(w("l_a"), picked, 2.0 ** -13, ALU.mult)
+        ts(w("li", 0, 16), picked, 255, ALU.bitwise_and)
+        ts(w("li", 16, 32), picked, 4, ALU.logical_shift_right, 255, ALU.bitwise_and)
+        la, lb, le = w("l_a", 0, 8), w("l_k", 0, 8), w("l_k", 16, 24)
+        copy(lb, w("li", 0, 8))
+        copy(le, w("li", 16, 24))
 
         for b in range(4):
             act(part("ag", b), ind(tw_(b), la), ACT.Copy, scale=2.0 ** -6)
         for b in range(4):
             tt(w("zt", b, 512, 4), ind(part("tw", b, 256), lb), part("ag", b), ALU.add)
-        tt(w("r4"), w("r3"), w("c128"), ALU.min)
         quant(w("zq"), w("zp"), w("zt"))
-        copy(w("l_x"), w("r4"))
+        if R == 1:
+            quant(w("vq"), w("vp"), w("vb"))
         for b in range(4):
             act(part("te", b), ind(tw_(b), le), ACT.Copy)
         for b in range(4):
             mm(4 + b, 128, part("wq", b), part("wp", b), w("zq"), w("zp"))
         for b in range(4):
-            tt(w("win", 384 * b, 384 * b + 128), w("ps%d" % (4 + b), 0, 128), part("te", b), ALU.add)
+            tt(w("win", 384 * b, 384 * b + 128), bank(4 + b, 128), part("te", b), ALU.add)
         for b in range(2):
             act(w("xs", b, 1024, 4), ind(fw(b), w("l_x")), ACT.Copy, scale=2.0 ** -5)
         ts(w("xs", 512 + 2, 1024, 4), ind(fw(2), w("l_x", 8, 16)), 2.0 ** -5, ALU.mult)

@@ -7,11 +7,16 @@ MASKS = [1, 2, 4]
 NV = 9
 NS = 16 - NV
 INT = True
-WV = 0
+PICKS = [("A", 0, 0, 0), ("A", 1, 0, 0), ("A", 2, 0, 0), ("A", 3, 0, 0), ("S", 0, 0, 16), ("S", 1, 0, 16), ("V", 2, 0, 8), ("V", 3, 0, 8), ("V", 2, 8, 16), ("S", 3, 8, 16), ("Q", 0, 0, 0), ("Q", 1, 0, 0)]
+BH = 2
+E0 = True
+XL = True
+RAW = True
+WV = 2
 BIG = 1.0e29
 WM = 8193
 LISTS = {"o_u": (0, 16), "o_d": (16, 4), "o_s": (20, 24), "o_m": (44, 24), "o_i": (68, 16), "o_t": (84, 2),
-         "o_c": (86, 32), "o_4": (118, 16), "o_e": (134, 2)}
+         "o_c": (86, 16), "o_4": (102, 16), "o_e": (118, 2)}
 
 
 def _sb(n, d):
@@ -23,20 +28,20 @@ SCRATCH = {
     "ub": _sb(512, B), "uq": _sb(128, X4), "up": _sb(128, U8), "u0q": _sb(256, X4), "u0p": _sb(256, U8),
     "vb": _sb(512, B), "vq": _sb(128, X4), "vp": _sb(128, U8),
     "wq": _sb(512, X4), "wp": _sb(512, U8),
-    "ones": _sb(128, B), "ident": _sb(128, B), "eb": _sb(520, B), "eq": _sb(512, X4), "ep": _sb(512, U8),
+    "ones": _sb(256, B), "ident": _sb(128, B), "eb": _sb(520, B), "eq": _sb(512, X4), "ep": _sb(512, U8),
     "gb": _sb(224, F), "gc": _sb(224, F), "pc": _sb(16, F), "i16": _sb(32, F), "ibc": _sb(16, F), "i01": _sb(16, F),
     "ist": _sb(16, F), "jj": _sb(256, B), "ft": _sb(136, F), "lo": _sb(136, U),
-    "kmax": _sb(256, B), "kz": _sb(512, B), "ka": _sb(32, F), "kb": _sb(32, F),
+    "kmax": _sb(256, B), "kq": _sb(256, B), "k4": _sb(64, B), "cm": _sb(256, B), "ka": _sb(32, F), "kb": _sb(32, F),
     "o1": _sb(288, F), "s0": _sb(384, F), "s1": _sb(512, F),
     "tt": _sb(1024, B), "win": _sb(4 * 384, B), "tw": _sb(1024, B),
-    "sm": _sb(384, F), "pm": _sb(640, F), "bc": _sb(256, F), "bst": _sb(32, F),
-    "ee": _sb(512, B), "es": _sb(512, B), "q1": _sb(32, F), "ac": _sb(128, F), "pw": _sb(256, F), "pr": _sb(256, F),
+    "sm": _sb(384, F), "pm": _sb(640, F), "bc": _sb(256, F), "bst": _sb(16, F),
+    "ee": _sb(256, B), "es": _sb(512, B), "q1": _sb(32, F), "ac": _sb(128, F), "pw": _sb(256, F), "pr": _sb(256, F),
     "cb": _sb(NV * 256, B), "so": _sb(16 * 128, B), "sg": _sb(NS * 256, B), "jk": _sb(NS * 256, B),
     "l_s": _sb(16, U), "sw": _sb(272, I if INT else F), "tb": _sb(256, I if INT else F), "i2": _sb(64, F),
     "o2": _sb(64, F), "vi": _sb(16, I), "li": _sb(32, I), "l_k": _sb(32, U), "l_a": _sb(16, U),
     "xa": _sb(32, F), "xb": _sb(32, F), "xo": _sb(32, F), "l_x": _sb(16, U),
     "ag": _sb(512, F), "te": _sb(512, F), "zt": _sb(512, B), "zq": _sb(128, X4), "zp": _sb(128, U8),
-    "yb": _sb(256, F),
+    "yb": _sb(256, F), "rq": _sb(128, X4), "rp": _sb(128, U8), "rt": _sb(512, B),
 }
 for _r in range(3):
     SCRATCH["ss%d" % _r] = _sb(64, F)
@@ -50,7 +55,7 @@ for _k in range(8):
 
 NC, ND = 110, 16
 SEMAPHORES = (["c%d" % k for k in range(NC)] + ["d%d" % k for k in range(ND)]
-              + ["%s%d" % (n, r) for n in ("as", "aq", "gs", "gq", "gp") for r in range(3)])
+              + ["%s%d" % (n, r) for n in ("as", "aq", "gs", "gq", "gp") for r in range(3)] + ["ar", "gr", "gx"])
 
 
 def _bits(engs):
@@ -185,17 +190,23 @@ def rank_program(g, core, T, topo):
     def flt(name, a=0, b=None):
         return lst(name, a, b, "ft")
 
-    dma("Y", w("x0"), T.x[:])
-    dma("S", w("ub"), T.u[:])
+    if XL:
+        dma("Y", part("x0", 0, 512), T.x[:, 0:512])
+        dma("S", w("ub"), T.u[:])
+        dma("Y", part("x0", 1, 512), T.x[:, 512:1024])
+    else:
+        dma("Y", w("x0"), T.x[:])
+        dma("S", w("ub"), T.u[:])
     memset(w("ones"), 1.0)
+    iota(flt("o_u"), [[16, 2], [32, 4], [0, 2]], 0)
     BASES = [("d", -1, (1, 0, 1)), ("y", 15, (0, 16, 0)), ("q", 0, (0, 2, 1)), ("hf", 0, (16, 0, 0)),
-             ("rf", 0, (16, 2, 1)), ("u", 128, (16, 16, 0))]
+             ("rf", 15, (16, -2, -1)), ("u", 128, (16, 16, 0))]
     base = {}
     for k, (name, b0, (sh, sb, st)) in enumerate(BASES):
         iota(part("gb", k, 32), [[sh, 2], [sb, 8], [st, 2]], b0)
         base[name] = 32 * k
         if k == 0:
-            op("G", "c", lambda e: e.affine_select(T.ident[:], T.ones[:], [[-1, 128]], ALU.is_equal, 0.0, 0, 1),
+            op("G", "c", lambda e: e.affine_select(T.ident[:], T.ones[:, 0:128], [[-1, 128]], ALU.is_equal, 0.0, 0, 1),
                [w("ones")], [w("ident")])
     base["oe"] = 192
     for h in range(2):
@@ -204,55 +215,62 @@ def rank_program(g, core, T, topo):
     def bs(name, n=1):
         return w("gc", base[name], base[name] + n)
 
-    iota(flt("o_u"), [[16, 2], [32, 4], [0, 2]], 0)
     iota(w("ibc"), [[1, 8], [0, 2]], 0)
     iota(w("i16"), [[16, 32]], 0)
     iota(w("ist"), [[32, 8], [256, 2]], 0)
     iota(w("i01"), [[0, 8], [32, 2]], 0)
-    iota(flt("o_i"), [[16, 16]], 15)
-    iota(flt("o_c"), [[1, 32]], 0)
-    iota(flt("o_4"), [[4, 16]], 0)
     memset(w("eb"), 0.0)
     memset(w("o1", 256, 288), 0.0)
+    copy(lst("o_u"), flt("o_u"))
     copy(w("eb", 3, 515, 4), w("ident"))
     for b in range(4):
         quant(part("eq", b), part("ep", b), w("eb", 3 - b, 515 - b))
+    quant(w("uq"), w("up"), w("ub"))
+    for h in range(2):
+        act(part("u0p", h), ind(w("up"), lst("o_u", 8 * h, 8 * h + 8)), ACT.Copy)
     trans(w("gc"), w("gb"))
     same, q_, hf, rf = col("pc", 0), bs("q"), bs("hf"), bs("rf")
     act(same, bs("d"), ACT.Abs)
     lin(col("pc", 1), bs("y"), 2.0, -285.0)
-    lin(col("pc", 3), hf, 15.0, q_)
+    lin(col("pc", 3), hf, 14.0, rf)
+    lin(col("pc", 8), q_, -1.0, 15.0)
     lin(col("pc", 2), col("pc", 1), same, 256.0)
     lin(flt("o_d"), w("ibc", 0, 4), 16.0, col("pc", 2))
     lin(flt("o_s", 0, 8), w("i16", 1, 16, 2), None, col("pc", 3))
     lin(flt("o_s", 8, 24), w("ist"), None, rf)
-    quant(w("uq"), w("up"), w("ub"))
     lin(flt("o_m", 0, 8), bs("hf", 8), None, rf)
-    lin(flt("o_m", 8, 24), w("i01"), None, q_)
+    lin(flt("o_m", 8, 24), w("i01"), None, col("pc", 8))
     lin(flt("o_t"), bs("u", 2), same, bs("y"))
     lin(flt("o_e"), bs("oe", 2))
 
+    def early_counts():
+        iota(flt("o_i"), [[16, 16]], 15)
+        iota(flt("o_c"), [[1, 16]], 0)
+        iota(flt("o_4"), [[4, 16]], 0)
+
     def late_counts():
         iota(w("jj"), [[0, 16], [1, 16]], 0)
-        iota(w("ka"), [[WM - 2, 2], [0, 16]], -WM)
+        iota(w("ka", 0, 16), [[0, 16]], WM)
+        iota(w("ka", 16, 31), [[0, 15]], -2)
+        iota(col("ka", 31), [[0, 1]], -1)
         iota(w("ac"), [[0, 128]], 0)
         iota(w("xa", 0, 32, 2), [[0, 16]], 1000)
         iota(w("sw", 0, 16), [[0, 16]], 0, small=not INT)
 
     def late_constants():
-        copy(w("lo", 44, 136), w("ft", 44, 136))
+        copy(w("lo", 44, 120), w("ft", 44, 120))
         ts(w("kmax"), w("jj"), 0.0, ALU.is_equal, -BIG, ALU.mult)
-        ts(w("kz", 0, 256), w("jj", 0, 256), 0.0, ALU.not_equal)
-        ts(w("kz", 256, 512), w("jj", 0, 256), q_, ALU.not_equal)
+        ts(w("k4"), w("jj", 0, 256, 4), 0.0, ALU.not_equal)
+        ts(w("kq"), w("jj"), q_, ALU.not_equal)
 
     def later_constants():
-        lin(col("pc", 4), q_, 16.0, 16.0 * WM)
+        lin(col("pc", 4), q_, 16.0, -float(WM))
         lin(w("kb", 16, 16 + NV), bs("hf", NV), 2.0, -256.0)
         lin(col("pc", 5), hf, 8208.0, col("pc", 4))
-        lin(w("kb", 16 + NV, 32), bs("hf", NS), 2.0)
-        lin(col("pc", 6), hf, -1.0, 128.0)
+        lin(w("kb", 16 + NV, 31), bs("hf", NS - 1), 2.0)
+        lin(col("kb", 31), hf, 1.0, 128.0)
         lin(w("kb", 0, 16), w("ibc"), 262656.0, col("pc", 5))
-        lin(col("pc", 7), hf, -1000.0, 500.0)
+        lin(col("pc", 7), hf, 1.0, 127.5)
         lin(w("xb", 1, 32, 2), w("i16", 8, 24), None, q_)
 
     def tw_(b):
@@ -264,6 +282,11 @@ def rank_program(g, core, T, topo):
     def bank(b, n=256):
         return w("ps%d" % b, 0, n)
 
+    def pick_u(h):
+        o, off = part("u0q", h), lst("o_u", 8 * h, 8 * h + 8)
+        op("V", "c", lambda e: e.tensor_copy(o[0].bitcast(dt.uint32), T.uq[:].bitcast(dt.uint32).indirect(off[0])),
+           [w("uq"), off], [o])
+
     def own_scores():
         for h in range(2):
             mm(5 + h, 256, part("u0q", h), part("u0p", h), w("xq"), w("xp"))
@@ -272,71 +295,81 @@ def rank_program(g, core, T, topo):
     for R, mask in enumerate(MASKS):
         peer = T.cores[rank ^ mask]
         en = topo.engines(core, peer)
-        if R == 0:
+        if R == 0 and not E0:
             e_s, e_q = en[:len(en) // 2], en[len(en) // 2:]
         else:
             e_s, e_q = en, en
-        quant_x(X)
+        raw = 128 if R == 0 and RAW else 0
+        if R == 0:
+            quant(part("xq", 0), part("xp", 0), part("x0", 0, 512))
+            if raw:
+                send(peer, T.rp[:], w("xp", 0, raw), "ar", "gr", en)
+            pick_u(0)
+            quant(part("xq", 1), part("xp", 1), part("x0", 1, 512))
+            early_counts()
         for h in range(2):
             mm(4 + 3 * h, 128, w("uq"), w("up"), part("xq", h), part("xp", h))
         if R == 0:
-            dma("Y", u8(w("wq")), (T.wc[:], w("x0")[1]))
-            dma("Y", w("wp"), T.ws[:])
-            dma("Y", w("vb"), T.v[:])
-        if R > 0:
-            own_scores()
+            pick_u(1)
+        own_scores()
         unpack("xq", "xp")
         for h in range(2):
             trans(part("o1", h), bank(4 + 3 * h, 128))
             if R == 0 and h == 0:
-                copy(w("lo", 0, 44), w("ft", 0, 44))
-                act(w("u0p"), ind(w("up"), lst("o_u")), ACT.Copy)
+                copy(w("lo", 16, 44), w("ft", 16, 44))
         copy(w("i2"), ind(w("o1"), lst("o_d")))
         trans(w("ss%d" % R), w("i2"))
         fold(peer, T["sl%d" % R][:], w("ss%d" % R, 0, 48), w("ss%d" % R, 16, 64), "as%d" % R, "gs%d" % R, e_s)
+        if raw:
+            send(peer, T.rq[:].bitcast(dt.uint8), u8(w("xq", 0, raw)), "ar", "gx", en)
         if R == 0:
             late_counts()
-            op("V", "c", lambda e: e.tensor_copy(T.u0q[:].bitcast(dt.uint32),
-                                                 T.uq[:].bitcast(dt.uint32).indirect(lst("o_u")[0])),
-               [w("uq"), lst("o_u")], [w("u0q")])
-            own_scores()
-            act(w("tt", 3, 1024, 4), bank(3), ACT.Copy)
         for h in range(2):
             act(part("s1", h, 256), bank(5 + h), ACT.Copy)
         act(w("s0"), ind(w("s1"), lst("o_s")), ACT.Copy)
-        if R > 0:
-            act(w("tt", 3, 1024, 4), bank(3), ACT.Copy)
+        act(w("tt", 4 * raw + 3, 1024, 4), w("ps3", raw, 256), ACT.Copy)
         for b in range(3):
-            copy(w("tt", b, 1024, 4), bank(b))
-        quant(w("tq%d" % R), w("tp%d" % R), w("tt"))
-        send(peer, T["lq%d" % R][:].bitcast(dt.uint8), u8(w("tq%d" % R)), "aq%d" % R, "gq%d" % R, e_q)
-        send(peer, T["lp%d" % R][:], w("tp%d" % R), "aq%d" % R, "gp%d" % R, e_q)
+            copy(w("tt", 4 * raw + b, 1024, 4), w("ps%d" % b, raw, 256))
+        quant(w("tq%d" % R, raw), w("tp%d" % R, raw), w("tt", 4 * raw))
+        send(peer, T["lq%d" % R][:, raw:256].bitcast(dt.uint8), u8(w("tq%d" % R, raw)), "aq%d" % R, "gq%d" % R, e_q)
+        send(peer, T["lp%d" % R][:, raw:256], w("tp%d" % R, raw), "aq%d" % R, "gp%d" % R, e_q)
+        for b in range(4):
+            if raw and b < WV:
+                ts(tw_(b), bank(b), 32.0, ALU.mult)
+            else:
+                act(tw_(b), bank(b), ACT.Copy, scale=32.0)
         if R == 0:
             late_constants()
             later_constants()
-        for b in range(4):
-            if b < WV:
-                ts(tw_(b), w("tt", b, 1024, 4), 32.0, ALU.mult)
-            else:
-                act(tw_(b), bank(b), ACT.Copy, scale=32.0)
         arrive([w("sl%d" % R)], "as%d" % R, len(e_s))
-        arrive([w("lq%d" % R), w("lp%d" % R)], "aq%d" % R, 2 * len(e_q))
+        arrive([w("lq%d" % R, raw), w("lp%d" % R, raw)], "aq%d" % R, 2 * len(e_q))
+        if R == 0:
+            dma("Y", u8(w("wq")), (T.wc[:], w("sl0")[1]))
+            dma("Y", w("wp"), T.ws[:])
+            dma("Y", w("vb"), T.v[:])
+        if raw:
+            arrive([w("rq"), w("rp")], "ar", 2 * len(en))
+            for b in range(4):
+                mm(4 + b, raw, part("eq", b), part("ep", b), w("rq"), w("rp"))
         row0 = 384
         tt(w("sm", 128, 384), ind(w("sl%d" % R), lst("o_m", 8, 24)), w("s0", 128, 384), ALU.add)
         tt(w("sm", 0, 128), ind(w("sl%d" % R), lst("o_m", 0, 8)), w("s0", 0, 128), ALU.add)
         scan(w("pm", 128, 384), w("kmax"), w("sm", 128, 384), 0.0, ALU.add, ALU.max)
         scan(w("pm", 0, 128), w("kmax", 0, 128), w("sm", 0, 128), 0.0, ALU.add, ALU.max)
-        act(w("bc"), ind(w("pm", 128, 384), lst("o_i")), ACT.Copy)
-        copy(w("bst", 0, 16), w("pm", 143, 384, 16))
-        act(w("bst", 16, 32), ind(w("pm", 0, 384), lst("o_t", 0, 1)), ACT.Copy)
-        for h in range(2):
-            tt(part("ee", h), ind(w("bst", 0, 16), lst("o_c", 8 * h, 8 * h + 8)), part("pm", 1 + h), ALU.is_equal)
-            if h == 0:
-                trans(w("pm", row0, row0 + 256), w("bc"))
-        tt(w("ee", 256, 512), ind(w("bst", 16, 32), lst("o_c", 0, 16)), w("pm", 384, 640), ALU.is_equal)
+        n = 256 // BH
+        for h in range(BH):
+            act(part("bc", h, n), ind(w("pm", 128, 384), lst("o_i", h * n // 16, (h + 1) * n // 16)), ACT.Copy)
+        act(w("bst"), ind(w("pm", 0, 384), lst("o_t", 0, 1)), ACT.Copy)
+        for b in range(4 if raw else 0):
+            act(w("rt", b, 4 * raw, 4), bank(4 + b, raw), ACT.Copy)
+        tt(w("cm"), ind(w("pm", 128, 384), lst("o_i")), w("sm", 128, 384), ALU.not_equal)
+        for h in range(BH):
+            trans(w("pm", row0 + h * n, row0 + h * n + n), part("bc", h, n))
+        scan(w("es", 0, 256), w("cm"), w("ones"), 0.0, ALU.mult, ALU.add)
+        tt(w("ee"), ind(w("bst"), lst("o_c")), w("pm", 384, 640), ALU.is_equal)
 
         def own(k):
-            return col("bst", 16 + k)
+            return col("bst", k)
 
         def row(a=0, b=256):
             return w("pm", row0 + a, row0 + b)
@@ -362,48 +395,52 @@ def rank_program(g, core, T, topo):
             act(w("jk", o, o + a), w("sg", o, o + a), ACT.Sign, bias=0.5, scale=-1.0, accum=slot(k, 1))
 
         v_cmp(0)
-        scan(w("es"), w("kz"), w("ee"), 0.0, ALU.mult, ALU.add)
+        scan(w("es", 256, 512), w("kq"), w("ee"), 0.0, ALU.mult, ALU.add)
         v_cmp(1)
         tt(w("q1"), w("es", 15, 512, 16), w("ka"), ALU.mult)
         v_cmp(2)
         tt(w("ac", 0, 128, 4), w("q1"), w("kb"), ALU.add)
+        if raw:
+            quant(w("lq0", 0, raw), w("lp0", 0, raw), w("rt"))
         s_cmp(NV)
         for k in range(NV, 16):
             if k + 1 < 16:
                 s_cmp(k + 1)
             s_sum(k)
-            if k == NV + 2:
+            if k == NV + 3:
                 act(w("pw"), ind(w("ac", 0, 64), lst("o_4")), ACT.Copy)
         for k in range(NV):
             if k + 3 < NV:
                 v_cmp(k + 3)
             v_sum(k)
         trans(part("pr", 0), part("pw", 0))
-        scan(w("so", 128 * NV + 31, 2048, 32), w("kz", 0, 16 * NS, 4), w("ac", 64 + 4 * NV, 128), 0.0, ALU.mult, ALU.add)
-        twice = w("so", 127, 2048, 128)
+        scan(w("so", 128 * NV + 31, 1920, 32), w("k4", 0, 4 * NS - 4), w("ac", 64 + 4 * NV, 124), 0.0,
+             ALU.mult, ALU.add)
         trans(part("pr", 1), part("pw", 1))
-        ts(w("l_s"), twice, 0.5, ALU.mult, 128.0, ALU.add)
-        ts(w("xb", 0, 32, 2), twice, 0.5, ALU.mult, col("pc", 6), ALU.add)
-        ts(w("xa", 1, 32, 2), twice, 500.0, ALU.mult, col("pc", 7), ALU.add)
+        ts(col("l_s", 15), slot(15, 1), 0.5, ALU.mult, slot(15, 0), ALU.add)
+        ts(w("l_s", 0, 15), w("so", 127, 1920, 128), 0.5, ALU.mult, 128.0, ALU.add)
         scatter(w("sw"), w("l_s"), w("pr"))
         unpack("lq%d" % R, "lp%d" % R)
         for b in range(4):
             act(part("tw", b, 256), bank(b), ACT.Copy, scale=0.5)
-        scan(w("xo"), w("xa"), w("xb"), 0.0, ALU.max, ALU.min)
+        ts(w("xb", 0, 32, 2), w("l_s"), hf, ALU.subtract)
+        ts(w("xa", 1, 32, 2), w("l_s"), col("pc", 7), ALU.subtract, 1000.0, ALU.mult)
         trans(part("tb", 0), w("sw", 0, 128))
         trans(part("tb", 1), w("sw", 16, 144))
-        copy(w("l_x"), w("xo", 1, 32, 2))
+        scan(w("xo"), w("xa"), w("xb"), 0.0, ALU.max, ALU.min)
         picked = ind(w("tb"), lst("o_e", 0, 1))
         ts(w("l_a"), picked, 2.0 ** -13, ALU.mult)
         ts(w("li", 0, 16), picked, 255, ALU.bitwise_and)
         ts(w("li", 16, 32), picked, 4, ALU.logical_shift_right, 255, ALU.bitwise_and)
+        copy(w("l_x"), w("xo", 1, 32, 2))
         la, lb, le = w("l_a", 0, 8), w("l_k", 0, 8), w("l_k", 16, 24)
         copy(lb, w("li", 0, 8))
         copy(le, w("li", 16, 24))
 
-        for b in range(4):
+        for b in range(3):
             act(part("ag", b), ind(tw_(b), la), ACT.Copy, scale=2.0 ** -6)
-        for b in range(4):
+        ts(part("ag", 3), ind(tw_(3), la), 2.0 ** -6, ALU.mult)
+        for b in (0, 3, 1, 2):
             tt(w("zt", b, 512, 4), ind(part("tw", b, 256), lb), part("ag", b), ALU.add)
         quant(w("zq"), w("zp"), w("zt"))
         if R == 1:
@@ -412,21 +449,24 @@ def rank_program(g, core, T, topo):
             act(part("te", b), ind(tw_(b), le), ACT.Copy)
         for b in range(4):
             mm(4 + b, 128, part("wq", b), part("wp", b), w("zq"), w("zp"))
-        for b in range(4):
-            tt(w("win", 384 * b, 384 * b + 128), bank(4 + b, 128), part("te", b), ALU.add)
-        for b in range(2):
-            act(w("xs", b, 1024, 4), ind(fw(b), w("l_x")), ACT.Copy, scale=2.0 ** -5)
-        ts(w("xs", 512 + 2, 1024, 4), ind(fw(2), w("l_x", 8, 16)), 2.0 ** -5, ALU.mult)
-        act(w("xs", 2, 512, 4), ind(fw(2), w("l_x", 0, 8)), ACT.Copy, scale=2.0 ** -5)
-        ts(w("xs", 3, 1024, 4), ind(fw(3), w("l_x")), 2.0 ** -5, ALU.mult)
-        X = "xs"
+        for q, b, c0, c1 in PICKS:
+            if q == "A":
+                tt(w("win", 384 * b, 384 * b + 128), bank(4 + b, 128), part("te", b), ALU.add)
+                continue
+            if q == "Q":
+                quant(part("xq", b), part("xp", b), part("xs", b, 512))
+                continue
+            o, i = w("xs", 64 * c0 + b, 64 * c1, 4), ind(fw(b), w("l_x", c0, c1))
+            if q == "S":
+                act(o, i, ACT.Copy, scale=2.0 ** -5)
+            else:
+                ts(o, i, 2.0 ** -5, ALU.mult)
 
-    quant_x(X)
     for h in range(2):
         mm(h, 128, w("vq"), w("vp"), part("xq", h), part("xp", h))
     dma("Y", T.oc[:], u8(w("xq")))
     for k in range(4):
-        dma("Y" if k < 2 else "S", T.osc[4 * k:4 * k + 4, :], (T.xp[32 * k:32 * k + 4, :], w("xp")[1]))
+        dma("Y", T.osc[4 * k:4 * k + 4, :], (T.xp[32 * k:32 * k + 4, :], w("xp")[1]))
     copy(part("yb", 0), w("ps0", 0, 128))
     act(part("yb", 1), w("ps1", 0, 128), ACT.Copy)
     dma("Y", T.y[:, 0:128], part("yb", 0))

@@ -1,20 +1,26 @@
 from concourse.bass import DstId, RemoteDMATransfer
-from concourse.mybir import dt, AluOpType, ActivationFunctionType
+from concourse.mybir import dt, AluOpType, AxisListType, ActivationFunctionType
 
 ALU, ACT = AluOpType, ActivationFunctionType
 F, B, I, U, X4, U8 = "float32", "bfloat16", "int32", "uint16", "float8_e4m3fn_x4", "uint8"
 MASKS = [1, 2, 4]
-NV = 9
-NS = 16 - NV
+VROWS = [6, 7, 8, 15]
+PW = 8
+SROWS = [k for k in range(16) if k not in VROWS]
+LEND = 16 * 127
+STEP = 2.0 ** -24 * (1 + 2.0 ** -23)
+TINY = 2.0 ** -120
 INT = True
-PICKS = [("A", 0, 0, 0), ("A", 1, 0, 0), ("A", 2, 0, 0), ("A", 3, 0, 0), ("S", 0, 0, 16), ("S", 1, 0, 16), ("V", 2, 0, 8), ("V", 3, 0, 8), ("V", 2, 8, 16), ("S", 3, 8, 16), ("Q", 0, 0, 0), ("Q", 1, 0, 0)]
+PICKS = [("A", 0, 0, 0), ("A", 1, 0, 0), ("A", 2, 0, 0), ("A", 3, 0, 0), ("S", 0, 0, 16), ("S", 1, 0, 16), ("V", 2, 0, 8), ("V", 3, 0, 10), ("V", 2, 8, 16), ("S", 3, 10, 16), ("Q", 0, 0, 0), ("Q", 1, 0, 0)]
 BH = 2
 E0 = True
 XL = True
 RAW = True
-WV = 2
+QL = ()
+HELP = 0
+WV = 1
 BIG = 1.0e29
-WM = 8193
+WM = 257
 LISTS = {"o_u": (0, 16), "o_d": (16, 4), "o_s": (20, 24), "o_m": (44, 24), "o_i": (68, 16), "o_t": (84, 2),
          "o_c": (86, 16), "o_4": (102, 16), "o_e": (118, 2)}
 
@@ -29,19 +35,19 @@ SCRATCH = {
     "vb": _sb(512, B), "vq": _sb(128, X4), "vp": _sb(128, U8),
     "wq": _sb(512, X4), "wp": _sb(512, U8),
     "ones": _sb(256, B), "ident": _sb(128, B), "eb": _sb(520, B), "eq": _sb(512, X4), "ep": _sb(512, U8),
-    "gb": _sb(224, F), "gc": _sb(224, F), "pc": _sb(16, F), "i16": _sb(32, F), "ibc": _sb(16, F), "i01": _sb(16, F),
+    "gb": _sb(256, F), "gc": _sb(256, F), "pc": _sb(16, F), "i16": _sb(32, F), "ibc": _sb(16, F), "i01": _sb(16, F),
     "ist": _sb(16, F), "jj": _sb(256, B), "ft": _sb(136, F), "lo": _sb(136, U),
-    "kmax": _sb(256, B), "kq": _sb(256, B), "k4": _sb(64, B), "cm": _sb(256, B), "ka": _sb(32, F), "kb": _sb(32, F),
+    "kmax": _sb(256, B), "k4": _sb(64, B), "cm": _sb(512, B), "sr": _sb(32, F), "ch": _sb(256, B), "ka": _sb(32, F), "kb": _sb(32, F),
     "o1": _sb(288, F), "s0": _sb(384, F), "s1": _sb(512, F),
     "tt": _sb(1024, B), "win": _sb(4 * 384, B), "tw": _sb(1024, B),
-    "sm": _sb(384, F), "pm": _sb(640, F), "bc": _sb(256, F), "bst": _sb(16, F),
-    "ee": _sb(256, B), "es": _sb(512, B), "q1": _sb(32, F), "ac": _sb(128, F), "pw": _sb(256, F), "pr": _sb(256, F),
-    "cb": _sb(NV * 256, B), "so": _sb(16 * 128, B), "sg": _sb(NS * 256, B), "jk": _sb(NS * 256, B),
+    "sm": _sb(384, F), "pm": _sb(640, F), "bc": _sb(256, F), "bst": _sb(80, F),
+    "ee": _sb(512, B), "es": _sb(512, B), "q1": _sb(80, F), "ac": _sb(32, F), "pw": _sb(256, U), "pr": _sb(256, U),
+    "cb": _sb(len(VROWS) * 256, B), "so": _sb(LEND + 16, U), "fl": _sb(len(SROWS) * 256, U),
     "l_s": _sb(16, U), "sw": _sb(272, I if INT else F), "tb": _sb(256, I if INT else F), "i2": _sb(64, F),
-    "o2": _sb(64, F), "vi": _sb(16, I), "li": _sb(32, I), "l_k": _sb(32, U), "l_a": _sb(16, U),
+    "o2": _sb(64, F), "vi": _sb(16, I), "li": _sb(48, I), "l_k": _sb(32, U), "l_a": _sb(16, U),
     "xa": _sb(32, F), "xb": _sb(32, F), "xo": _sb(32, F), "l_x": _sb(16, U),
     "ag": _sb(512, F), "te": _sb(512, F), "zt": _sb(512, B), "zq": _sb(128, X4), "zp": _sb(128, U8),
-    "yb": _sb(256, F), "rq": _sb(128, X4), "rp": _sb(128, U8), "rt": _sb(512, B),
+    "yb": _sb(256, F), "rq": _sb(128, X4), "rp": _sb(128, U8), "rt": _sb(512, B), "hq": _sb(128, X4),
 }
 for _r in range(3):
     SCRATCH["ss%d" % _r] = _sb(64, F)
@@ -55,7 +61,7 @@ for _k in range(8):
 
 NC, ND = 110, 16
 SEMAPHORES = (["c%d" % k for k in range(NC)] + ["d%d" % k for k in range(ND)]
-              + ["%s%d" % (n, r) for n in ("as", "aq", "gs", "gq", "gp") for r in range(3)] + ["ar", "gr", "gx"])
+              + ["%s%d" % (n, r) for n in ("as", "aq", "gs", "gq", "gp") for r in range(3)] + ["ar", "gr", "gx", "ah"])
 
 
 def _bits(engs):
@@ -65,10 +71,32 @@ def _bits(engs):
     return m
 
 
+def _helpers(T, topo):
+    out = {}
+    for c in T.cores:
+        free = [x for x in topo.cores_of(c) if topo.die(x) != topo.die(c) and x not in T.cores and x not in out.values()]
+        out[c] = free[0]
+    return out
+
+
+def _hand_on(g, core, T, topo):
+    for c, mate in _helpers(T, topo).items():
+        if mate == core:
+            for R, mask in enumerate(MASKS):
+                peer = T.cores[T.rank_of(c) ^ mask]
+                if topo.chip(peer) != topo.chip(c):
+                    en = topo.engines(core, peer)
+                    rid, pid, _ = topo.addr(peer)
+                    g.wait_ge(T.sem.ah, len(topo.engines(c, core)) - len(topo.engines(c, peer)))
+                    g.remote_dma(T["lq%d" % R][:, 128:256].bitcast(dt.uint8), T.hq[:].bitcast(dt.uint8),
+                                 T.sem["aq%d" % R], T.sem.gx, pid, rid, _bits(en))
+                    g.wait_ge(T.sem.gx, len(en))
+
+
 def rank_program(g, core, T, topo):
     rank = T.rank_of(core)
     if rank is None:
-        return
+        return _hand_on(g, core, T, topo)
     eng = {"G": g, "V": g.vector, "S": g.scalar, "P": g.tensor, "Y": g.sync}
     ops = []
 
@@ -198,78 +226,82 @@ def rank_program(g, core, T, topo):
         dma("Y", w("x0"), T.x[:])
         dma("S", w("ub"), T.u[:])
     memset(w("ones"), 1.0)
-    iota(flt("o_u"), [[16, 2], [32, 4], [0, 2]], 0)
-    BASES = [("d", -1, (1, 0, 1)), ("y", 15, (0, 16, 0)), ("q", 0, (0, 2, 1)), ("hf", 0, (16, 0, 0)),
-             ("rf", 15, (16, -2, -1)), ("u", 128, (16, 16, 0))]
+    BASES = [("od", 1, (0, 32, 0)), ("hf", 0, (16, 0, 0)), ("rf", 15, (16, -2, -1)), ("d", -1, (1, 0, 1))]
     base = {}
     for k, (name, b0, (sh, sb, st)) in enumerate(BASES):
-        iota(part("gb", k, 32), [[sh, 2], [sb, 8], [st, 2]], b0)
         base[name] = 32 * k
+        iota(part("gb", k, 32), [[sh, 2], [sb, 8], [st, 2]], b0)
         if k == 0:
+            op("G", "c", lambda e: e.affine_select(T.gb[:, 0:32], T.gb[:, 0:32], [[1, 2], [0, 8], [-1, 2]], ALU.is_equal,
+                                                   256.0, 0, 0), [part("gb", 0, 32)], [part("gb", 0, 32)])
+            iota(w("ibc"), [[1, 8], [0, 2]], 0)
             op("G", "c", lambda e: e.affine_select(T.ident[:], T.ones[:, 0:128], [[-1, 128]], ALU.is_equal, 0.0, 0, 1),
                [w("ones")], [w("ident")])
-    base["oe"] = 192
-    for h in range(2):
-        iota(part("gb", 12 + h, 16), [[0, 2], [32, 4], [128, 2]], 16 * h)
+            iota(flt("o_u"), [[16, 2], [32, 4], [0, 2]], 0)
+    iota(w("i16"), [[16, 32]], 0)
+    iota(w("ist"), [[32, 8], [256, 2]], 0)
 
     def bs(name, n=1):
         return w("gc", base[name], base[name] + n)
 
-    iota(w("ibc"), [[1, 8], [0, 2]], 0)
-    iota(w("i16"), [[16, 32]], 0)
-    iota(w("ist"), [[32, 8], [256, 2]], 0)
-    iota(w("i01"), [[0, 8], [32, 2]], 0)
+    def fill(o, n, c):
+        act(o, w("ones", 0, n), ACT.Copy, scale=float(c))
+
     memset(w("eb"), 0.0)
     memset(w("o1", 256, 288), 0.0)
-    copy(lst("o_u"), flt("o_u"))
+    trans(part("gc", 0, 32), part("gb", 0, 32))
+    fill(w("kmax"), 256, 0)
+    lin(flt("o_d"), w("ibc", 0, 4), 16.0, bs("od"))
+    fill(w("kmax", 0, 256, 16), 16, -BIG)
+    fill(w("ee", 0, 256), 256, 1)
+    fill(w("ka", 0, 16), 16, WM)
+    fill(w("ka", 16, 32), 16, -1)
+    fill(w("xa", 0, 32, 2), 16, 1000)
+    fill(w("i01", 0, 16, 2), 8, 0)
+    fill(w("i01", 1, 16, 2), 8, 32)
+    fill(flt("o_t", 1, 2), 1, 0)
     copy(w("eb", 3, 515, 4), w("ident"))
+    copy(w("lo", 0, 20), w("ft", 0, 20))
     for b in range(4):
         quant(part("eq", b), part("ep", b), w("eb", 3 - b, 515 - b))
-    quant(w("uq"), w("up"), w("ub"))
-    for h in range(2):
-        act(part("u0p", h), ind(w("up"), lst("o_u", 8 * h, 8 * h + 8)), ACT.Copy)
-    trans(w("gc"), w("gb"))
-    same, q_, hf, rf = col("pc", 0), bs("q"), bs("hf"), bs("rf")
-    act(same, bs("d"), ACT.Abs)
-    lin(col("pc", 1), bs("y"), 2.0, -285.0)
+    hf, rf, d_ = bs("hf"), bs("rf"), bs("d")
+    same, q_, qr, t_, b16, u_, y_, oe = [col("pc", k) for k in (0, 1, 8, 2, 9, 10, 11, 12)]
+    trans(w("gc", 32, 128), w("gb", 32, 128))
+    memset(w("sw", 0, 16), 0)
     lin(col("pc", 3), hf, 14.0, rf)
-    lin(col("pc", 8), q_, -1.0, 15.0)
-    lin(col("pc", 2), col("pc", 1), same, 256.0)
-    lin(flt("o_d"), w("ibc", 0, 4), 16.0, col("pc", 2))
-    lin(flt("o_s", 0, 8), w("i16", 1, 16, 2), None, col("pc", 3))
+    lin(qr, hf, -1.0, rf)
+    lin(t_, hf, -0.0625, d_)
     lin(flt("o_s", 8, 24), w("ist"), None, rf)
-    lin(flt("o_m", 0, 8), bs("hf", 8), None, rf)
-    lin(flt("o_m", 8, 24), w("i01"), None, col("pc", 8))
-    lin(flt("o_t"), bs("u", 2), same, bs("y"))
-    lin(flt("o_e"), bs("oe", 2))
+    lin(flt("o_s", 0, 8), w("i16", 1, 16, 2), None, col("pc", 3))
 
-    def early_counts():
-        iota(flt("o_i"), [[16, 16]], 15)
-        iota(flt("o_c"), [[1, 16]], 0)
-        iota(flt("o_4"), [[4, 16]], 0)
+    def first_constants():
+        act(same, d_, ACT.Abs)
+        lin(q_, qr, -1.0, 15.0)
+        lin(b16, t_, 1.0, qr)
+        lin(flt("o_m", 0, 8), bs("hf", 8), None, rf)
+        lin(flt("o_m", 8, 24), w("i01"), None, qr)
+        lin(oe, t_, 112.0, hf)
+        lin(y_, b16, -8.0, 127.0)
+        lin(u_, b16, -8.0, hf)
+
+    def early_constants():
+        lin(flt("o_i"), w("i16", 0, 16), 1.0, 15.0)
+        lin(flt("o_c"), w("i16", 0, 16), 0.0625)
+        lin(col("pc", 13), same, 240.0, y_)
+        lin(col("pc", 14), q_, 16.0, oe)
+        lin(flt("o_t", 0, 1), u_, same, col("pc", 13))
 
     def late_counts():
         iota(w("jj"), [[0, 16], [1, 16]], 0)
-        iota(w("ka", 0, 16), [[0, 16]], WM)
-        iota(w("ka", 16, 31), [[0, 15]], -2)
-        iota(col("ka", 31), [[0, 1]], -1)
-        iota(w("ac"), [[0, 128]], 0)
-        iota(w("xa", 0, 32, 2), [[0, 16]], 1000)
-        iota(w("sw", 0, 16), [[0, 16]], 0, small=not INT)
 
     def late_constants():
-        copy(w("lo", 44, 120), w("ft", 44, 120))
-        ts(w("kmax"), w("jj"), 0.0, ALU.is_equal, -BIG, ALU.mult)
-        ts(w("k4"), w("jj", 0, 256, 4), 0.0, ALU.not_equal)
-        ts(w("kq"), w("jj"), q_, ALU.not_equal)
+        ts(lst("o_e", 0, 1), col("pc", 14), 112.0, ALU.add, 255.0, ALU.min)
 
     def later_constants():
         lin(col("pc", 4), q_, 16.0, -float(WM))
-        lin(w("kb", 16, 16 + NV), bs("hf", NV), 2.0, -256.0)
-        lin(col("pc", 5), hf, 8208.0, col("pc", 4))
-        lin(w("kb", 16 + NV, 31), bs("hf", NS - 1), 2.0)
-        lin(col("kb", 31), hf, 1.0, 128.0)
-        lin(w("kb", 0, 16), w("ibc"), 262656.0, col("pc", 5))
+        lin(w("kb", 16, 32), bs("hf", 16))
+        lin(col("pc", 5), hf, 256.0, col("pc", 4))
+        lin(w("kb", 0, 16), w("ibc"), 8192.0, col("pc", 5))
         lin(col("pc", 7), hf, 1.0, 127.5)
         lin(w("xb", 1, 32, 2), w("i16", 8, 24), None, q_)
 
@@ -301,48 +333,82 @@ def rank_program(g, core, T, topo):
             e_s, e_q = en, en
         raw = 128 if R == 0 and RAW else 0
         if R == 0:
+            quant(w("uq"), w("up"), w("ub"))
+            for h in range(2):
+                act(part("u0p", h), ind(w("up"), lst("o_u", 8 * h, 8 * h + 8)), ACT.Copy)
+            first_constants()
             quant(part("xq", 0), part("xp", 0), part("x0", 0, 512))
             if raw:
                 send(peer, T.rp[:], w("xp", 0, raw), "ar", "gr", en)
             pick_u(0)
             quant(part("xq", 1), part("xp", 1), part("x0", 1, 512))
-            early_counts()
         for h in range(2):
             mm(4 + 3 * h, 128, w("uq"), w("up"), part("xq", h), part("xp", h))
         if R == 0:
             pick_u(1)
-        own_scores()
+        far = topo.chip(peer) != topo.chip(core)
+        if not far:
+            own_scores()
         unpack("xq", "xp")
+        if far:
+            own_scores()
+            for b in range(3):
+                act(w("tt", b, 1024, 4), bank(b), ACT.Copy)
         for h in range(2):
             trans(part("o1", h), bank(4 + 3 * h, 128))
-            if R == 0 and h == 0:
-                copy(w("lo", 16, 44), w("ft", 16, 44))
+        if R == 0:
+            copy(lst("o_s"), flt("o_s"))
         copy(w("i2"), ind(w("o1"), lst("o_d")))
         trans(w("ss%d" % R), w("i2"))
         fold(peer, T["sl%d" % R][:], w("ss%d" % R, 0, 48), w("ss%d" % R, 16, 64), "as%d" % R, "gs%d" % R, e_s)
         if raw:
             send(peer, T.rq[:].bitcast(dt.uint8), u8(w("xq", 0, raw)), "ar", "gx", en)
-        if R == 0:
-            late_counts()
         for h in range(2):
             act(part("s1", h, 256), bank(5 + h), ACT.Copy)
-        act(w("s0"), ind(w("s1"), lst("o_s")), ACT.Copy)
-        act(w("tt", 4 * raw + 3, 1024, 4), w("ps3", raw, 256), ACT.Copy)
-        for b in range(3):
+        if R == 0:
+            late_counts()
+        act(w("s0", 128, 384), ind(w("s1"), lst("o_s", 8, 24)), ACT.Copy)
+        if R == 0:
+            early_constants()
+        if not far:
+            act(w("tt", 4 * raw + 3, 1024, 4), w("ps3", raw, 256), ACT.Copy)
+        act(w("s0", 0, 128), ind(w("s1"), lst("o_s", 0, 8)), ACT.Copy)
+        for b in [3] if far else range(3):
             copy(w("tt", 4 * raw + b, 1024, 4), w("ps%d" % b, raw, 256))
-        quant(w("tq%d" % R, raw), w("tp%d" % R, raw), w("tt", 4 * raw))
-        send(peer, T["lq%d" % R][:, raw:256].bitcast(dt.uint8), u8(w("tq%d" % R, raw)), "aq%d" % R, "gq%d" % R, e_q)
-        send(peer, T["lp%d" % R][:, raw:256], w("tp%d" % R, raw), "aq%d" % R, "gp%d" % R, e_q)
+        if R == 0:
+            copy(w("lo", 44, 102), w("ft", 44, 102))
+            late_constants()
+
+        def send_codes():
+            quant(w("tq%d" % R, raw), w("tp%d" % R, raw), w("tt", 4 * raw))
+            if far:
+                mate = _helpers(T, topo)[core]
+                spare = [e for e in topo.engines(core, mate) if e not in en]
+                both = [(peer, T["lq%d" % R][:, 0:128], part("tq%d" % R, 0), "aq%d" % R, en),
+                        (mate, T.hq[:], part("tq%d" % R, 1), "ah", spare)]
+                op("G", "r", lambda e: e.remote_dma_fused(
+                    [RemoteDMATransfer(dst_ids=[DstId(rid=topo.addr(c)[0], pnc=topo.addr(c)[1])],
+                                       dma_engine_mask=_bits(m), remote_sem=T.sem[s], src=u8(i)[0],
+                                       dst=o.bitcast(dt.uint8)) for c, o, i, s, m in both],
+                    local_sem=T.sem["gq%d" % R]), [w("tq%d" % R)], [], ("gq%d" % R, len(en) + len(spare)))
+            else:
+                send(peer, T["lq%d" % R][:, raw:256].bitcast(dt.uint8), u8(w("tq%d" % R, raw)), "aq%d" % R, "gq%d" % R,
+                     e_q)
+            send(peer, T["lp%d" % R][:, raw:256], w("tp%d" % R, raw), "aq%d" % R, "gp%d" % R, e_q)
+
+        if R not in QL:
+            send_codes()
         for b in range(4):
             if raw and b < WV:
                 ts(tw_(b), bank(b), 32.0, ALU.mult)
+            elif far:
+                ts(tw_(b), w("tt", b, 1024, 4), 32.0, ALU.mult)
             else:
                 act(tw_(b), bank(b), ACT.Copy, scale=32.0)
         if R == 0:
-            late_constants()
             later_constants()
         arrive([w("sl%d" % R)], "as%d" % R, len(e_s))
-        arrive([w("lq%d" % R, raw), w("lp%d" % R, raw)], "aq%d" % R, 2 * len(e_q))
+        arrive([w("lq%d" % R, raw), w("lp%d" % R, raw)], "aq%d" % R, (3 if far else 2) * len(e_q))
         if R == 0:
             dma("Y", u8(w("wq")), (T.wc[:], w("sl0")[1]))
             dma("Y", w("wp"), T.ws[:])
@@ -352,21 +418,40 @@ def rank_program(g, core, T, topo):
             for b in range(4):
                 mm(4 + b, raw, part("eq", b), part("ep", b), w("rq"), w("rp"))
         row0 = 384
-        tt(w("sm", 128, 384), ind(w("sl%d" % R), lst("o_m", 8, 24)), w("s0", 128, 384), ALU.add)
-        tt(w("sm", 0, 128), ind(w("sl%d" % R), lst("o_m", 0, 8)), w("s0", 0, 128), ALU.add)
-        scan(w("pm", 128, 384), w("kmax"), w("sm", 128, 384), 0.0, ALU.add, ALU.max)
-        scan(w("pm", 0, 128), w("kmax", 0, 128), w("sm", 0, 128), 0.0, ALU.add, ALU.max)
-        n = 256 // BH
-        for h in range(BH):
-            act(part("bc", h, n), ind(w("pm", 128, 384), lst("o_i", h * n // 16, (h + 1) * n // 16)), ACT.Copy)
-        act(w("bst"), ind(w("pm", 0, 384), lst("o_t", 0, 1)), ACT.Copy)
+        ends = lst("o_i", 0, 8)
+
+        def sums(k):
+            tt(part("sm", k), ind(w("sl%d" % R), lst("o_m", 8 * k, 8 * k + 8)), part("s0", k), ALU.add)
+
+        def maxima(k):
+            scan(part("pm", k), w("kmax", 0, 128), part("sm", k), 0.0, ALU.add, ALU.max)
+            if k:
+                act(part("bc", k - 1), ind(part("pm", k), ends), ACT.Copy)
+
+        def middles(k):
+            tt(part("cm", k - 1), ind(part("pm", k), ends), part("sm", k), ALU.not_equal)
+
+        sums(1)
+        sums(2)
+        maxima(1)
+        maxima(2)
+        sums(0)
+        middles(1)
+        maxima(0)
+        mine = ind(w("pm", 0, 384), lst("o_t", 0, 1))
+        act(w("bst", 0, 16), mine, ACT.Copy)
+        act(w("bst", 16, 32), mine, ACT.Copy, scale=-1.0)
+        act(w("bst", 32, 48), mine, ACT.Abs, scale=STEP)
+        act(w("bst", 48, 64), mine, ACT.Identity, scale=-1.0, bias=TINY)
         for b in range(4 if raw else 0):
             act(w("rt", b, 4 * raw, 4), bank(4 + b, raw), ACT.Copy)
-        tt(w("cm"), ind(w("pm", 128, 384), lst("o_i")), w("sm", 128, 384), ALU.not_equal)
-        for h in range(BH):
-            trans(w("pm", row0 + h * n, row0 + h * n + n), part("bc", h, n))
-        scan(w("es", 0, 256), w("cm"), w("ones"), 0.0, ALU.mult, ALU.add)
-        tt(w("ee"), ind(w("bst"), lst("o_c")), w("pm", 384, 640), ALU.is_equal)
+        for h in range(2):
+            trans(part("pm", 3 + h), part("bc", h))
+        middles(2)
+        if R in QL:
+            send_codes()
+        tt(w("ee", 256, 512), ind(w("bst", 0, 16), lst("o_c")), w("pm", 384, 640), ALU.is_equal)
+        tt(w("bst", 64, 80), w("bst", 32, 48), w("bst", 48, 64), ALU.add)
 
         def own(k):
             return col("bst", k)
@@ -374,75 +459,83 @@ def rank_program(g, core, T, topo):
         def row(a=0, b=256):
             return w("pm", row0 + a, row0 + b)
 
-        def slot(k, n):
-            return col("ac", 64 + 4 * k + n)
+        def counted(k, n):
+            return w("so", LEND + k - 16 * (n - 1), LEND + 16, 16)
 
         def v_cmp(k):
-            a = 16 * (k + 1)
-            ts(w("cb", 256 * k, 256 * k + a), row(0, a), own(k), ALU.is_ge, 2.0, ALU.mult)
-            ts(w("cb", 256 * k + a, 256 * k + 256), row(a, 256), own(k), ALU.is_gt, 2.0, ALU.mult)
+            a, o = 16 * (k + 1), 256 * VROWS.index(k)
+            ts(w("cb", o, o + a), row(0, a), own(k), ALU.is_ge)
+            if a < 256:
+                ts(w("cb", o + a, o + 256), row(a, 256), own(k), ALU.is_gt)
 
         def v_sum(k):
-            scan(part("so", k), part("cb", 2 * k), part("cb", 2 * k + 1), slot(k, 0), ALU.add, ALU.add)
+            o = 2 * VROWS.index(k)
+            scan(counted(k, 128), part("cb", o), part("cb", o + 1), col("ac", 16 + k), ALU.add, ALU.add)
 
-        def s_cmp(k):
-            act(part("sg", k - NV, 256), row(), ACT.Sign, bias=own(k), scale=-1.0)
+        def s_cmp(k, later):
+            a, o = 16 * (k + 1), 256 * SROWS.index(k)
+            if later:
+                act(w("fl", o + a, o + 256), row(a, 256), ACT.Sign, bias=col("bst", 16 + k))
+            else:
+                act(w("fl", o, o + a), row(0, a), ACT.Sign, bias=col("bst", 64 + k))
 
         def s_sum(k):
-            o, a = 256 * (k - NV), 16 * (k + 1)
-            if a < 256:
-                act(w("jk", o + a, o + 256), w("sg", o + a, o + 256), ACT.Sign, bias=-0.5, scale=-1.0, accum=slot(k, 2))
-            act(w("jk", o, o + a), w("sg", o, o + a), ACT.Sign, bias=0.5, scale=-1.0, accum=slot(k, 1))
+            o = 2 * SROWS.index(k)
+            scan(counted(k, 128), part("fl", o), part("fl", o + 1), col("ac", 16 + k), ALU.add, ALU.add)
 
-        v_cmp(0)
-        scan(w("es", 256, 512), w("kq"), w("ee"), 0.0, ALU.mult, ALU.add)
-        v_cmp(1)
-        tt(w("q1"), w("es", 15, 512, 16), w("ka"), ALU.mult)
-        v_cmp(2)
-        tt(w("ac", 0, 128, 4), w("q1"), w("kb"), ALU.add)
+        if R == 0:
+            ts(w("cm", 256, 512), w("jj"), q_, ALU.not_equal)
+        v_cmp(VROWS[0])
+        scan(w("es"), w("cm"), w("ee"), 0.0, ALU.mult, ALU.add)
+        v_cmp(VROWS[1])
+        tt(w("q1", 0, 32), w("es", 15, 512, 16), w("ka"), ALU.mult)
+        for k in VROWS[2:3]:
+            v_cmp(k)
+        tt(w("ac"), w("q1", 0, 32), w("kb"), ALU.add)
         if raw:
             quant(w("lq0", 0, raw), w("lp0", 0, raw), w("rt"))
-        s_cmp(NV)
-        for k in range(NV, 16):
-            if k + 1 < 16:
-                s_cmp(k + 1)
-            s_sum(k)
-            if k == NV + 3:
-                act(w("pw"), ind(w("ac", 0, 64), lst("o_4")), ACT.Copy)
-        for k in range(NV):
-            if k + 3 < NV:
-                v_cmp(k + 3)
+        for k in VROWS[3:]:
+            v_cmp(k)
+        for k in SROWS[:3]:
+            s_cmp(k, True)
+        for n, k in enumerate(SROWS):
+            if n >= 3:
+                s_cmp(k, True)
+            s_cmp(k, False)
+            if n == PW:
+                act(w("pw"), ind(w("ac", 0, 16), lst("o_c")), ACT.Copy)
+        for k in VROWS:
             v_sum(k)
-        trans(part("pr", 0), part("pw", 0))
-        scan(w("so", 128 * NV + 31, 1920, 32), w("k4", 0, 4 * NS - 4), w("ac", 64 + 4 * NV, 124), 0.0,
-             ALU.mult, ALU.add)
-        trans(part("pr", 1), part("pw", 1))
-        ts(col("l_s", 15), slot(15, 1), 0.5, ALU.mult, slot(15, 0), ALU.add)
-        ts(w("l_s", 0, 15), w("so", 127, 1920, 128), 0.5, ALU.mult, 128.0, ALU.add)
-        scatter(w("sw"), w("l_s"), w("pr"))
+        for n, k in enumerate(SROWS):
+            if n == len(SROWS) - 2:
+                trans(w("pr"), w("pw"))
+            s_sum(k)
+        l_s = w("so", LEND, LEND + 16)
+        scatter(w("sw"), l_s, w("pr"))
         unpack("lq%d" % R, "lp%d" % R)
         for b in range(4):
             act(part("tw", b, 256), bank(b), ACT.Copy, scale=0.5)
-        ts(w("xb", 0, 32, 2), w("l_s"), hf, ALU.subtract)
-        ts(w("xa", 1, 32, 2), w("l_s"), col("pc", 7), ALU.subtract, 1000.0, ALU.mult)
+        ts(w("xb", 0, 32, 2), l_s, hf, ALU.subtract)
+        ts(w("xa", 1, 32, 2), l_s, col("pc", 7), ALU.subtract, 1000.0, ALU.mult)
         trans(part("tb", 0), w("sw", 0, 128))
         trans(part("tb", 1), w("sw", 16, 144))
         scan(w("xo"), w("xa"), w("xb"), 0.0, ALU.max, ALU.min)
         picked = ind(w("tb"), lst("o_e", 0, 1))
-        ts(w("l_a"), picked, 2.0 ** -13, ALU.mult)
+        ts(w("l_a"), picked, 2.0 ** -8, ALU.mult, -0.498, ALU.add)
         ts(w("li", 0, 16), picked, 255, ALU.bitwise_and)
-        ts(w("li", 16, 32), picked, 4, ALU.logical_shift_right, 255, ALU.bitwise_and)
-        copy(w("l_x"), w("xo", 1, 32, 2))
+        ts(w("li", 16, 32), picked, 8, ALU.logical_shift_right, 240, ALU.bitwise_and)
+        ts(w("li", 32, 48), picked, 4, ALU.logical_shift_right, 15, ALU.bitwise_and)
         la, lb, le = w("l_a", 0, 8), w("l_k", 0, 8), w("l_k", 16, 24)
         copy(lb, w("li", 0, 8))
-        copy(le, w("li", 16, 24))
 
         for b in range(3):
             act(part("ag", b), ind(tw_(b), la), ACT.Copy, scale=2.0 ** -6)
         ts(part("ag", 3), ind(tw_(3), la), 2.0 ** -6, ALU.mult)
+        tt(le, w("li", 16, 24), w("li", 32, 40), ALU.add)
         for b in (0, 3, 1, 2):
             tt(w("zt", b, 512, 4), ind(part("tw", b, 256), lb), part("ag", b), ALU.add)
         quant(w("zq"), w("zp"), w("zt"))
+        copy(w("l_x"), w("xo", 1, 32, 2))
         if R == 1:
             quant(w("vq"), w("vp"), w("vb"))
         for b in range(4):
@@ -464,19 +557,25 @@ def rank_program(g, core, T, topo):
 
     for h in range(2):
         mm(h, 128, w("vq"), w("vp"), part("xq", h), part("xp", h))
-    dma("Y", T.oc[:], u8(w("xq")))
-    for k in range(4):
-        dma("Y", T.osc[4 * k:4 * k + 4, :], (T.xp[32 * k:32 * k + 4, :], w("xp")[1]))
-    copy(part("yb", 0), w("ps0", 0, 128))
-    act(part("yb", 1), w("ps1", 0, 128), ACT.Copy)
-    dma("Y", T.y[:, 0:128], part("yb", 0))
-    dma("S", T.y[:, 128:256], part("yb", 1))
+    def scales(q, k):
+        dma(q, T.osc[4 * k:4 * k + 4, :], (T.xp[32 * k:32 * k + 4, :], w("xp")[1]))
+
+    dma("Y", T.oc[:, 0:512], u8(part("xq", 0)))
+    act(part("yb", 0), w("ps0", 0, 128), ACT.Copy)
+    copy(part("yb", 1), w("ps1", 0, 128))
+    dma("Y", T.oc[:, 512:1024], u8(part("xq", 1)))
+    scales("Y", 0)
+    dma("S", T.y[:, 0:128], part("yb", 0))
+    dma("Y", T.y[:, 128:256], part("yb", 1))
+    for k in range(1, 4):
+        scales("S", k)
 
     _emit(eng, ops, T)
 
 
 def _emit(eng, ops, T):
     known = {q: 0 for q in eng}
+    done = {q: 0 for q in eng}
     seen = {}
     for n, o in enumerate(ops):
         deps = set()
@@ -501,8 +600,11 @@ def _emit(eng, ops, T):
             if not known[q] >> k & 1:
                 o["waits"].append(k)
                 ops[k]["sig"] = True
-                known[q] |= ops[k]["clo"] | 1 << k
+                known[q] |= ops[k]["clo"] | ops[k].get("before", 0) | 1 << k
         o["clo"] = known[q]
+        if o["kind"] == "c":
+            o["before"] = done[q]
+            done[q] |= 1 << n
     tail = [k for k, o in enumerate(ops) if o["kind"] == "r" and not o["sig"]]
     tail_d = [k for k, o in enumerate(ops) if o["kind"] == "d" and not o["sig"]]
     for k in tail_d:

@@ -4,7 +4,7 @@ from concourse.mybir import dt, AluOpType, AxisListType, ActivationFunctionType
 ALU, ACT = AluOpType, ActivationFunctionType
 F, B, I, U, X4, U8 = "float32", "bfloat16", "int32", "uint16", "float8_e4m3fn_x4", "uint8"
 MASKS = [1, 2, 4]
-VROWS = [6, 7, 8, 15]
+VROWS = [5, 6, 7, 8, 9, 15]
 PW = 8
 SROWS = [k for k in range(16) if k not in VROWS]
 LEND = 16 * 127
@@ -37,11 +37,11 @@ SCRATCH = {
     "ones": _sb(256, B), "ident": _sb(128, B), "eb": _sb(520, B), "eq": _sb(512, X4), "ep": _sb(512, U8),
     "gb": _sb(256, F), "gc": _sb(256, F), "pc": _sb(16, F), "i16": _sb(32, F), "ibc": _sb(16, F), "i01": _sb(16, F),
     "ist": _sb(16, F), "jj": _sb(256, B), "ft": _sb(136, F), "lo": _sb(136, U),
-    "kmax": _sb(256, B), "k4": _sb(64, B), "cm": _sb(512, B), "sr": _sb(32, F), "ch": _sb(256, B), "ka": _sb(32, F), "kb": _sb(32, F),
+    "kmax": _sb(256, B), "k4": _sb(64, B), "cm": _sb(512, B), "sr": _sb(32, F), "ch": _sb(256, B), "kb": _sb(16, F),
     "o1": _sb(288, F), "s0": _sb(384, F), "s1": _sb(512, F),
     "tt": _sb(1024, B), "win": _sb(4 * 384, B), "tw": _sb(1024, B),
     "sm": _sb(384, F), "pm": _sb(640, F), "bc": _sb(256, F), "bst": _sb(80, F),
-    "ee": _sb(512, B), "es": _sb(512, B), "q1": _sb(80, F), "ac": _sb(32, F), "pw": _sb(256, U), "pr": _sb(256, U),
+    "ee": _sb(512, B), "es": _sb(512, B), "q1": _sb(16, F), "ac": _sb(16, F), "e0": _sb(16, B), "pw": _sb(256, U), "pr": _sb(256, U),
     "cb": _sb(len(VROWS) * 256, B), "so": _sb(LEND + 16, U), "fl": _sb(len(SROWS) * 256, U),
     "l_s": _sb(16, U), "sw": _sb(272, I if INT else F), "tb": _sb(256, I if INT else F), "i2": _sb(64, F),
     "o2": _sb(64, F), "vi": _sb(16, I), "li": _sb(48, I), "l_k": _sb(32, U), "l_a": _sb(16, U),
@@ -254,8 +254,6 @@ def rank_program(g, core, T, topo):
     lin(flt("o_d"), w("ibc", 0, 4), 16.0, bs("od"))
     fill(w("kmax", 0, 256, 16), 16, -BIG)
     fill(w("ee", 0, 256), 256, 1)
-    fill(w("ka", 0, 16), 16, WM)
-    fill(w("ka", 16, 32), 16, -1)
     fill(w("xa", 0, 32, 2), 16, 1000)
     fill(w("i01", 0, 16, 2), 8, 0)
     fill(w("i01", 1, 16, 2), 8, 32)
@@ -299,7 +297,6 @@ def rank_program(g, core, T, topo):
 
     def later_constants():
         lin(col("pc", 4), q_, 16.0, -float(WM))
-        lin(w("kb", 16, 32), bs("hf", 16))
         lin(col("pc", 5), hf, 256.0, col("pc", 4))
         lin(w("kb", 0, 16), w("ibc"), 8192.0, col("pc", 5))
         lin(col("pc", 7), hf, 1.0, 127.5)
@@ -470,7 +467,7 @@ def rank_program(g, core, T, topo):
 
         def v_sum(k):
             o = 2 * VROWS.index(k)
-            scan(counted(k, 128), part("cb", o), part("cb", o + 1), col("ac", 16 + k), ALU.add, ALU.add)
+            scan(counted(k, 128), part("cb", o), part("cb", o + 1), col("e0", k), ALU.add, ALU.add)
 
         def s_cmp(k, later):
             a, o = 16 * (k + 1), 256 * SROWS.index(k)
@@ -481,17 +478,18 @@ def rank_program(g, core, T, topo):
 
         def s_sum(k):
             o = 2 * SROWS.index(k)
-            scan(counted(k, 128), part("fl", o), part("fl", o + 1), col("ac", 16 + k), ALU.add, ALU.add)
+            scan(counted(k, 128), part("fl", o), part("fl", o + 1), col("e0", k), ALU.add, ALU.add)
 
         if R == 0:
             ts(w("cm", 256, 512), w("jj"), q_, ALU.not_equal)
         v_cmp(VROWS[0])
         scan(w("es"), w("cm"), w("ee"), 0.0, ALU.mult, ALU.add)
         v_cmp(VROWS[1])
-        tt(w("q1", 0, 32), w("es", 15, 512, 16), w("ka"), ALU.mult)
+        ts(w("q1"), w("es", 15, 256, 16), float(WM), ALU.mult)
+        ts(w("e0"), w("es", 271, 512, 16), -1.0, ALU.mult, hf, ALU.add)
         for k in VROWS[2:3]:
             v_cmp(k)
-        tt(w("ac"), w("q1", 0, 32), w("kb"), ALU.add)
+        tt(w("ac"), w("q1"), w("kb"), ALU.add)
         if raw:
             quant(w("lq0", 0, raw), w("lp0", 0, raw), w("rt"))
         for k in VROWS[3:]:

@@ -4,25 +4,31 @@ from concourse.mybir import dt, AluOpType, AxisListType, ActivationFunctionType
 ALU, ACT = AluOpType, ActivationFunctionType
 F, B, I, U, X4, U8 = "float32", "bfloat16", "int32", "uint16", "float8_e4m3fn_x4", "uint8"
 MASKS = [1, 2, 4]
-VROWS = [5, 6, 7, 8, 9, 15]
-PW = 8
-SROWS = [k for k in range(16) if k not in VROWS]
+RANK = "su1 su2 mx1 bc1 zz0 mx2 bc2 su0 mg1 mx0 rw0 rw1 rw2 rw3 ng ab tr1 tr2 mt2 ee be ve4 vl4 es ve5 vl5 pa pb sl0 sl1 sl2 sl3 ve6 vl6 rw4 ve7 vl7 vl14 se0 se1 se2 se3 sl8 se8 sl9 se9 sl10 se10 sl11 se11 sl12 se12 sl13 se13 se14 se15 ct4 ct5 pr ct6 ct7 ct0 ct1 ct2 ct3 ct8 ct9 ct10 ct11 ct12 sc0 ct13 ct14 ct15 sc1"
+CUTS = [10]
+MEAN = "xb as0 as1 as2 bs2 av3 bv3 zg0 zp3 zg1 zp2 qz lx te0 te1 te2 te3"
+OUT0 = "po0 po1 t10 t11 g2 ck pe0 pe1 pe2 pe3 t2 go cj s10 s11 cl tv0 tv1 tv2 tv3 sa sb qs ws0 ws1 ws2 ws3"
+OUT1 = "qv po0 pe0 pe1 po1 pe2 pe3 t10 t11 g2 t2 go s10 ts0 s11 tv1 tv2 sa tv3 sb qs ws0 ws1 ws2 ws3"
+OUT2 = "pe0 pe1 pe2 pe3 po0 po1 ts0 ts1 ts2 t10 t11 g2 t2 go s10 s11 sa sb tv3 qs wt0 wt1 wt2 wt3"
+OUT = [OUT0, OUT1, OUT2]
+LATE = ["||", "||", "||"]
+SPLIT = True
+LOAD = 0
+XQF = False
+STORE = 4
+IDF = 3
+UN0 = 4
+UN1 = 4
 LEND = 16 * 127
 STEP = 2.0 ** -24 * (1 + 2.0 ** -23)
 TINY = 2.0 ** -120
-INT = True
-PICKS = [("A", 0, 0, 0), ("A", 1, 0, 0), ("A", 2, 0, 0), ("A", 3, 0, 0), ("S", 0, 0, 16), ("S", 1, 0, 16), ("V", 2, 0, 8), ("V", 3, 0, 10), ("V", 2, 8, 16), ("S", 3, 10, 16), ("Q", 0, 0, 0), ("Q", 1, 0, 0)]
-BH = 2
-E0 = True
-XL = True
+TB = ()
+MMO = (0, 1, 2, 3)
+PICKS = [("A", 0, 0, 0), ("A", 1, 0, 0), ("A", 2, 0, 0), ("A", 3, 0, 0), ("S", 0, 0, 16), ("S", 2, 0, 16), ("V", 1, 0, 8), ("V", 3, 0, 12), ("V", 1, 8, 16), ("S", 3, 12, 16), ("Q", 0, 0, 0), ("Q", 1, 0, 0)]
 RAW = True
-QL = ()
-HELP = 0
-WV = 1
 BIG = 1.0e29
-WM = 257
-LISTS = {"o_u": (0, 16), "o_d": (16, 4), "o_s": (20, 24), "o_m": (44, 24), "o_i": (68, 16), "o_t": (84, 2),
-         "o_c": (86, 16), "o_4": (102, 16), "o_e": (118, 2)}
+LISTS = {"o_u": (0, 16), "o_d": (16, 4), "o_s": (20, 24), "o_m": (44, 24), "o_i": (68, 8), "o_t": (76, 2),
+         "o_y": (78, 16), "o_e": (94, 2), "o_q": (96, 16)}
 
 
 def _sb(n, d):
@@ -35,18 +41,17 @@ SCRATCH = {
     "vb": _sb(512, B), "vq": _sb(128, X4), "vp": _sb(128, U8),
     "wq": _sb(512, X4), "wp": _sb(512, U8),
     "ones": _sb(256, B), "ident": _sb(128, B), "eb": _sb(520, B), "eq": _sb(512, X4), "ep": _sb(512, U8),
-    "gb": _sb(256, F), "gc": _sb(256, F), "pc": _sb(16, F), "i16": _sb(32, F), "ibc": _sb(16, F), "i01": _sb(16, F),
-    "ist": _sb(16, F), "jj": _sb(256, B), "ft": _sb(136, F), "lo": _sb(136, U),
-    "kmax": _sb(256, B), "k4": _sb(64, B), "cm": _sb(512, B), "sr": _sb(32, F), "ch": _sb(256, B), "kb": _sb(16, F),
+    "gb": _sb(128, F), "gc": _sb(128, F), "pc": _sb(32, F), "i16": _sb(32, F), "ibc": _sb(16, F), "i01": _sb(16, F),
+    "ist": _sb(16, F), "ft": _sb(16, F), "lo": _sb(112, U),
+    "kmax": _sb(128, B), "cm": _sb(512, B), "kb": _sb(16, F),
     "o1": _sb(288, F), "s0": _sb(384, F), "s1": _sb(512, F),
     "tt": _sb(1024, B), "win": _sb(4 * 384, B), "tw": _sb(1024, B),
     "sm": _sb(384, F), "pm": _sb(640, F), "bc": _sb(256, F), "bst": _sb(80, F),
-    "ee": _sb(512, B), "es": _sb(512, B), "q1": _sb(16, F), "ac": _sb(16, F), "e0": _sb(16, B), "pw": _sb(256, U), "pr": _sb(256, U),
-    "cb": _sb(len(VROWS) * 256, B), "so": _sb(LEND + 16, U), "fl": _sb(len(SROWS) * 256, U),
-    "l_s": _sb(16, U), "sw": _sb(272, I if INT else F), "tb": _sb(256, I if INT else F), "i2": _sb(64, F),
-    "o2": _sb(64, F), "vi": _sb(16, I), "li": _sb(48, I), "l_k": _sb(32, U), "l_a": _sb(16, U),
-    "xa": _sb(32, F), "xb": _sb(32, F), "xo": _sb(32, F), "l_x": _sb(16, U),
-    "ag": _sb(512, F), "te": _sb(512, F), "zt": _sb(512, B), "zq": _sb(128, X4), "zp": _sb(128, U8),
+    "ee": _sb(512, B), "es": _sb(512, B), "pw": _sb(256, B), "pr": _sb(256, B),
+    "so": _sb(LEND + 16, U), "fl": _sb(16 * 256, U),
+    "sw": _sb(272, B), "tb": _sb(288, B), "i2": _sb(64, F), "l_k": _sb(32, U),
+    "xa": _sb(16, F), "xb": _sb(16, F), "xc": _sb(16, F), "l_x": _sb(16, U), "hz": _sb(384 * len(TB) + 8, F),
+    "ag": _sb(512, F), "bg": _sb(512, F), "te": _sb(512, F), "zt": _sb(512, B), "zq": _sb(128, X4), "zp": _sb(128, U8),
     "yb": _sb(256, F), "rq": _sb(128, X4), "rp": _sb(128, U8), "rt": _sb(512, B), "hq": _sb(128, X4),
 }
 for _r in range(3):
@@ -61,7 +66,7 @@ for _k in range(8):
 
 NC, ND = 110, 16
 SEMAPHORES = (["c%d" % k for k in range(NC)] + ["d%d" % k for k in range(ND)]
-              + ["%s%d" % (n, r) for n in ("as", "aq", "gs", "gq", "gp") for r in range(3)] + ["ar", "gr", "gx", "ah"])
+              + ["%s%d" % (n, r) for n in ("as", "aq", "gs", "gq", "gp") for r in range(3)] + ["ar", "gr", "gx", "ah", "aw"])
 
 
 def _bits(engs):
@@ -89,7 +94,7 @@ def _hand_on(g, core, T, topo):
                     rid, pid, _ = topo.addr(peer)
                     g.wait_ge(T.sem.ah, len(topo.engines(c, core)) - len(topo.engines(c, peer)))
                     g.remote_dma(T["lq%d" % R][:, 128:256].bitcast(dt.uint8), T.hq[:].bitcast(dt.uint8),
-                                 T.sem["aq%d" % R], T.sem.gx, pid, rid, _bits(en))
+                                 T.sem.aw, T.sem.gx, pid, rid, _bits(en))
                     g.wait_ge(T.sem.gx, len(en))
 
 
@@ -215,29 +220,42 @@ def rank_program(g, core, T, topo):
         o, n = LISTS[name]
         return w(table, o + a, o + (n if b is None else b))
 
-    def flt(name, a=0, b=None):
-        return lst(name, a, b, "ft")
-
-    if XL:
+    if LOAD == 0:
         dma("Y", part("x0", 0, 512), T.x[:, 0:512])
         dma("S", w("ub"), T.u[:])
         dma("Y", part("x0", 1, 512), T.x[:, 512:1024])
-    else:
-        dma("Y", w("x0"), T.x[:])
+    elif LOAD == 1:
+        for k, q in enumerate("YS"):
+            dma(q, (T.x0[64 * k:64 * k + 64, 0:512], part("x0", k, 256)[1]), T.x[64 * k:64 * k + 64, 0:512])
+        dma("Y", part("x0", 1, 512), T.x[:, 512:1024])
         dma("S", w("ub"), T.u[:])
+    else:
+        dma("S", part("x0", 0, 512), T.x[:, 0:512])
+        dma("Y", w("ub"), T.u[:])
+        dma("S", part("x0", 1, 512), T.x[:, 512:1024])
     memset(w("ones"), 1.0)
     BASES = [("od", 1, (0, 32, 0)), ("hf", 0, (16, 0, 0)), ("rf", 15, (16, -2, -1)), ("d", -1, (1, 0, 1))]
     base = {}
+
+    def identity():
+        op("G", "c", lambda e: e.affine_select(T.ident[:], T.ones[:, 0:128], [[-1, 128]], ALU.is_equal, 0.0, 0, 1),
+           [w("ones")], [w("ident")])
+
+    def unit(b):
+        quant(part("eq", b), part("ep", b), w("eb", 3 - b, 515 - b))
+
     for k, (name, b0, (sh, sb, st)) in enumerate(BASES):
         base[name] = 32 * k
         iota(part("gb", k, 32), [[sh, 2], [sb, 8], [st, 2]], b0)
-        if k == 0:
+        if k == 1:
+            if IDF:
+                identity()
             op("G", "c", lambda e: e.affine_select(T.gb[:, 0:32], T.gb[:, 0:32], [[1, 2], [0, 8], [-1, 2]], ALU.is_equal,
                                                    256.0, 0, 0), [part("gb", 0, 32)], [part("gb", 0, 32)])
-            iota(w("ibc"), [[1, 8], [0, 2]], 0)
-            op("G", "c", lambda e: e.affine_select(T.ident[:], T.ones[:, 0:128], [[-1, 128]], ALU.is_equal, 0.0, 0, 1),
-               [w("ones")], [w("ident")])
-            iota(flt("o_u"), [[16, 2], [32, 4], [0, 2]], 0)
+    iota(w("ft"), [[16, 2], [32, 4], [0, 2]], 0)
+    iota(w("ibc"), [[1, 8], [0, 2]], 0)
+    if not IDF:
+        identity()
     iota(w("i16"), [[16, 32]], 0)
     iota(w("ist"), [[32, 8], [256, 2]], 0)
 
@@ -249,58 +267,73 @@ def rank_program(g, core, T, topo):
 
     memset(w("eb"), 0.0)
     memset(w("o1", 256, 288), 0.0)
-    trans(part("gc", 0, 32), part("gb", 0, 32))
-    fill(w("kmax"), 256, 0)
-    lin(flt("o_d"), w("ibc", 0, 4), 16.0, bs("od"))
-    fill(w("kmax", 0, 256, 16), 16, -BIG)
+    memset(w("pw"), 0.0)
+    memset(w("sw", 0, 16), 0.0)
+    memset(w("kmax"), 0.0)
+    for k in range(len(TB)):
+        memset(w("hz", 384 * k + 128, 384 * k + 384), 0.0)
     fill(w("ee", 0, 256), 256, 1)
-    fill(w("xa", 0, 32, 2), 16, 1000)
     fill(w("i01", 0, 16, 2), 8, 0)
     fill(w("i01", 1, 16, 2), 8, 32)
-    fill(flt("o_t", 1, 2), 1, 0)
-    copy(w("eb", 3, 515, 4), w("ident"))
-    copy(w("lo", 0, 20), w("ft", 0, 20))
-    for b in range(4):
-        quant(part("eq", b), part("ep", b), w("eb", 3 - b, 515 - b))
+    fill(w("kmax", 0, 128, 16), 8, -BIG)
+    if IDF:
+        copy(w("eb", 3, 515, 4), w("ident"))
+        for b in range(IDF):
+            unit(b)
+    trans(w("gc"), w("gb"))
+    copy(lst("o_u"), w("ft"))
     hf, rf, d_ = bs("hf"), bs("rf"), bs("d")
-    same, q_, qr, t_, b16, u_, y_, oe = [col("pc", k) for k in (0, 1, 8, 2, 9, 10, 11, 12)]
-    trans(w("gc", 32, 128), w("gb", 32, 128))
-    memset(w("sw", 0, 16), 0)
-    lin(col("pc", 3), hf, 14.0, rf)
+    same, q_, qr, t_, b16, u_, y_ = [col("pc", k) for k in (0, 1, 8, 2, 9, 10, 11)]
     lin(qr, hf, -1.0, rf)
     lin(t_, hf, -0.0625, d_)
-    lin(flt("o_s", 8, 24), w("ist"), None, rf)
-    lin(flt("o_s", 0, 8), w("i16", 1, 16, 2), None, col("pc", 3))
+    act(same, d_, ACT.Abs)
+    lin(lst("o_d"), w("ibc", 0, 4), 16.0, bs("od"))
+    lin(col("pc", 3), hf, 14.0, rf)
+    lin(q_, qr, -1.0, 15.0)
+    lin(b16, t_, 1.0, qr)
+    lin(lst("o_m", 0, 8), bs("hf", 8), None, rf)
+    lin(lst("o_m", 8, 24), w("i01"), None, qr)
+    if not IDF:
+        copy(w("eb", 3, 515, 4), w("ident"))
 
     def first_constants():
-        act(same, d_, ACT.Abs)
-        lin(q_, qr, -1.0, 15.0)
-        lin(b16, t_, 1.0, qr)
-        lin(flt("o_m", 0, 8), bs("hf", 8), None, rf)
-        lin(flt("o_m", 8, 24), w("i01"), None, qr)
-        lin(oe, t_, 112.0, hf)
         lin(y_, b16, -8.0, 127.0)
         lin(u_, b16, -8.0, hf)
-
-    def early_constants():
-        lin(flt("o_i"), w("i16", 0, 16), 1.0, 15.0)
-        lin(flt("o_c"), w("i16", 0, 16), 0.0625)
+        lin(lst("o_s", 8, 24), w("ist"), None, rf)
+        lin(lst("o_s", 0, 8), w("i16", 1, 16, 2), None, col("pc", 3))
         lin(col("pc", 13), same, 240.0, y_)
-        lin(col("pc", 14), q_, 16.0, oe)
-        lin(flt("o_t", 0, 1), u_, same, col("pc", 13))
+        lin(lst("o_i"), w("i16", 0, 8), 1.0, 15.0)
+        lin(col("pc", 16), hf, -0.0625, 2.0)
+        lin(col("pc", 17), hf, -8.0, 143.0)
+        lin(col("pc", 18), hf, 0.0625, 1.0)
+        lin(col("pc", 19), hf, 9.0, 15.0)
+        lin(lst("o_t", 0, 1), u_, same, col("pc", 13))
 
-    def late_counts():
-        iota(w("jj"), [[0, 16], [1, 16]], 0)
+    def kind_constants():
+        ts(col("pc", 21), q_, 8.0, ALU.is_ge, -127.0, ALU.mult)
+        ts(col("pc", 12), same, -1.0, ALU.add)
 
-    def late_constants():
-        ts(lst("o_e", 0, 1), col("pc", 14), 112.0, ALU.add, 255.0, ALU.min)
+    def entry_constants():
+        lin(lst("o_q"), w("ee", 0, 16), q_)
+        lin(col("pc", 5), hf, 1.0, -1.0)
+        lin(col("pc", 6), hf, 1.0, q_)
+        lin(col("pc", 4), q_, 16.0, -1.0)
+        lin(w("kb"), w("ibc"), 32.0, col("pc", 5))
+        lin(w("pw", 2, 256, 16), w("ibc"), 32.0, col("pc", 6))
+
+    def row_constants():
+        for t in range(2):
+            o = LISTS["o_y"][0]
+            lin(w("lo", o + t, o + 16, 2), w("i16", 0, 8), col("pc", 16 + 2 * t), col("pc", 17 + 2 * t))
 
     def later_constants():
-        lin(col("pc", 4), q_, 16.0, -float(WM))
-        lin(col("pc", 5), hf, 256.0, col("pc", 4))
-        lin(w("kb", 0, 16), w("ibc"), 8192.0, col("pc", 5))
-        lin(col("pc", 7), hf, 1.0, 127.5)
-        lin(w("xb", 1, 32, 2), w("i16", 8, 24), None, q_)
+        lin(col("pc", 22), q_, 16.0, col("pc", 21))
+        lin(w("xc"), w("i16", 8, 24), None, q_)
+        ts(col("pc", 23), col("pc", 12), -144.0, ALU.mult, col("pc", 22), ALU.add)
+        lin(lst("o_e"), w("i16", 0, 2), 0.125, col("pc", 23))
+
+    def up(b):
+        return 1.0 if b in TB else 32.0
 
     def tw_(b):
         return w("win", 384 * b + 128, 384 * b + 384)
@@ -324,57 +357,40 @@ def rank_program(g, core, T, topo):
     for R, mask in enumerate(MASKS):
         peer = T.cores[rank ^ mask]
         en = topo.engines(core, peer)
-        if R == 0 and not E0:
-            e_s, e_q = en[:len(en) // 2], en[len(en) // 2:]
-        else:
-            e_s, e_q = en, en
+        e_s, e_q = en, en
         raw = 128 if R == 0 and RAW else 0
         if R == 0:
+            for b in range(IDF, UN0):
+                unit(b)
+            if XQF:
+                quant(part("xq", 0), part("xp", 0), part("x0", 0, 512))
             quant(w("uq"), w("up"), w("ub"))
+            for b in range(max(IDF, UN0), UN1):
+                unit(b)
+            if not IDF:
+                entry_constants()
+            if XQF:
+                first_constants()
             for h in range(2):
                 act(part("u0p", h), ind(w("up"), lst("o_u", 8 * h, 8 * h + 8)), ACT.Copy)
-            first_constants()
-            quant(part("xq", 0), part("xp", 0), part("x0", 0, 512))
+            if not XQF:
+                first_constants()
+            if IDF:
+                entry_constants()
+            row_constants()
+            if not XQF:
+                quant(part("xq", 0), part("xp", 0), part("x0", 0, 512))
             if raw:
                 send(peer, T.rp[:], w("xp", 0, raw), "ar", "gr", en)
+            if XQF:
+                quant(part("xq", 1), part("xp", 1), part("x0", 1, 512))
             pick_u(0)
-            quant(part("xq", 1), part("xp", 1), part("x0", 1, 512))
+            pick_u(1)
+            if not XQF:
+                quant(part("xq", 1), part("xp", 1), part("x0", 1, 512))
         for h in range(2):
             mm(4 + 3 * h, 128, w("uq"), w("up"), part("xq", h), part("xp", h))
-        if R == 0:
-            pick_u(1)
         far = topo.chip(peer) != topo.chip(core)
-        if not far:
-            own_scores()
-        unpack("xq", "xp")
-        if far:
-            own_scores()
-            for b in range(3):
-                act(w("tt", b, 1024, 4), bank(b), ACT.Copy)
-        for h in range(2):
-            trans(part("o1", h), bank(4 + 3 * h, 128))
-        if R == 0:
-            copy(lst("o_s"), flt("o_s"))
-        copy(w("i2"), ind(w("o1"), lst("o_d")))
-        trans(w("ss%d" % R), w("i2"))
-        fold(peer, T["sl%d" % R][:], w("ss%d" % R, 0, 48), w("ss%d" % R, 16, 64), "as%d" % R, "gs%d" % R, e_s)
-        if raw:
-            send(peer, T.rq[:].bitcast(dt.uint8), u8(w("xq", 0, raw)), "ar", "gx", en)
-        for h in range(2):
-            act(part("s1", h, 256), bank(5 + h), ACT.Copy)
-        if R == 0:
-            late_counts()
-        act(w("s0", 128, 384), ind(w("s1"), lst("o_s", 8, 24)), ACT.Copy)
-        if R == 0:
-            early_constants()
-        if not far:
-            act(w("tt", 4 * raw + 3, 1024, 4), w("ps3", raw, 256), ACT.Copy)
-        act(w("s0", 0, 128), ind(w("s1"), lst("o_s", 0, 8)), ACT.Copy)
-        for b in [3] if far else range(3):
-            copy(w("tt", 4 * raw + b, 1024, 4), w("ps%d" % b, raw, 256))
-        if R == 0:
-            copy(w("lo", 44, 102), w("ft", 44, 102))
-            late_constants()
 
         def send_codes():
             quant(w("tq%d" % R, raw), w("tp%d" % R, raw), w("tt", 4 * raw))
@@ -393,19 +409,43 @@ def rank_program(g, core, T, topo):
                      e_q)
             send(peer, T["lp%d" % R][:, raw:256], w("tp%d" % R, raw), "aq%d" % R, "gp%d" % R, e_q)
 
-        if R not in QL:
-            send_codes()
-        for b in range(4):
-            if raw and b < WV:
-                ts(tw_(b), bank(b), 32.0, ALU.mult)
-            elif far:
-                ts(tw_(b), w("tt", b, 1024, 4), 32.0, ALU.mult)
-            else:
-                act(tw_(b), bank(b), ACT.Copy, scale=32.0)
-        if R == 0:
-            later_constants()
+        def scores_out():
+            fold(peer, T["sl%d" % R][:], w("ss%d" % R, 0, 48), w("ss%d" % R, 16, 64), "as%d" % R, "gs%d" % R, e_s)
+            if raw:
+                send(peer, T.rq[:].bitcast(dt.uint8), u8(w("xq", 0, raw)), "ar", "gx", en)
+
+        def step(name):
+            k, b = name[:2], int(name[2:] or 0)
+            tile = w("tt", 4 * raw + b, 1024, 4), w("ps%d" % b, raw, 256)
+            {"po": lambda: mm(5 + b, 256, part("u0q", b), part("u0p", b), w("xq"), w("xp")),
+             "pe": lambda: mm(b, 256, part("eq", b), part("ep", b), w("xq"), w("xp")),
+             "un": lambda: unit(b),
+             "t1": lambda: trans(part("o1", b), bank(4 + 3 * b, 128)),
+             "g2": lambda: copy(w("i2"), ind(w("o1"), lst("o_d"))),
+             "t2": lambda: trans(w("ss%d" % R), w("i2")),
+             "go": scores_out,
+             "s1": lambda: act(part("s1", b, 256), bank(5 + b), ACT.Copy),
+             "sa": lambda: act(w("s0", 128, 384), ind(w("s1"), lst("o_s", 8, 24)), ACT.Copy),
+             "sb": lambda: act(w("s0", 0, 128), ind(w("s1"), lst("o_s", 0, 8)), ACT.Copy),
+             "tv": lambda: copy(*tile),
+             "ts": lambda: act(tile[0], tile[1], ACT.Copy),
+             "qs": send_codes,
+             "qv": lambda: quant(w("vq"), w("vp"), w("vb")),
+             "wv": lambda: ts(tw_(b), bank(b), up(b), ALU.mult),
+             "wt": lambda: ts(tw_(b), w("tt", b, 1024, 4), up(b), ALU.mult),
+             "ws": lambda: act(tw_(b), bank(b), ACT.Copy, scale=up(b)),
+             "ck": kind_constants,
+             "cj": lambda: ts(w("cm", 256, 512), ind(part("gb", 2, 32), lst("o_q")), qr, ALU.not_equal),
+             "cl": later_constants}[k]()
+
+        for name in OUT[R].split():
+            step(name)
         arrive([w("sl%d" % R)], "as%d" % R, len(e_s))
-        arrive([w("lq%d" % R, raw), w("lp%d" % R, raw)], "aq%d" % R, (3 if far else 2) * len(e_q))
+        if far:
+            arrive([part("lq%d" % R, 0), w("lp%d" % R)], "aq%d" % R, 2 * len(e_q))
+            arrive([part("lq%d" % R, 1)], "aw", len(e_q))
+        else:
+            arrive([w("lq%d" % R, raw), w("lp%d" % R, raw)], "aq%d" % R, 2 * len(e_q))
         if R == 0:
             dma("Y", u8(w("wq")), (T.wc[:], w("sl0")[1]))
             dma("Y", w("wp"), T.ws[:])
@@ -417,38 +457,12 @@ def rank_program(g, core, T, topo):
         row0 = 384
         ends = lst("o_i", 0, 8)
 
-        def sums(k):
-            tt(part("sm", k), ind(w("sl%d" % R), lst("o_m", 8 * k, 8 * k + 8)), part("s0", k), ALU.add)
+        def spread(k):
+            return ind(w("sl%d" % R), lst("o_m", 8 * k, 8 * k + 8))
 
-        def maxima(k):
-            scan(part("pm", k), w("kmax", 0, 128), part("sm", k), 0.0, ALU.add, ALU.max)
-            if k:
-                act(part("bc", k - 1), ind(part("pm", k), ends), ACT.Copy)
-
-        def middles(k):
-            tt(part("cm", k - 1), ind(part("pm", k), ends), part("sm", k), ALU.not_equal)
-
-        sums(1)
-        sums(2)
-        maxima(1)
-        maxima(2)
-        sums(0)
-        middles(1)
-        maxima(0)
         mine = ind(w("pm", 0, 384), lst("o_t", 0, 1))
-        act(w("bst", 0, 16), mine, ACT.Copy)
-        act(w("bst", 16, 32), mine, ACT.Copy, scale=-1.0)
-        act(w("bst", 32, 48), mine, ACT.Abs, scale=STEP)
-        act(w("bst", 48, 64), mine, ACT.Identity, scale=-1.0, bias=TINY)
-        for b in range(4 if raw else 0):
-            act(w("rt", b, 4 * raw, 4), bank(4 + b, raw), ACT.Copy)
-        for h in range(2):
-            trans(part("pm", 3 + h), part("bc", h))
-        middles(2)
-        if R in QL:
-            send_codes()
-        tt(w("ee", 256, 512), ind(w("bst", 0, 16), lst("o_c")), w("pm", 384, 640), ALU.is_equal)
-        tt(w("bst", 64, 80), w("bst", 32, 48), w("bst", 48, 64), ALU.add)
+        mid = w("es", 15, 256, 16)
+        l_s = w("so", LEND, LEND + 16)
 
         def own(k):
             return col("bst", k)
@@ -456,99 +470,102 @@ def rank_program(g, core, T, topo):
         def row(a=0, b=256):
             return w("pm", row0 + a, row0 + b)
 
-        def counted(k, n):
-            return w("so", LEND + k - 16 * (n - 1), LEND + 16, 16)
+        def flags(k, later):
+            a = 16 * (k + 1)
+            a, b = (a, 256) if later else (0, a)
+            return w("fl", 256 * k + a, 256 * k + b), row(a, b)
 
-        def v_cmp(k):
-            a, o = 16 * (k + 1), 256 * VROWS.index(k)
-            ts(w("cb", o, o + a), row(0, a), own(k), ALU.is_ge)
-            if a < 256:
-                ts(w("cb", o + a, o + 256), row(a, 256), own(k), ALU.is_gt)
+        def raw_step(k):
+            if raw and k < 4:
+                act(w("rt", k, 4 * raw, 4), bank(4 + k, raw), ACT.Copy)
+            elif raw:
+                quant(w("lq0", 0, raw), w("lp0", 0, raw), w("rt"))
 
-        def v_sum(k):
-            o = 2 * VROWS.index(k)
-            scan(counted(k, 128), part("cb", o), part("cb", o + 1), col("e0", k), ALU.add, ALU.add)
+        def piece(k):
+            a, b = ([0] + CUTS + [16])[k:k + 2]
+            scatter(w("sw", 16, 272), w("so", LEND + a, LEND + b), w("pr", 16 * a, 16 * b))
 
-        def s_cmp(k, later):
-            a, o = 16 * (k + 1), 256 * SROWS.index(k)
-            if later:
-                act(w("fl", o + a, o + 256), row(a, 256), ACT.Sign, bias=col("bst", 16 + k))
-            else:
-                act(w("fl", o, o + a), row(0, a), ACT.Sign, bias=col("bst", 64 + k))
+        def rank_step(name):
+            c, k = name[:2], int(name[2:] or 0)
+            {"su": lambda: tt(part("sm", k), spread(k), part("s0", k), ALU.add),
+             "mx": lambda: scan(part("pm", k), w("kmax"), part("sm", k), 0.0, ALU.add, ALU.max),
+             "bc": lambda: act(part("bc", k - 1), ind(part("pm", k), ends), ACT.Copy),
+             "mg": lambda: tt(part("cm", k - 1), ind(part("pm", k), ends), part("sm", k), ALU.not_equal),
+             "mt": lambda: tt(part("cm", k - 1), part("bc", k - 1), part("sm", k), ALU.not_equal),
+             "ng": lambda: act(w("bst", 0, 16), mine, ACT.Copy, scale=-1.0),
+             "ab": lambda: act(w("bst", 16, 32), mine, ACT.Abs, scale=STEP, bias=-TINY),
+             "be": lambda: tt(w("bst", 32, 48), w("bst", 16, 32), w("bst", 0, 16), ALU.add),
+             "tr": lambda: trans(part("pm", 2 + k), part("bc", k - 1)),
+             "ee": lambda: tt(w("ee", 256, 512), ind(w("pm", 0, 384), lst("o_y")), row(), ALU.is_equal),
+             "es": lambda: scan(w("es"), w("cm"), w("ee"), 0.0, ALU.mult, ALU.subtract),
+             "eh": lambda: scan(part("es", k, 256), part("cm", k, 256), part("ee", k, 256), 0.0, ALU.mult, ALU.subtract),
+             "pa": lambda: tt(w("pw", 0, 256, 16), w("kb"), mid, ALU.subtract),
+             "pb": lambda: ts(w("pw", 1, 256, 16), mid, -1.0, ALU.mult, col("pc", 4), ALU.add),
+             "pc": lambda: lin(w("pw", 1, 256, 16), mid, -1.0, col("pc", 4)),
+             "pr": lambda: trans(w("pr"), w("pw")),
+             "rw": lambda: raw_step(k),
+             "ve": lambda: ts(*flags(k, False), own(k), ALU.add, 0.0, ALU.is_ge),
+             "vl": lambda: ts(*flags(k, True), own(k), ALU.add, 0.0, ALU.is_gt),
+             "se": lambda: act(*flags(k, False), ACT.Sign, bias=col("bst", 32 + k)),
+             "sl": lambda: act(*flags(k, True), ACT.Sign, bias=own(k)),
+             "ct": lambda: scan(w("so", LEND + k - 16 * 127, LEND + 16, 16), part("fl", 2 * k), part("fl", 2 * k + 1),
+                                col("es", 271 + 16 * k), ALU.add, ALU.add),
+             "zz": lambda: [step(x) for x in LATE[R].split("|")[k].split()],
+             "sc": lambda: piece(k)}[c]()
 
-        def s_sum(k):
-            o = 2 * SROWS.index(k)
-            scan(counted(k, 128), part("fl", o), part("fl", o + 1), col("e0", k), ALU.add, ALU.add)
+        for name in RANK.split():
+            rank_step(name)
+        if far and SPLIT:
+            for h in range(2):
+                for b in range(4):
+                    mm(4 * h + b, 128, part("eq", b), part("ep", b), part("lq%d" % R, h), part("lp%d" % R, h))
+            for h in range(2):
+                for b in range(4):
+                    act(part("tw", 2 * b + h), bank(4 * h + b, 128), ACT.Copy, scale=0.5)
+        else:
+            unpack("lq%d" % R, "lp%d" % R)
+            for b in range(4):
+                act(part("tw", b, 256), bank(b), ACT.Copy, scale=0.5)
+        act(w("xa"), l_s, ACT.Relu, scale=1000.0, bias=-127500.0)
+        trans(w("tb", 0, 128), w("sw", 16, 144))
+        trans(w("tb", 128, 288), w("sw", 0, 160))
+        copy(w("l_k"), ind(w("tb"), lst("o_e")))
+        la, lb, le = w("l_k", 0, 8), w("l_k", 8, 16), w("l_k", 16, 24)
 
-        if R == 0:
-            ts(w("cm", 256, 512), w("jj"), q_, ALU.not_equal)
-        v_cmp(VROWS[0])
-        scan(w("es"), w("cm"), w("ee"), 0.0, ALU.mult, ALU.add)
-        v_cmp(VROWS[1])
-        ts(w("q1"), w("es", 15, 256, 16), float(WM), ALU.mult)
-        ts(w("e0"), w("es", 271, 512, 16), -1.0, ALU.mult, hf, ALU.add)
-        for k in VROWS[2:3]:
-            v_cmp(k)
-        tt(w("ac"), w("q1"), w("kb"), ALU.add)
-        if raw:
-            quant(w("lq0", 0, raw), w("lp0", 0, raw), w("rt"))
-        for k in VROWS[3:]:
-            v_cmp(k)
-        for k in SROWS[:3]:
-            s_cmp(k, True)
-        for n, k in enumerate(SROWS):
-            if n >= 3:
-                s_cmp(k, True)
-            s_cmp(k, False)
-            if n == PW:
-                act(w("pw"), ind(w("ac", 0, 16), lst("o_c")), ACT.Copy)
-        for k in VROWS:
-            v_sum(k)
-        for n, k in enumerate(SROWS):
-            if n == len(SROWS) - 2:
-                trans(w("pr"), w("pw"))
-            s_sum(k)
-        l_s = w("so", LEND, LEND + 16)
-        scatter(w("sw"), l_s, w("pr"))
-        unpack("lq%d" % R, "lp%d" % R)
-        for b in range(4):
-            act(part("tw", b, 256), bank(b), ACT.Copy, scale=0.5)
-        ts(w("xb", 0, 32, 2), l_s, hf, ALU.subtract)
-        ts(w("xa", 1, 32, 2), l_s, col("pc", 7), ALU.subtract, 1000.0, ALU.mult)
-        trans(part("tb", 0), w("sw", 0, 128))
-        trans(part("tb", 1), w("sw", 16, 144))
-        scan(w("xo"), w("xa"), w("xb"), 0.0, ALU.max, ALU.min)
-        picked = ind(w("tb"), lst("o_e", 0, 1))
-        ts(w("l_a"), picked, 2.0 ** -8, ALU.mult, -0.498, ALU.add)
-        ts(w("li", 0, 16), picked, 255, ALU.bitwise_and)
-        ts(w("li", 16, 32), picked, 8, ALU.logical_shift_right, 240, ALU.bitwise_and)
-        ts(w("li", 32, 48), picked, 4, ALU.logical_shift_right, 15, ALU.bitwise_and)
-        la, lb, le = w("l_a", 0, 8), w("l_k", 0, 8), w("l_k", 16, 24)
-        copy(lb, w("li", 0, 8))
-
-        for b in range(3):
-            act(part("ag", b), ind(tw_(b), la), ACT.Copy, scale=2.0 ** -6)
-        ts(part("ag", 3), ind(tw_(3), la), 2.0 ** -6, ALU.mult)
-        tt(le, w("li", 16, 24), w("li", 32, 40), ALU.add)
-        for b in (0, 3, 1, 2):
-            tt(w("zt", b, 512, 4), ind(part("tw", b, 256), lb), part("ag", b), ALU.add)
-        quant(w("zq"), w("zp"), w("zt"))
-        copy(w("l_x"), w("xo", 1, 32, 2))
-        if R == 1:
-            quant(w("vq"), w("vp"), w("vb"))
-        for b in range(4):
-            act(part("te", b), ind(tw_(b), le), ACT.Copy)
-        for b in range(4):
+        for name in MEAN.split():
+            c, b = name[:2], int(name[2:] or 0)
+            theirs = ind(part("tw", b, 256), lb)
+            {"as": lambda: act(part("ag", b), ind(tw_(b), la), ACT.Copy, scale=0.5 / up(b)),
+             "av": lambda: ts(part("ag", b), ind(tw_(b), la), 0.5 / up(b), ALU.mult),
+             "bs": lambda: act(part("bg", b), theirs, ACT.Copy),
+             "bv": lambda: copy(part("bg", b), theirs),
+             "zg": lambda: tt(w("zt", b, 512, 4), theirs, part("ag", b), ALU.add),
+             "zp": lambda: tt(w("zt", b, 512, 4), part("bg", b), part("ag", b), ALU.add),
+             "qz": lambda: quant(w("zq"), w("zp"), w("zt")),
+             "xb": lambda: tt(w("xb"), w("xa"), l_s, ALU.add),
+             "lx": lambda: tt(w("l_x"), w("xb"), w("xc"), ALU.min),
+             "te": lambda: act(part("te", b), ind(tw_(b), le), ACT.Copy)}[c]()
+        for b in MMO:
             mm(4 + b, 128, part("wq", b), part("wp", b), w("zq"), w("zp"))
         for q, b, c0, c1 in PICKS:
             if q == "A":
                 tt(w("win", 384 * b, 384 * b + 128), bank(4 + b, 128), part("te", b), ALU.add)
                 continue
+            if q in "CD":
+                o = w("hz", 384 * TB.index(b), 384 * TB.index(b) + 128)
+                if q == "C":
+                    act(o, bank(4 + b, 128), ACT.Copy, scale=2.0 ** -5)
+                else:
+                    ts(o, bank(4 + b, 128), 2.0 ** -5, ALU.mult)
+                continue
             if q == "Q":
                 quant(part("xq", b), part("xp", b), part("xs", b, 512))
                 continue
             o, i = w("xs", 64 * c0 + b, 64 * c1, 4), ind(fw(b), w("l_x", c0, c1))
-            if q == "S":
+            if q == "T":
+                tt(o, ind(part("hz", TB.index(b), 384), w("l_x", c0, c1)),
+                   w("win", 384 * b + 128 + 16 * c0, 384 * b + 128 + 16 * c1), ALU.add)
+            elif q == "S":
                 act(o, i, ACT.Copy, scale=2.0 ** -5)
             else:
                 ts(o, i, 2.0 ** -5, ALU.mult)
@@ -558,15 +575,25 @@ def rank_program(g, core, T, topo):
     def scales(q, k):
         dma(q, T.osc[4 * k:4 * k + 4, :], (T.xp[32 * k:32 * k + 4, :], w("xp")[1]))
 
-    dma("Y", T.oc[:, 0:512], u8(part("xq", 0)))
-    act(part("yb", 0), w("ps0", 0, 128), ACT.Copy)
-    copy(part("yb", 1), w("ps1", 0, 128))
-    dma("Y", T.oc[:, 512:1024], u8(part("xq", 1)))
-    scales("Y", 0)
-    dma("S", T.y[:, 0:128], part("yb", 0))
-    dma("Y", T.y[:, 128:256], part("yb", 1))
-    for k in range(1, 4):
-        scales("S", k)
+    if STORE == 0:
+        dma("Y", T.oc[:, 0:512], u8(part("xq", 0)))
+        act(part("yb", 0), w("ps0", 0, 128), ACT.Copy)
+        copy(part("yb", 1), w("ps1", 0, 128))
+        dma("Y", T.oc[:, 512:1024], u8(part("xq", 1)))
+        scales("Y", 0)
+        dma("S", T.y[:, 0:128], part("yb", 0))
+        dma("Y", T.y[:, 128:256], part("yb", 1))
+        for k in range(1, 4):
+            scales("S", k)
+    else:
+        dma("Y", T.oc[:], u8(w("xq")))
+        act(part("yb", 0), w("ps0", 0, 128), ACT.Copy)
+        copy(part("yb", 1), w("ps1", 0, 128))
+        for k in range(STORE):
+            scales("Y", k)
+        dma("S", T.y[:], w("yb"))
+        for k in range(STORE, 4):
+            scales("S", k)
 
     _emit(eng, ops, T)
 

from concourse.bass import DstId, RemoteDMATransfer
from concourse.mybir import dt, AluOpType, AxisListType, ActivationFunctionType

ALU, ACT = AluOpType, ActivationFunctionType
F, B, I, U, X4, U8 = "float32", "bfloat16", "int32", "uint16", "float8_e4m3fn_x4", "uint8"
MASKS = [1, 2, 4]
RANK = "su1 su2 mx1 bc1 zz0 mx2 bc2 su0 mg1 mx0 rw0 rw1 rw2 rw3 ng ab tr1 tr2 mt2 ee be ve4 vl4 es ve5 vl5 pa pb sl0 sl1 sl2 sl3 ve6 vl6 rw4 ve7 vl7 vl14 se0 se1 se2 se3 sl8 se8 sl9 se9 sl10 se10 sl11 se11 sl12 se12 sl13 se13 se14 se15 ct4 ct5 pr ct6 ct7 ct0 ct1 ct2 ct3 ct8 ct9 ct10 ct11 ct12 sc0 ct13 ct14 ct15 sc1"
CUTS = [10]
MEAN = "xb as0 as1 as2 bs2 av3 bv3 zg0 zp3 zg1 zp2 qz lx te0 te1 te2 te3"
OUT0 = "po0 po1 t10 t11 g2 ck pe0 pe1 pe2 pe3 t2 go cj s10 s11 cl tv0 tv1 tv2 tv3 sa sb qs ws0 ws1 ws2 ws3"
OUT1 = "qv po0 pe0 pe1 po1 pe2 pe3 t10 t11 g2 t2 go s10 ts0 s11 tv1 tv2 sa tv3 sb qs ws0 ws1 ws2 ws3"
OUT2 = "pe0 pe1 pe2 pe3 po0 po1 ts0 ts1 ts2 t10 t11 g2 t2 go s10 s11 sa sb tv3 qs wt0 wt1 wt2 wt3"
OUT = [OUT0, OUT1, OUT2]
LATE = ["||", "||", "||"]
SPLIT = True
LOAD = 0
XQF = False
STORE = 4
IDF = 3
UN0 = 4
UN1 = 4
LEND = 16 * 127
STEP = 2.0 ** -24 * (1 + 2.0 ** -23)
TINY = 2.0 ** -120
TB = ()
MMO = (0, 1, 2, 3)
PICKS = [("A", 0, 0, 0), ("A", 1, 0, 0), ("A", 2, 0, 0), ("A", 3, 0, 0), ("S", 0, 0, 16), ("S", 2, 0, 16), ("V", 1, 0, 8), ("V", 3, 0, 12), ("V", 1, 8, 16), ("S", 3, 12, 16), ("Q", 0, 0, 0), ("Q", 1, 0, 0)]
RAW = True
BIG = 1.0e29
LISTS = {"o_u": (0, 16), "o_d": (16, 4), "o_s": (20, 24), "o_m": (44, 24), "o_i": (68, 8), "o_t": (76, 2),
         "o_y": (78, 16), "o_e": (94, 2), "o_q": (96, 16)}


def _sb(n, d):
    return ("sbuf", [128, n], d)


SCRATCH = {
    "x0": _sb(1024, B), "xs": _sb(1024, B), "xq": _sb(256, X4), "xp": _sb(256, U8),
    "ub": _sb(512, B), "uq": _sb(128, X4), "up": _sb(128, U8), "u0q": _sb(256, X4), "u0p": _sb(256, U8),
    "vb": _sb(512, B), "vq": _sb(128, X4), "vp": _sb(128, U8),
    "wq": _sb(512, X4), "wp": _sb(512, U8),
    "ones": _sb(256, B), "ident": _sb(128, B), "eb": _sb(520, B), "eq": _sb(512, X4), "ep": _sb(512, U8),
    "gb": _sb(128, F), "gc": _sb(128, F), "pc": _sb(32, F), "i16": _sb(32, F), "ibc": _sb(16, F), "i01": _sb(16, F),
    "ist": _sb(16, F), "ft": _sb(16, F), "lo": _sb(112, U),
    "kmax": _sb(128, B), "cm": _sb(512, B), "kb": _sb(16, F),
    "o1": _sb(288, F), "s0": _sb(384, F), "s1": _sb(512, F),
    "tt": _sb(1024, B), "win": _sb(4 * 384, B), "tw": _sb(1024, B),
    "sm": _sb(384, F), "pm": _sb(640, F), "bc": _sb(256, F), "bst": _sb(80, F),
    "ee": _sb(512, B), "es": _sb(512, B), "pw": _sb(256, B), "pr": _sb(256, B),
    "so": _sb(LEND + 16, U), "fl": _sb(16 * 256, U),
    "sw": _sb(272, B), "tb": _sb(288, B), "i2": _sb(64, F), "l_k": _sb(32, U),
    "xa": _sb(16, F), "xb": _sb(16, F), "xc": _sb(16, F), "l_x": _sb(16, U), "hz": _sb(384 * len(TB) + 8, F),
    "ag": _sb(512, F), "bg": _sb(512, F), "te": _sb(512, F), "zt": _sb(512, B), "zq": _sb(128, X4), "zp": _sb(128, U8),
    "yb": _sb(256, F), "rq": _sb(128, X4), "rp": _sb(128, U8), "rt": _sb(512, B), "hq": _sb(128, X4),
}
for _r in range(3):
    SCRATCH["ss%d" % _r] = _sb(64, F)
    SCRATCH["sl%d" % _r] = _sb(48, F)
    SCRATCH["tq%d" % _r] = _sb(256, X4)
    SCRATCH["tp%d" % _r] = _sb(256, U8)
    SCRATCH["lq%d" % _r] = _sb(256, X4)
    SCRATCH["lp%d" % _r] = _sb(256, U8)
for _k in range(8):
    SCRATCH["ps%d" % _k] = ("psum", [128, 512], F)

NC, ND = 110, 16
SEMAPHORES = (["c%d" % k for k in range(NC)] + ["d%d" % k for k in range(ND)]
              + ["%s%d" % (n, r) for n in ("as", "aq", "gs", "gq", "gp") for r in range(3)] + ["ar", "gr", "gx", "ah", "aw"])


def _bits(engs):
    m = 0
    for e in engs:
        m |= 1 << e
    return m


def _helpers(T, topo):
    out = {}
    for c in T.cores:
        free = [x for x in topo.cores_of(c) if topo.die(x) != topo.die(c) and x not in T.cores and x not in out.values()]
        out[c] = free[0]
    return out


def _hand_on(g, core, T, topo):
    for c, mate in _helpers(T, topo).items():
        if mate == core:
            for R, mask in enumerate(MASKS):
                peer = T.cores[T.rank_of(c) ^ mask]
                if topo.chip(peer) != topo.chip(c):
                    en = topo.engines(core, peer)
                    rid, pid, _ = topo.addr(peer)
                    g.wait_ge(T.sem.ah, len(topo.engines(c, core)) - len(topo.engines(c, peer)))
                    g.remote_dma(T["lq%d" % R][:, 128:256].bitcast(dt.uint8), T.hq[:].bitcast(dt.uint8),
                                 T.sem.aw, T.sem.gx, pid, rid, _bits(en))
                    g.wait_ge(T.sem.gx, len(en))


def rank_program(g, core, T, topo):
    rank = T.rank_of(core)
    if rank is None:
        return _hand_on(g, core, T, topo)
    eng = {"G": g, "V": g.vector, "S": g.scalar, "P": g.tensor, "Y": g.sync}
    ops = []

    def w(name, a=0, b=None, s=1):
        if b is None:
            b = SCRATCH[name][1][1]
        ap = T[name][:, a:b] if s == 1 else T[name][:, a:b:s]
        if s == 1:
            m = ((1 << (b - a)) - 1) << a
        else:
            m = _bits(range(a, b, s))
        return (ap, [(name, m)])

    def ind(win, off):
        return (win[0].indirect(off[0]), win[1] + off[1])

    def ap(v):
        return v[0] if isinstance(v, tuple) else v

    def acc(vs):
        out = []
        for v in vs:
            if isinstance(v, tuple):
                out += v[1]
        return out

    def op(q, kind, fn, reads, writes, sem=None):
        ops.append({"q": q, "kind": kind, "fn": fn, "r": acc(reads), "w": acc(writes), "sem": sem})

    def copy(o, i):
        op("V", "c", lambda e: e.tensor_copy(ap(o), ap(i)), [i], [o])

    def scatter(win, off, i):
        op("V", "c", lambda e: e.tensor_copy(win[0].indirect(off[0]), ap(i)), [i, off], [win])

    def tt(o, a, b, f):
        op("V", "c", lambda e: e.tensor_tensor(ap(o), ap(a), ap(b), f), [a, b], [o])

    def ts(o, a, s1, f1, s2=None, f2=None):
        if f2 is None:
            op("V", "c", lambda e: e.tensor_scalar(ap(o), ap(a), ap(s1), None, f1), [a, s1], [o])
        else:
            op("V", "c", lambda e: e.tensor_scalar(ap(o), ap(a), ap(s1), ap(s2), f1, f2), [a, s1, s2], [o])

    def scan(o, a, b, init, f0, f1):
        op("V", "c", lambda e: e.tensor_tensor_scan(ap(o), ap(a), ap(b), ap(init), f0, f1), [a, b, init], [o])

    def trans(o, i):
        op("V", "c", lambda e: e.transpose(ap(o), ap(i)), [i], [o])

    def memset(o, c):
        op("V", "c", lambda e: e.memset(ap(o), c), [], [o])

    def quant(q, p, i):
        op("V", "c", lambda e: e.quantize_mx(ap(q), ap(p), ap(i)), [i], [q, p])

    def act(o, i, f, bias=None, scale=None, accum=None):
        kw = {}
        if bias is not None:
            kw["bias"] = ap(bias)
        if scale is not None:
            kw["scale"] = ap(scale)
        if accum is not None:
            kw["accum_out"] = ap(accum)
        op("S", "c", lambda e: e.activation(ap(o), ap(i), f, **kw), [i, bias, scale], [o, accum])

    def lin(o, i, scale=None, bias=None):
        act(o, i, ACT.Identity, bias=bias, scale=scale)

    def mm(bank, n, lq, lp, rq, rp):
        o = w("ps%d" % bank, 0, n)
        op("P", "c", lambda e: e.matmul_mx(ap(o), ap(lq), ap(lp), ap(rq), ap(rp), True, True), [lq, lp, rq, rp], [o])

    def iota(o, pat, base, cm=0, small=True):
        if small:
            op("G", "c", lambda e: e.iota(ap(o), pat, base, cm, allow_small_or_imprecise_dtypes=True), [], [o])
        else:
            op("G", "c", lambda e: e.iota(ap(o), pat, base, cm), [], [o])

    def dma(q, o, i):
        op(q, "d", lambda e: e.dma_start(ap(o), ap(i)), [i], [o])

    def u8(v):
        return (v[0].bitcast(dt.uint8), v[1])

    def send(dst, o, i, rsem, lsem, engs):
        rid, pid, _ = topo.addr(dst)
        op("G", "r", lambda e: e.remote_dma(o, ap(i), T.sem[rsem], T.sem[lsem], pid, rid, _bits(engs)),
           [i], [], (lsem, len(engs)))

    def fold(dst, o, a, b, rsem, lsem, engs):
        rid, pid, _ = topo.addr(dst)
        op("G", "r", lambda e: e.remote_dma_fused(
            [RemoteDMATransfer(dst_ids=[DstId(rid=rid, pnc=pid)], dma_engine_mask=_bits(engs), remote_sem=T.sem[rsem],
                               srcs=[ap(a), ap(b)], dsts=[o], alu_op=1)], local_sem=T.sem[lsem]),
           [a, b], [], (lsem, len(engs)))

    def arrive(views, sem, n):
        op("X", "x", None, [], views, (sem, n))

    def col(name, k):
        return w(name, k, k + 1)

    def part(name, k, n=128):
        return w(name, n * k, n * k + n)

    def quant_x(name):
        for h in range(2):
            quant(part("xq", h), part("xp", h), part(name, h, 512))

    def unpack(q, p):
        for b in range(4):
            mm(b, 256, part("eq", b), part("ep", b), w(q), w(p))

    def lst(name, a=0, b=None, table="lo"):
        o, n = LISTS[name]
        return w(table, o + a, o + (n if b is None else b))

    if LOAD == 0:
        dma("Y", part("x0", 0, 512), T.x[:, 0:512])
        dma("S", w("ub"), T.u[:])
        dma("Y", part("x0", 1, 512), T.x[:, 512:1024])
    elif LOAD == 1:
        for k, q in enumerate("YS"):
            dma(q, (T.x0[64 * k:64 * k + 64, 0:512], part("x0", k, 256)[1]), T.x[64 * k:64 * k + 64, 0:512])
        dma("Y", part("x0", 1, 512), T.x[:, 512:1024])
        dma("S", w("ub"), T.u[:])
    else:
        dma("S", part("x0", 0, 512), T.x[:, 0:512])
        dma("Y", w("ub"), T.u[:])
        dma("S", part("x0", 1, 512), T.x[:, 512:1024])
    memset(w("ones"), 1.0)
    BASES = [("od", 1, (0, 32, 0)), ("hf", 0, (16, 0, 0)), ("rf", 15, (16, -2, -1)), ("d", -1, (1, 0, 1))]
    base = {}

    def identity():
        op("G", "c", lambda e: e.affine_select(T.ident[:], T.ones[:, 0:128], [[-1, 128]], ALU.is_equal, 0.0, 0, 1),
           [w("ones")], [w("ident")])

    def unit(b):
        quant(part("eq", b), part("ep", b), w("eb", 3 - b, 515 - b))

    for k, (name, b0, (sh, sb, st)) in enumerate(BASES):
        base[name] = 32 * k
        iota(part("gb", k, 32), [[sh, 2], [sb, 8], [st, 2]], b0)
        if k == 1:
            if IDF:
                identity()
            op("G", "c", lambda e: e.affine_select(T.gb[:, 0:32], T.gb[:, 0:32], [[1, 2], [0, 8], [-1, 2]], ALU.is_equal,
                                                   256.0, 0, 0), [part("gb", 0, 32)], [part("gb", 0, 32)])
    iota(w("ft"), [[16, 2], [32, 4], [0, 2]], 0)
    iota(w("ibc"), [[1, 8], [0, 2]], 0)
    if not IDF:
        identity()
    iota(w("i16"), [[16, 32]], 0)
    iota(w("ist"), [[32, 8], [256, 2]], 0)

    def bs(name, n=1):
        return w("gc", base[name], base[name] + n)

    def fill(o, n, c):
        act(o, w("ones", 0, n), ACT.Copy, scale=float(c))

    memset(w("eb"), 0.0)
    memset(w("o1", 256, 288), 0.0)
    memset(w("pw"), 0.0)
    memset(w("sw", 0, 16), 0.0)
    memset(w("kmax"), 0.0)
    for k in range(len(TB)):
        memset(w("hz", 384 * k + 128, 384 * k + 384), 0.0)
    fill(w("ee", 0, 256), 256, 1)
    fill(w("i01", 0, 16, 2), 8, 0)
    fill(w("i01", 1, 16, 2), 8, 32)
    fill(w("kmax", 0, 128, 16), 8, -BIG)
    if IDF:
        copy(w("eb", 3, 515, 4), w("ident"))
        for b in range(IDF):
            unit(b)
    trans(w("gc"), w("gb"))
    copy(lst("o_u"), w("ft"))
    hf, rf, d_ = bs("hf"), bs("rf"), bs("d")
    same, q_, qr, t_, b16, u_, y_ = [col("pc", k) for k in (0, 1, 8, 2, 9, 10, 11)]
    lin(qr, hf, -1.0, rf)
    lin(t_, hf, -0.0625, d_)
    act(same, d_, ACT.Abs)
    lin(lst("o_d"), w("ibc", 0, 4), 16.0, bs("od"))
    lin(col("pc", 3), hf, 14.0, rf)
    lin(q_, qr, -1.0, 15.0)
    lin(b16, t_, 1.0, qr)
    lin(lst("o_m", 0, 8), bs("hf", 8), None, rf)
    lin(lst("o_m", 8, 24), w("i01"), None, qr)
    if not IDF:
        copy(w("eb", 3, 515, 4), w("ident"))

    def first_constants():
        lin(y_, b16, -8.0, 127.0)
        lin(u_, b16, -8.0, hf)
        lin(lst("o_s", 8, 24), w("ist"), None, rf)
        lin(lst("o_s", 0, 8), w("i16", 1, 16, 2), None, col("pc", 3))
        lin(col("pc", 13), same, 240.0, y_)
        lin(lst("o_i"), w("i16", 0, 8), 1.0, 15.0)
        lin(col("pc", 16), hf, -0.0625, 2.0)
        lin(col("pc", 17), hf, -8.0, 143.0)
        lin(col("pc", 18), hf, 0.0625, 1.0)
        lin(col("pc", 19), hf, 9.0, 15.0)
        lin(lst("o_t", 0, 1), u_, same, col("pc", 13))

    def kind_constants():
        ts(col("pc", 21), q_, 8.0, ALU.is_ge, -127.0, ALU.mult)
        ts(col("pc", 12), same, -1.0, ALU.add)

    def entry_constants():
        lin(lst("o_q"), w("ee", 0, 16), q_)
        lin(col("pc", 5), hf, 1.0, -1.0)
        lin(col("pc", 6), hf, 1.0, q_)
        lin(col("pc", 4), q_, 16.0, -1.0)
        lin(w("kb"), w("ibc"), 32.0, col("pc", 5))
        lin(w("pw", 2, 256, 16), w("ibc"), 32.0, col("pc", 6))

    def row_constants():
        for t in range(2):
            o = LISTS["o_y"][0]
            lin(w("lo", o + t, o + 16, 2), w("i16", 0, 8), col("pc", 16 + 2 * t), col("pc", 17 + 2 * t))

    def later_constants():
        lin(col("pc", 22), q_, 16.0, col("pc", 21))
        lin(w("xc"), w("i16", 8, 24), None, q_)
        ts(col("pc", 23), col("pc", 12), -144.0, ALU.mult, col("pc", 22), ALU.add)
        lin(lst("o_e"), w("i16", 0, 2), 0.125, col("pc", 23))

    def up(b):
        return 1.0 if b in TB else 32.0

    def tw_(b):
        return w("win", 384 * b + 128, 384 * b + 384)

    def fw(b):
        return part("win", b, 384)

    def bank(b, n=256):
        return w("ps%d" % b, 0, n)

    def pick_u(h):
        o, off = part("u0q", h), lst("o_u", 8 * h, 8 * h + 8)
        op("V", "c", lambda e: e.tensor_copy(o[0].bitcast(dt.uint32), T.uq[:].bitcast(dt.uint32).indirect(off[0])),
           [w("uq"), off], [o])

    def own_scores():
        for h in range(2):
            mm(5 + h, 256, part("u0q", h), part("u0p", h), w("xq"), w("xp"))

    X = "x0"
    for R, mask in enumerate(MASKS):
        peer = T.cores[rank ^ mask]
        en = topo.engines(core, peer)
        e_s, e_q = en, en
        raw = 128 if R == 0 and RAW else 0
        if R == 0:
            for b in range(IDF, UN0):
                unit(b)
            if XQF:
                quant(part("xq", 0), part("xp", 0), part("x0", 0, 512))
            quant(w("uq"), w("up"), w("ub"))
            for b in range(max(IDF, UN0), UN1):
                unit(b)
            if not IDF:
                entry_constants()
            if XQF:
                first_constants()
            for h in range(2):
                act(part("u0p", h), ind(w("up"), lst("o_u", 8 * h, 8 * h + 8)), ACT.Copy)
            if not XQF:
                first_constants()
            if IDF:
                entry_constants()
            row_constants()
            if not XQF:
                quant(part("xq", 0), part("xp", 0), part("x0", 0, 512))
            if raw:
                send(peer, T.rp[:], w("xp", 0, raw), "ar", "gr", en)
            if XQF:
                quant(part("xq", 1), part("xp", 1), part("x0", 1, 512))
            pick_u(0)
            pick_u(1)
            if not XQF:
                quant(part("xq", 1), part("xp", 1), part("x0", 1, 512))
        for h in range(2):
            mm(4 + 3 * h, 128, w("uq"), w("up"), part("xq", h), part("xp", h))
        far = topo.chip(peer) != topo.chip(core)

        def send_codes():
            quant(w("tq%d" % R, raw), w("tp%d" % R, raw), w("tt", 4 * raw))
            if far:
                mate = _helpers(T, topo)[core]
                spare = [e for e in topo.engines(core, mate) if e not in en]
                both = [(peer, T["lq%d" % R][:, 0:128], part("tq%d" % R, 0), "aq%d" % R, en),
                        (mate, T.hq[:], part("tq%d" % R, 1), "ah", spare)]
                op("G", "r", lambda e: e.remote_dma_fused(
                    [RemoteDMATransfer(dst_ids=[DstId(rid=topo.addr(c)[0], pnc=topo.addr(c)[1])],
                                       dma_engine_mask=_bits(m), remote_sem=T.sem[s], src=u8(i)[0],
                                       dst=o.bitcast(dt.uint8)) for c, o, i, s, m in both],
                    local_sem=T.sem["gq%d" % R]), [w("tq%d" % R)], [], ("gq%d" % R, len(en) + len(spare)))
            else:
                send(peer, T["lq%d" % R][:, raw:256].bitcast(dt.uint8), u8(w("tq%d" % R, raw)), "aq%d" % R, "gq%d" % R,
                     e_q)
            send(peer, T["lp%d" % R][:, raw:256], w("tp%d" % R, raw), "aq%d" % R, "gp%d" % R, e_q)

        def scores_out():
            fold(peer, T["sl%d" % R][:], w("ss%d" % R, 0, 48), w("ss%d" % R, 16, 64), "as%d" % R, "gs%d" % R, e_s)
            if raw:
                send(peer, T.rq[:].bitcast(dt.uint8), u8(w("xq", 0, raw)), "ar", "gx", en)

        def step(name):
            k, b = name[:2], int(name[2:] or 0)
            tile = w("tt", 4 * raw + b, 1024, 4), w("ps%d" % b, raw, 256)
            {"po": lambda: mm(5 + b, 256, part("u0q", b), part("u0p", b), w("xq"), w("xp")),
             "pe": lambda: mm(b, 256, part("eq", b), part("ep", b), w("xq"), w("xp")),
             "un": lambda: unit(b),
             "t1": lambda: trans(part("o1", b), bank(4 + 3 * b, 128)),
             "g2": lambda: copy(w("i2"), ind(w("o1"), lst("o_d"))),
             "t2": lambda: trans(w("ss%d" % R), w("i2")),
             "go": scores_out,
             "s1": lambda: act(part("s1", b, 256), bank(5 + b), ACT.Copy),
             "sa": lambda: act(w("s0", 128, 384), ind(w("s1"), lst("o_s", 8, 24)), ACT.Copy),
             "sb": lambda: act(w("s0", 0, 128), ind(w("s1"), lst("o_s", 0, 8)), ACT.Copy),
             "tv": lambda: copy(*tile),
             "ts": lambda: act(tile[0], tile[1], ACT.Copy),
             "qs": send_codes,
             "qv": lambda: quant(w("vq"), w("vp"), w("vb")),
             "wv": lambda: ts(tw_(b), bank(b), up(b), ALU.mult),
             "wt": lambda: ts(tw_(b), w("tt", b, 1024, 4), up(b), ALU.mult),
             "ws": lambda: act(tw_(b), bank(b), ACT.Copy, scale=up(b)),
             "ck": kind_constants,
             "cj": lambda: ts(w("cm", 256, 512), ind(part("gb", 2, 32), lst("o_q")), qr, ALU.not_equal),
             "cl": later_constants}[k]()

        for name in OUT[R].split():
            step(name)
        arrive([w("sl%d" % R)], "as%d" % R, len(e_s))
        if far:
            arrive([part("lq%d" % R, 0), w("lp%d" % R)], "aq%d" % R, 2 * len(e_q))
            arrive([part("lq%d" % R, 1)], "aw", len(e_q))
        else:
            arrive([w("lq%d" % R, raw), w("lp%d" % R, raw)], "aq%d" % R, 2 * len(e_q))
        if R == 0:
            dma("Y", u8(w("wq")), (T.wc[:], w("sl0")[1]))
            dma("Y", w("wp"), T.ws[:])
            dma("Y", w("vb"), T.v[:])
        if raw:
            arrive([w("rq"), w("rp")], "ar", 2 * len(en))
            for b in range(4):
                mm(4 + b, raw, part("eq", b), part("ep", b), w("rq"), w("rp"))
        row0 = 384
        ends = lst("o_i", 0, 8)

        def spread(k):
            return ind(w("sl%d" % R), lst("o_m", 8 * k, 8 * k + 8))

        mine = ind(w("pm", 0, 384), lst("o_t", 0, 1))
        mid = w("es", 15, 256, 16)
        l_s = w("so", LEND, LEND + 16)

        def own(k):
            return col("bst", k)

        def row(a=0, b=256):
            return w("pm", row0 + a, row0 + b)

        def flags(k, later):
            a = 16 * (k + 1)
            a, b = (a, 256) if later else (0, a)
            return w("fl", 256 * k + a, 256 * k + b), row(a, b)

        def raw_step(k):
            if raw and k < 4:
                act(w("rt", k, 4 * raw, 4), bank(4 + k, raw), ACT.Copy)
            elif raw:
                quant(w("lq0", 0, raw), w("lp0", 0, raw), w("rt"))

        def piece(k):
            a, b = ([0] + CUTS + [16])[k:k + 2]
            scatter(w("sw", 16, 272), w("so", LEND + a, LEND + b), w("pr", 16 * a, 16 * b))

        def rank_step(name):
            c, k = name[:2], int(name[2:] or 0)
            {"su": lambda: tt(part("sm", k), spread(k), part("s0", k), ALU.add),
             "mx": lambda: scan(part("pm", k), w("kmax"), part("sm", k), 0.0, ALU.add, ALU.max),
             "bc": lambda: act(part("bc", k - 1), ind(part("pm", k), ends), ACT.Copy),
             "mg": lambda: tt(part("cm", k - 1), ind(part("pm", k), ends), part("sm", k), ALU.not_equal),
             "mt": lambda: tt(part("cm", k - 1), part("bc", k - 1), part("sm", k), ALU.not_equal),
             "ng": lambda: act(w("bst", 0, 16), mine, ACT.Copy, scale=-1.0),
             "ab": lambda: act(w("bst", 16, 32), mine, ACT.Abs, scale=STEP, bias=-TINY),
             "be": lambda: tt(w("bst", 32, 48), w("bst", 16, 32), w("bst", 0, 16), ALU.add),
             "tr": lambda: trans(part("pm", 2 + k), part("bc", k - 1)),
             "ee": lambda: tt(w("ee", 256, 512), ind(w("pm", 0, 384), lst("o_y")), row(), ALU.is_equal),
             "es": lambda: scan(w("es"), w("cm"), w("ee"), 0.0, ALU.mult, ALU.subtract),
             "eh": lambda: scan(part("es", k, 256), part("cm", k, 256), part("ee", k, 256), 0.0, ALU.mult, ALU.subtract),
             "pa": lambda: tt(w("pw", 0, 256, 16), w("kb"), mid, ALU.subtract),
             "pb": lambda: ts(w("pw", 1, 256, 16), mid, -1.0, ALU.mult, col("pc", 4), ALU.add),
             "pc": lambda: lin(w("pw", 1, 256, 16), mid, -1.0, col("pc", 4)),
             "pr": lambda: trans(w("pr"), w("pw")),
             "rw": lambda: raw_step(k),
             "ve": lambda: ts(*flags(k, False), own(k), ALU.add, 0.0, ALU.is_ge),
             "vl": lambda: ts(*flags(k, True), own(k), ALU.add, 0.0, ALU.is_gt),
             "se": lambda: act(*flags(k, False), ACT.Sign, bias=col("bst", 32 + k)),
             "sl": lambda: act(*flags(k, True), ACT.Sign, bias=own(k)),
             "ct": lambda: scan(w("so", LEND + k - 16 * 127, LEND + 16, 16), part("fl", 2 * k), part("fl", 2 * k + 1),
                                col("es", 271 + 16 * k), ALU.add, ALU.add),
             "zz": lambda: [step(x) for x in LATE[R].split("|")[k].split()],
             "sc": lambda: piece(k)}[c]()

        for name in RANK.split():
            rank_step(name)
        if far and SPLIT:
            for h in range(2):
                for b in range(4):
                    mm(4 * h + b, 128, part("eq", b), part("ep", b), part("lq%d" % R, h), part("lp%d" % R, h))
            for h in range(2):
                for b in range(4):
                    act(part("tw", 2 * b + h), bank(4 * h + b, 128), ACT.Copy, scale=0.5)
        else:
            unpack("lq%d" % R, "lp%d" % R)
            for b in range(4):
                act(part("tw", b, 256), bank(b), ACT.Copy, scale=0.5)
        act(w("xa"), l_s, ACT.Relu, scale=1000.0, bias=-127500.0)
        trans(w("tb", 0, 128), w("sw", 16, 144))
        trans(w("tb", 128, 288), w("sw", 0, 160))
        copy(w("l_k"), ind(w("tb"), lst("o_e")))
        la, lb, le = w("l_k", 0, 8), w("l_k", 8, 16), w("l_k", 16, 24)

        for name in MEAN.split():
            c, b = name[:2], int(name[2:] or 0)
            theirs = ind(part("tw", b, 256), lb)
            {"as": lambda: act(part("ag", b), ind(tw_(b), la), ACT.Copy, scale=0.5 / up(b)),
             "av": lambda: ts(part("ag", b), ind(tw_(b), la), 0.5 / up(b), ALU.mult),
             "bs": lambda: act(part("bg", b), theirs, ACT.Copy),
             "bv": lambda: copy(part("bg", b), theirs),
             "zg": lambda: tt(w("zt", b, 512, 4), theirs, part("ag", b), ALU.add),
             "zp": lambda: tt(w("zt", b, 512, 4), part("bg", b), part("ag", b), ALU.add),
             "qz": lambda: quant(w("zq"), w("zp"), w("zt")),
             "xb": lambda: tt(w("xb"), w("xa"), l_s, ALU.add),
             "lx": lambda: tt(w("l_x"), w("xb"), w("xc"), ALU.min),
             "te": lambda: act(part("te", b), ind(tw_(b), le), ACT.Copy)}[c]()
        for b in MMO:
            mm(4 + b, 128, part("wq", b), part("wp", b), w("zq"), w("zp"))
        for q, b, c0, c1 in PICKS:
            if q == "A":
                tt(w("win", 384 * b, 384 * b + 128), bank(4 + b, 128), part("te", b), ALU.add)
                continue
            if q in "CD":
                o = w("hz", 384 * TB.index(b), 384 * TB.index(b) + 128)
                if q == "C":
                    act(o, bank(4 + b, 128), ACT.Copy, scale=2.0 ** -5)
                else:
                    ts(o, bank(4 + b, 128), 2.0 ** -5, ALU.mult)
                continue
            if q == "Q":
                quant(part("xq", b), part("xp", b), part("xs", b, 512))
                continue
            o, i = w("xs", 64 * c0 + b, 64 * c1, 4), ind(fw(b), w("l_x", c0, c1))
            if q == "T":
                tt(o, ind(part("hz", TB.index(b), 384), w("l_x", c0, c1)),
                   w("win", 384 * b + 128 + 16 * c0, 384 * b + 128 + 16 * c1), ALU.add)
            elif q == "S":
                act(o, i, ACT.Copy, scale=2.0 ** -5)
            else:
                ts(o, i, 2.0 ** -5, ALU.mult)

    for h in range(2):
        mm(h, 128, w("vq"), w("vp"), part("xq", h), part("xp", h))
    def scales(q, k):
        dma(q, T.osc[4 * k:4 * k + 4, :], (T.xp[32 * k:32 * k + 4, :], w("xp")[1]))

    if STORE == 0:
        dma("Y", T.oc[:, 0:512], u8(part("xq", 0)))
        act(part("yb", 0), w("ps0", 0, 128), ACT.Copy)
        copy(part("yb", 1), w("ps1", 0, 128))
        dma("Y", T.oc[:, 512:1024], u8(part("xq", 1)))
        scales("Y", 0)
        dma("S", T.y[:, 0:128], part("yb", 0))
        dma("Y", T.y[:, 128:256], part("yb", 1))
        for k in range(1, 4):
            scales("S", k)
    else:
        dma("Y", T.oc[:], u8(w("xq")))
        act(part("yb", 0), w("ps0", 0, 128), ACT.Copy)
        copy(part("yb", 1), w("ps1", 0, 128))
        for k in range(STORE):
            scales("Y", k)
        dma("S", T.y[:], w("yb"))
        for k in range(STORE, 4):
            scales("S", k)

    _emit(eng, ops, T)


def _emit(eng, ops, T):
    known = {q: 0 for q in eng}
    done = {q: 0 for q in eng}
    seen = {}
    for n, o in enumerate(ops):
        deps = set()
        for wr, accs in ((False, o["r"]), (True, o["w"])):
            for name, m in accs:
                psum = name.startswith("ps") and name[2:].isdigit()
                for k, kw, km in seen.get(name, []):
                    if psum and ops[k]["q"] != o["q"]:
                        deps.add(k)
                    elif (wr or kw) and (m & km):
                        deps.add(k)
        for wr, accs in ((False, o["r"]), (True, o["w"])):
            for name, m in accs:
                seen.setdefault(name, []).append((n, wr, m))
        deps.discard(n)
        o["waits"], o["sig"] = [], False
        if o["kind"] == "x":
            o["clo"] = 0
            continue
        q = o["q"]
        for k in sorted(deps, reverse=True):
            if not known[q] >> k & 1:
                o["waits"].append(k)
                ops[k]["sig"] = True
                known[q] |= ops[k]["clo"] | ops[k].get("before", 0) | 1 << k
        o["clo"] = known[q]
        if o["kind"] == "c":
            o["before"] = done[q]
            done[q] |= 1 << n
    tail = [k for k, o in enumerate(ops) if o["kind"] == "r" and not o["sig"]]
    tail_d = [k for k, o in enumerate(ops) if o["kind"] == "d" and not o["sig"]]
    for k in tail_d:
        ops[k]["sig"] = True
    waiters = {}
    for n, o in enumerate(ops):
        for k in o["waits"]:
            waiters.setdefault(k, []).append(n)
    groups = {}
    for n, o in enumerate(ops):
        if o["kind"] in ("c", "d") and o["sig"]:
            groups.setdefault((o["kind"], tuple(waiters.get(n, [-n]))), []).append(n)
    pool = {"c": [[0, 0] for _ in range(NC)], "d": [[0, 0] for _ in range(ND)]}
    for (kind, _), members in groups.items():
        step = 1 if kind == "c" else 16
        for s, st in enumerate(pool[kind]):
            if all(st[0] & ~ops[k]["clo"] == 0 for k in members):
                st[0] = _bits(members)
                st[1] += step * len(members)
                for k in members:
                    ops[k]["sem"] = ("%s%d" % (kind, s), st[1])
                    ops[k]["step"] = step
                break
        else:
            raise ValueError("out of semaphores")
    for o in ops:
        if o["kind"] == "x":
            continue
        e = eng[o["q"]]
        for sem in dict.fromkeys(ops[k]["sem"] for k in o["waits"]):
            e.wait_ge(T.sem[sem[0]], sem[1])
        ins = o["fn"](e)
        if o["kind"] != "r" and o["sig"]:
            ins.then_inc(T.sem[o["sem"][0]], o["step"])
    for k in tail:
        eng["G"].wait_ge(T.sem[ops[k]["sem"][0]], ops[k]["sem"][1])
    for k in tail_d:
        eng[ops[k]["q"]].wait_ge(T.sem[ops[k]["sem"][0]], ops[k]["sem"][1])
